import numpy as np
import ml_dtypes


def mxq(x, axis, fmt="e4m3"):
    dtype, down = {"e4m3": (ml_dtypes.float8_e4m3fn, 7), "e5m2": (ml_dtypes.float8_e5m2, 14)}[fmt]
    v = np.moveaxis(np.asarray(x, np.float32).astype(ml_dtypes.bfloat16).astype(np.float64), axis, -1)
    blocks = v.reshape(v.shape[:-1] + (-1, 32))
    amax = np.abs(blocks).max(-1, keepdims=True)
    byte = np.maximum(np.where(amax > 0, np.frexp(amax)[1] - 1 + 127, 0) - down, 1)
    scale = np.exp2(byte - 127.0)
    codes = (blocks / scale).astype(np.float32).astype(dtype).astype(np.float64)
    return np.moveaxis((codes * scale).reshape(v.shape), -1, axis)


WIDE = False


def mx_kscale(k):
    if not WIDE:
        return np.ones(k)
    levels = np.array([18, -18])
    if k % 512:
        return np.exp2(np.random.permutation(np.resize(levels, k // 32))).repeat(32)
    a = np.empty((k // 512, 16))
    for p in range(k // 512):
        a[p, :8] = np.random.permutation(np.resize(levels, 8))
        for g in range(8):
            far = levels[np.abs(levels - a[p, g]) >= 10]
            a[p, g + 8] = far[np.random.randint(len(far))]
    return np.exp2(a.ravel()).repeat(32)


def f64(x):
    return np.asarray(x).astype(np.float64)


def striped(idx):
    return np.tile(np.asarray(idx).reshape(-1, 16).T, (8, 1)).astype(np.uint16)


def unstriped(offs):
    return offs[:16].T.reshape(-1).astype(np.int64)


def setup_inputs():
    n = np.random.standard_normal
    uni = np.random.uniform
    idx = np.random.permutation(2048)[:512]
    f_d = mx_kscale(512)
    f_e = mx_kscale(512)
    f_r = mx_kscale(512)
    return {
        "kT": (n((512, 2048)) * f_d[:, None]).astype(np.float32),
        "vT": (n((512, 2048)) / np.sqrt(512) * f_e[:, None]).astype(np.float32),
        "cd": (uni(0.75, 1.3, (512, 1))).astype(np.float32),
        "ce": np.tile(uni(0.75, 1.3, 512), (128, 1)).astype(np.float32),
        "do": (n((512, 512)) * f_r[:, None] / f_e[None, :]).astype(np.float32),
        "qT": (n((512, 512)) / np.sqrt(512) / f_d[:, None] / f_r[None, :]).astype(np.float32),
        "ts": np.tile(uni(0.75, 1.3, 2048), (128, 1)).astype(np.float32),
        "offs": striped(idx),
    }


def reference(kT, vT, cd, ce, do, qT, ts, offs):
    idx = unstriped(offs)
    kT_i = f64(kT)[:, idx]
    vT_i = f64(vT)[:, idx]
    S = mxq(f64(qT), 1, "e4m3") @ mxq(f64(do), 0, "e5m2")
    s = f64(cd) * f64(ce)[:1] * S
    ts_i = f64(ts)[:1][:, idx]
    dk0 = mxq(s, 1, "e5m2") @ mxq(vT_i, 0, "e4m3")
    dk = ts_i * dk0
    out_0 = np.zeros((512, 2048))
    out_0[:, idx] = dk
    dv0 = mxq(s, 0, "e5m2").T @ mxq(kT_i, 0, "e4m3")
    dv = ts_i * dv0
    out_1 = np.zeros((512, 2048))
    out_1[:, idx] = dv
    return out_0, out_1

@@ -1,0 +1,172 @@
+from contextlib import ExitStack
+
+import concourse.mybir as mybir
+from concourse.masks import make_identity
+
+F32 = mybir.dt.float32
+BF16 = mybir.dt.bfloat16
+U32 = mybir.dt.uint32
+U16 = mybir.dt.uint16
+U8 = mybir.dt.uint8
+E4M3 = mybir.dt.float8_e4m3fn_x4
+E5M2 = mybir.dt.float8_e5m2_x4
+MULT = mybir.AluOpType.mult
+COPY = mybir.ActivationFunctionType.Copy
+
+P = 128
+PACK = 4
+K = 512
+TOKENS = 2048
+SLOTS = 512
+WINDOWS = 3
+FLOPS = 3 * 2 * K * K * K
+
+
+def tile_attend_glin_kv_kernel(tc, kT, vT, cd, ce, do, qT, ts, offs, out_0, out_1):
+    nc = tc.nc
+    with ExitStack() as ctx:
+        sb = ctx.enter_context(tc.tile_pool(name="sb", bufs=1))
+        ps = ctx.enter_context(tc.psum_pool(name="ps", bufs=1))
+
+        def weave(engine_copy, woven, planes):
+            engine_copy(
+                out=woven[:].rearrange("p (c i) t -> p c t i", i=4),
+                in_=planes[:].rearrange("p t (c i) -> p c t i", i=4),
+            )
+
+        def quantise(name, woven, fmt):
+            codes = sb.tile([P, K], U32, name=name + "_codes", align_bytes=64)
+            scales = sb.tile([P, K], U8, name=name + "_scales", align_bytes=64)
+            nc.vector.quantize_mx(out=codes[:].bitcast(fmt), scales=scales[:], in_=woven[:].rearrange("p c t -> p (c t)"))
+            return codes, scales, fmt
+
+        def product(bank, stationary, j, moving):
+            cols = slice(P * j, P * (j + 1))
+            nc.tensor.matmul_mx(
+                out=bank[:],
+                lhsT=stationary[0][:, cols].bitcast(stationary[2]),
+                lhsT_scale=stationary[1][:, cols],
+                rhs=moving[0][:].bitcast(moving[2]),
+                rhs_scale=moving[1][:],
+                start=True,
+                stop=True,
+            )
+
+        def turn(woven, rows, ident):
+            woven_words = woven[:].rearrange("p c t -> p (c t)").bitcast(F32).rearrange("p (t m u) -> p t m u", t=PACK, u=2)
+            for half in range(2):
+                bank = ps.tile([P, 2, 2, P], F32, name="turn_bank", tag="turn%d" % half)
+                for tt in range(2):
+                    words = rows[2 * half + tt].bitcast(F32)
+                    for u in range(2):
+                        nc.tensor.transpose(bank[:, tt, u, :], words[:, u : K // 2 : 2], ident[:])
+                nc.scalar.copy(out=woven_words[:, 2 * half : 2 * half + 2], in_=bank[:].rearrange("p t u m -> p t m u"))
+
+        offsets = sb.tile([P, SLOTS // 16], U16, name="offsets")
+        q_raw = sb.tile([P, PACK, K], F32, name="q_raw")
+        do_raw = sb.tile([P, PACK, K], F32, name="do_raw")
+        cd_cols = sb.tile([P, PACK], F32, name="cd_cols")
+        ce_cols = sb.tile([P, PACK], F32, name="ce_cols")
+        ts_pool = sb.tile([P, TOKENS], F32, name="ts_pool")
+        nc.vector.memset(ts_pool[0 : P - 1, :], 0.0)
+        nc.sync.dma_start(out=q_raw[:], in_=qT.rearrange("(m t) r -> m t r", t=PACK))
+        nc.sync.dma_start(offsets[:], offs)
+        nc.sync.dma_start(out=do_raw[:], in_=do.rearrange("(p j) e -> p j e", j=PACK))
+        nc.scalar.dma_start(out=ce_cols[:], in_=ce[0:1, :].rearrange("o (p j) -> (o p) j", j=PACK))
+        nc.scalar.dma_start(out=cd_cols[:], in_=cd.rearrange("(p t) o -> p (t o)", t=PACK))
+        nc.scalar.dma_start(out=ts_pool[P - 1 : P, :], in_=ts[0:1, :])
+        k_rows = kT.rearrange("(p t) n -> t p n", t=PACK)
+        v_rows = vT.rearrange("(p t) n -> t p n", t=PACK)
+        k_raw = [sb.tile([P, TOKENS], F32, name="k_raw%d" % t) for t in range(PACK)]
+        v_raw = [sb.tile([P, TOKENS], F32, name="v_raw%d" % t) for t in range(PACK)]
+        for t in range(PACK):
+            nc.sync.dma_start(out=k_raw[t][:], in_=k_rows[t])
+        for t in range(PACK):
+            nc.sync.dma_start(out=v_raw[t][:], in_=v_rows[t])
+
+        ident = sb.tile([P, P], F32, name="ident")
+        make_identity(nc, ident[:])
+        windows = [sb.tile([P, TOKENS], F32, name="window%d" % w) for w in range(WINDOWS)]
+        for w in range(2):
+            nc.vector.memset(windows[w][:], 0.0)
+
+        q_bf = [sb.tile([P, K], BF16, name="q_bf%d" % t) for t in range(PACK)]
+        for t in range(PACK):
+            nc.vector.tensor_copy(out=q_bf[t][:], in_=q_raw[:, t, :])
+        q_woven = sb.tile([P, K, PACK], BF16, name="q_woven", align_bytes=64)
+        turn(q_woven, [q_bf[t][:] for t in range(PACK)], ident)
+        do_woven = sb.tile([P, K, PACK], BF16, name="do_woven", align_bytes=64)
+        weave(nc.vector.tensor_copy, do_woven, do_raw)
+        q_mx = quantise("q", q_woven, E4M3)
+        do_mx = quantise("do", do_woven, E5M2)
+
+        ce_bank = ps.tile([P, PACK, P], F32, name="ce_bank", tag="spread0")
+        for j in range(PACK):
+            nc.tensor.transpose(ce_bank[:, j, :], ce_cols[:, j : j + 1].to_broadcast([P, P]), ident[:])
+        ce_rows = sb.tile([P, P, PACK], F32, name="ce_rows")
+        nc.scalar.copy(out=ce_rows[:], in_=ce_bank[:].rearrange("p j n -> p n j"))
+
+        s_planes = sb.tile([P, PACK, K], BF16, name="s_planes")
+        for t in range(PACK):
+            bank = ps.tile([P, K], F32, name="s_bank", tag="sum%d" % t)
+            product(bank, q_mx, t, do_mx)
+            nc.vector.scalar_tensor_tensor(
+                out=s_planes[:, t, :], in0=bank[:], scalar=cd_cols[:, t : t + 1],
+                in1=ce_rows[:].rearrange("p n j -> p (n j)"), op0=MULT, op1=MULT)
+        sd_woven = sb.tile([P, K, PACK], BF16, name="sd_woven", align_bytes=64)
+        weave(nc.scalar.copy, sd_woven, s_planes)
+        se_woven = sb.tile([P, K, PACK], BF16, name="se_woven", align_bytes=64)
+        turn(se_woven, [s_planes[:, t, :] for t in range(PACK)], ident)
+
+        ts_row = sb.tile([P, SLOTS], F32, name="ts_row")
+        nc.vector.tensor_copy(out=ts_row[:], in_=ts_pool[:].indirect(offsets[:]))
+        ts_bank = ps.tile([P, PACK, P], F32, name="ts_bank", tag="spread1")
+        for j in range(PACK):
+            nc.tensor.transpose(ts_bank[:, j, :], ts_row[:, P * j : P * (j + 1)], ident[:])
+        ts_cols = sb.tile([P, PACK], F32, name="ts_cols")
+        nc.scalar.copy(out=ts_cols[:], in_=ts_bank[:, :, P - 1])
+        ts_bank2 = ps.tile([P, PACK, P], F32, name="ts_bank2", tag="spread0")
+        for j in range(PACK):
+            nc.tensor.transpose(ts_bank2[:, j, :], ts_cols[:, j : j + 1].to_broadcast([P, P]), ident[:])
+        ts_rows = sb.tile([P, SLOTS], F32, name="ts_rows")
+        nc.scalar.copy(out=ts_rows[:], in_=ts_bank2[:].rearrange("p j n -> p (j n)"))
+
+        k_planes = sb.tile([P, PACK, SLOTS], BF16, name="k_planes")
+        for t in range(PACK):
+            nc.vector.tensor_copy(out=k_planes[:, t, :], in_=k_raw[t][:].indirect(offsets[:]))
+        sd_mx = quantise("sd", sd_woven, E5M2)
+        k_woven = sb.tile([P, SLOTS, PACK], BF16, name="k_woven", align_bytes=64)
+        weave(nc.vector.tensor_copy, k_woven, k_planes)
+        k_mx = quantise("k", k_woven, E4M3)
+        se_mx = quantise("se", se_woven, E5M2)
+
+        def result_tile(n, stationary, j, moving, rows, tag):
+            bank = ps.tile([P, SLOTS], F32, name="sum_bank", tag="sum%d" % j)
+            product(bank, stationary, j, moving)
+            sums = sb.tile([P, SLOTS], F32, name="sums%d" % n, tag=tag)
+            nc.scalar.copy(out=sums[:], in_=bank[:])
+            window = windows[n % WINDOWS]
+            nc.vector.tensor_tensor(out=window[:].indirect(offsets[:]), in0=sums[:], in1=ts_rows[:], op=MULT)
+            nc.sync.dma_start(out=rows, in_=window[:])
+
+        dv_rows = out_1.rearrange("(j p) n -> j p n", p=P)
+        dk_rows = out_0.rearrange("(m t) n -> t m n", t=PACK)
+        for j in range(2):
+            result_tile(j, sd_mx, j, k_mx, dv_rows[j], "sums%d" % j)
+
+        v_planes = sb.tile([P, PACK, SLOTS], BF16, name="v_planes")
+        for t in range(PACK):
+            if t in (1, 2):
+                v_bf = sb.tile([P, TOKENS], BF16, name="v_bf%d" % t)
+                nc.scalar.activation(out=v_bf[:], in_=v_raw[t][:], func=COPY)
+                nc.scalar.activation(out=v_planes[:, t, :], in_=v_bf[:].indirect(offsets[:]), func=COPY)
+            else:
+                nc.vector.tensor_copy(out=v_planes[:, t, :], in_=v_raw[t][:].indirect(offsets[:]))
+        nc.vector.memset(windows[2][:], 0.0)
+        result_tile(2, sd_mx, 2, k_mx, dv_rows[2], "v_raw2")
+        v_woven = sb.tile([P, SLOTS, PACK], BF16, name="v_woven", align_bytes=64)
+        weave(nc.scalar.copy, v_woven, v_planes)
+        v_mx = quantise("v", v_woven, E4M3)
+        result_tile(3, sd_mx, 3, k_mx, dv_rows[3], "v_planes")
+        for t in range(PACK):
+            result_tile(PACK + t, se_mx, t, v_mx, dk_rows[t], "sums%d" % (PACK + t))

@@ -28,14 +28,14 @@ def tile_attend_glin_kv_kernel(tc, kT, vT, cd, ce, do, qT, ts, offs, out_0, out_
         sb = ctx.enter_context(tc.tile_pool(name="sb", bufs=1))
         ps = ctx.enter_context(tc.psum_pool(name="ps", bufs=1))
 
-        def weave(engine_copy, woven, planes):
+        def weave(engine_copy, woven, planes, first=0, last=K):
             engine_copy(
-                out=woven[:].rearrange("p (c i) t -> p c t i", i=4),
-                in_=planes[:].rearrange("p t (c i) -> p c t i", i=4),
+                out=woven[:, first:last, :].rearrange("p (c i) t -> p c t i", i=4),
+                in_=planes[:, :, first:last].rearrange("p t (c i) -> p c t i", i=4),
             )
 
-        def quantise(name, woven, fmt):
-            codes = sb.tile([P, K], U32, name=name + "_codes", align_bytes=64)
+        def quantise(name, woven, fmt, tag=""):
+            codes = sb.tile([P, K], U32, name=name + "_codes", align_bytes=64, tag=tag or name + "_codes")
             scales = sb.tile([P, K], U8, name=name + "_scales", align_bytes=64)
             nc.vector.quantize_mx(out=codes[:].bitcast(fmt), scales=scales[:], in_=woven[:].rearrange("p c t -> p (c t)"))
             return codes, scales, fmt
@@ -66,19 +66,19 @@ def tile_attend_glin_kv_kernel(tc, kT, vT, cd, ce, do, qT, ts, offs, out_0, out_
         q_raw = sb.tile([P, PACK, K], F32, name="q_raw")
         do_raw = sb.tile([P, PACK, K], F32, name="do_raw")
         cd_cols = sb.tile([P, PACK], F32, name="cd_cols")
-        ce_cols = sb.tile([P, PACK], F32, name="ce_cols")
+        ce_cols = sb.tile([P, PACK], F32, name="ce_cols", align_bytes=64)
         ts_pool = sb.tile([P, TOKENS], F32, name="ts_pool")
-        nc.vector.memset(ts_pool[0 : P - 1, :], 0.0)
+        ts_cols = sb.tile([P, TOKENS // P], F32, name="ts_cols")
+        nc.sync.dma_start(out=ts_cols[:], in_=ts[0:1, :].rearrange("o (p j) -> (o p) j", p=P))
         nc.sync.dma_start(out=q_raw[:], in_=qT.rearrange("(m t) r -> m t r", t=PACK))
         nc.sync.dma_start(offsets[:], offs)
         nc.sync.dma_start(out=do_raw[:], in_=do.rearrange("(p j) e -> p j e", j=PACK))
         nc.scalar.dma_start(out=ce_cols[:], in_=ce[0:1, :].rearrange("o (p j) -> (o p) j", j=PACK))
         nc.scalar.dma_start(out=cd_cols[:], in_=cd.rearrange("(p t) o -> p (t o)", t=PACK))
-        nc.scalar.dma_start(out=ts_pool[P - 1 : P, :], in_=ts[0:1, :])
         k_rows = kT.rearrange("(p t) n -> t p n", t=PACK)
         v_rows = vT.rearrange("(p t) n -> t p n", t=PACK)
-        k_raw = [sb.tile([P, TOKENS], F32, name="k_raw%d" % t) for t in range(PACK)]
-        v_raw = [sb.tile([P, TOKENS], F32, name="v_raw%d" % t) for t in range(PACK)]
+        k_raw = [sb.tile([P, TOKENS], F32, name="k_raw%d" % t, align_bytes=64) for t in range(PACK)]
+        v_raw = [sb.tile([P, TOKENS], F32, name="v_raw%d" % t, align_bytes=64) for t in range(PACK)]
         for t in range(PACK):
             nc.sync.dma_start(out=k_raw[t][:], in_=k_rows[t])
         for t in range(PACK):
@@ -87,8 +87,16 @@ def tile_attend_glin_kv_kernel(tc, kT, vT, cd, ce, do, qT, ts, offs, out_0, out_
         ident = sb.tile([P, P], F32, name="ident")
         make_identity(nc, ident[:])
         windows = [sb.tile([P, TOKENS], F32, name="window%d" % w) for w in range(WINDOWS)]
-        for w in range(2):
+        for w in range(WINDOWS):
             nc.vector.memset(windows[w][:], 0.0)
+
+        ts_lines = ts_pool[:].rearrange("p (n b j) -> p n b j", b=PACK, j=PACK)
+        for b in range(PACK):
+            ts_bank = ps.tile([P, PACK, P], F32, name="ts_bank", tag="sum%d" % b)
+            for j in range(PACK):
+                col = PACK * b + j
+                nc.tensor.transpose(ts_bank[:, j, :], ts_cols[:, col : col + 1].to_broadcast([P, P]), ident[:])
+            nc.scalar.activation(out=ts_lines[:, :, b, :], in_=ts_bank[:].rearrange("p j n -> p n j"), func=COPY)
 
         q_bf = [sb.tile([P, K], BF16, name="q_bf%d" % t) for t in range(PACK)]
         for t in range(PACK):
@@ -97,14 +105,19 @@ def tile_attend_glin_kv_kernel(tc, kT, vT, cd, ce, do, qT, ts, offs, out_0, out_
         turn(q_woven, [q_bf[t][:] for t in range(PACK)], ident)
         do_woven = sb.tile([P, K, PACK], BF16, name="do_woven", align_bytes=64)
         weave(nc.vector.tensor_copy, do_woven, do_raw)
-        q_mx = quantise("q", q_woven, E4M3)
         do_mx = quantise("do", do_woven, E5M2)
+        q_mx = quantise("q", q_woven, E4M3)
+        ts_rows = sb.tile([P, SLOTS], F32, name="ts_rows", tag="q_woven", align_bytes=64)
+        nc.vector.tensor_copy(out=ts_rows[:], in_=ts_pool[:].indirect(offsets[:]))
 
-        ce_bank = ps.tile([P, PACK, P], F32, name="ce_bank", tag="spread0")
+        ce_bank = ps.tile([P, PACK, P], F32, name="ce_bank", tag="turn0")
         for j in range(PACK):
             nc.tensor.transpose(ce_bank[:, j, :], ce_cols[:, j : j + 1].to_broadcast([P, P]), ident[:])
         ce_rows = sb.tile([P, P, PACK], F32, name="ce_rows")
         nc.scalar.copy(out=ce_rows[:], in_=ce_bank[:].rearrange("p j n -> p n j"))
+
+        k_bf = sb.tile([P, TOKENS], BF16, name="k_bf", tag="ce_cols", align_bytes=64)
+        nc.scalar.activation(out=k_bf[:], in_=k_raw[0][:], func=COPY)
 
         s_planes = sb.tile([P, PACK, K], BF16, name="s_planes")
         for t in range(PACK):
@@ -113,37 +126,26 @@ def tile_attend_glin_kv_kernel(tc, kT, vT, cd, ce, do, qT, ts, offs, out_0, out_
             nc.vector.scalar_tensor_tensor(
                 out=s_planes[:, t, :], in0=bank[:], scalar=cd_cols[:, t : t + 1],
                 in1=ce_rows[:].rearrange("p n j -> p (n j)"), op0=MULT, op1=MULT)
+        k_planes = sb.tile([P, PACK, SLOTS], BF16, name="k_planes", tag="q_codes", align_bytes=64)
+        nc.scalar.activation(out=k_planes[:, 0, :], in_=k_bf[:].indirect(offsets[:]), func=COPY)
         sd_woven = sb.tile([P, K, PACK], BF16, name="sd_woven", align_bytes=64)
         weave(nc.scalar.copy, sd_woven, s_planes)
         se_woven = sb.tile([P, K, PACK], BF16, name="se_woven", align_bytes=64)
         turn(se_woven, [s_planes[:, t, :] for t in range(PACK)], ident)
 
-        ts_row = sb.tile([P, SLOTS], F32, name="ts_row")
-        nc.vector.tensor_copy(out=ts_row[:], in_=ts_pool[:].indirect(offsets[:]))
-        ts_bank = ps.tile([P, PACK, P], F32, name="ts_bank", tag="spread1")
-        for j in range(PACK):
-            nc.tensor.transpose(ts_bank[:, j, :], ts_row[:, P * j : P * (j + 1)], ident[:])
-        ts_cols = sb.tile([P, PACK], F32, name="ts_cols")
-        nc.scalar.copy(out=ts_cols[:], in_=ts_bank[:, :, P - 1])
-        ts_bank2 = ps.tile([P, PACK, P], F32, name="ts_bank2", tag="spread0")
-        for j in range(PACK):
-            nc.tensor.transpose(ts_bank2[:, j, :], ts_cols[:, j : j + 1].to_broadcast([P, P]), ident[:])
-        ts_rows = sb.tile([P, SLOTS], F32, name="ts_rows")
-        nc.scalar.copy(out=ts_rows[:], in_=ts_bank2[:].rearrange("p j n -> p (j n)"))
-
-        k_planes = sb.tile([P, PACK, SLOTS], BF16, name="k_planes")
-        for t in range(PACK):
+        for t in range(1, PACK):
             nc.vector.tensor_copy(out=k_planes[:, t, :], in_=k_raw[t][:].indirect(offsets[:]))
         sd_mx = quantise("sd", sd_woven, E5M2)
         k_woven = sb.tile([P, SLOTS, PACK], BF16, name="k_woven", align_bytes=64)
-        weave(nc.vector.tensor_copy, k_woven, k_planes)
+        weave(nc.vector.tensor_copy, k_woven, k_planes, 0, 352)
+        weave(nc.scalar.copy, k_woven, k_planes, 352, K)
         k_mx = quantise("k", k_woven, E4M3)
-        se_mx = quantise("se", se_woven, E5M2)
+        se_mx = quantise("se", se_woven, E5M2, "k_raw3")
 
         def result_tile(n, stationary, j, moving, rows, tag):
             bank = ps.tile([P, SLOTS], F32, name="sum_bank", tag="sum%d" % j)
             product(bank, stationary, j, moving)
-            sums = sb.tile([P, SLOTS], F32, name="sums%d" % n, tag=tag)
+            sums = sb.tile([P, SLOTS], F32, name="sums%d" % n, tag=tag, align_bytes=64)
             nc.scalar.copy(out=sums[:], in_=bank[:])
             window = windows[n % WINDOWS]
             nc.vector.tensor_tensor(out=window[:].indirect(offsets[:]), in0=sums[:], in1=ts_rows[:], op=MULT)
@@ -154,7 +156,7 @@ def tile_attend_glin_kv_kernel(tc, kT, vT, cd, ce, do, qT, ts, offs, out_0, out_
         for j in range(2):
             result_tile(j, sd_mx, j, k_mx, dv_rows[j], "sums%d" % j)
 
-        v_planes = sb.tile([P, PACK, SLOTS], BF16, name="v_planes")
+        v_planes = sb.tile([P, PACK, SLOTS], BF16, name="v_planes", tag="k_woven", align_bytes=64)
         for t in range(PACK):
             if t in (1, 2):
                 v_bf = sb.tile([P, TOKENS], BF16, name="v_bf%d" % t)
@@ -162,11 +164,10 @@ def tile_attend_glin_kv_kernel(tc, kT, vT, cd, ce, do, qT, ts, offs, out_0, out_
                 nc.scalar.activation(out=v_planes[:, t, :], in_=v_bf[:].indirect(offsets[:]), func=COPY)
             else:
                 nc.vector.tensor_copy(out=v_planes[:, t, :], in_=v_raw[t][:].indirect(offsets[:]))
-        nc.vector.memset(windows[2][:], 0.0)
         result_tile(2, sd_mx, 2, k_mx, dv_rows[2], "v_raw2")
         v_woven = sb.tile([P, SLOTS, PACK], BF16, name="v_woven", align_bytes=64)
         weave(nc.scalar.copy, v_woven, v_planes)
         v_mx = quantise("v", v_woven, E4M3)
-        result_tile(3, sd_mx, 3, k_mx, dv_rows[3], "v_planes")
+        result_tile(3, sd_mx, 3, k_mx, dv_rows[3], "k_woven")
         for t in range(PACK):
             result_tile(PACK + t, se_mx, t, v_mx, dk_rows[t], "sums%d" % (PACK + t))

@@ -1,7 +1,6 @@
 from contextlib import ExitStack
 
 import concourse.mybir as mybir
-from concourse.masks import make_identity
 
 F32 = mybir.dt.float32
 BF16 = mybir.dt.bfloat16
@@ -34,10 +33,10 @@ def tile_attend_glin_kv_kernel(tc, kT, vT, cd, ce, do, qT, ts, offs, out_0, out_
                 in_=planes[:, :, first:last].rearrange("p t (c i) -> p c t i", i=4),
             )
 
-        def quantise(name, woven, fmt, tag=""):
-            codes = sb.tile([P, K], U32, name=name + "_codes", align_bytes=64, tag=tag or name + "_codes")
-            scales = sb.tile([P, K], U8, name=name + "_scales", align_bytes=64)
-            nc.vector.quantize_mx(out=codes[:].bitcast(fmt), scales=scales[:], in_=woven[:].rearrange("p c t -> p (c t)"))
+        def quantise(name, woven, fmt, tag="", first=0, last=K):
+            codes = sb.tile([P, last - first], U32, name=name + "_codes", align_bytes=64, tag=tag or name + "_codes")
+            scales = sb.tile([P, last - first], U8, name=name + "_scales", align_bytes=64)
+            nc.vector.quantize_mx(out=codes[:].bitcast(fmt), scales=scales[:], in_=woven[:, first:last, :].rearrange("p c t -> p (c t)"))
             return codes, scales, fmt
 
         def product(bank, stationary, j, moving):
@@ -85,10 +84,13 @@ def tile_attend_glin_kv_kernel(tc, kT, vT, cd, ce, do, qT, ts, offs, out_0, out_
             nc.sync.dma_start(out=v_raw[t][:], in_=v_rows[t])
 
         ident = sb.tile([P, P], F32, name="ident")
-        make_identity(nc, ident[:])
+        zeros = sb.tile([P, P], F32, name="zeros", tag="window2")
+        nc.gpsimd.memset(zeros[:], 0.0)
+        nc.gpsimd.affine_select(out=ident[:], in_=zeros[:], compare_op=mybir.AluOpType.not_equal, fill=1.0, base=0,
+                                pattern=[[-1, P]], channel_multiplier=1)
         windows = [sb.tile([P, TOKENS], F32, name="window%d" % w) for w in range(WINDOWS)]
         for w in range(WINDOWS):
-            nc.vector.memset(windows[w][:], 0.0)
+            (nc.vector if w < 2 else nc.gpsimd).memset(windows[w][:], 0.0)
 
         ts_lines = ts_pool[:].rearrange("p (n b j) -> p n b j", b=PACK, j=PACK)
         for b in range(PACK):
@@ -135,16 +137,17 @@ def tile_attend_glin_kv_kernel(tc, kT, vT, cd, ce, do, qT, ts, offs, out_0, out_
 
         for t in range(1, PACK):
             nc.vector.tensor_copy(out=k_planes[:, t, :], in_=k_raw[t][:].indirect(offsets[:]))
-        sd_mx = quantise("sd", sd_woven, E5M2)
+        sd_mx = [quantise("sd%d" % h, sd_woven, E5M2, "", 256 * h, 256 * (h + 1)) for h in range(2)]
         k_woven = sb.tile([P, SLOTS, PACK], BF16, name="k_woven", align_bytes=64)
         weave(nc.vector.tensor_copy, k_woven, k_planes, 0, 352)
         weave(nc.scalar.copy, k_woven, k_planes, 352, K)
         k_mx = quantise("k", k_woven, E4M3)
-        se_mx = quantise("se", se_woven, E5M2, "k_raw3")
+        dv_banks = [ps.tile([P, SLOTS], F32, name="dv_bank%d" % j, tag="sum%d" % j) for j in range(PACK)]
+        for j in range(PACK):
+            product(dv_banks[j], sd_mx[j // 2], j % 2, k_mx)
+        se_mx = quantise("se", se_woven, E5M2, "q_codes")
 
-        def result_tile(n, stationary, j, moving, rows, tag):
-            bank = ps.tile([P, SLOTS], F32, name="sum_bank", tag="sum%d" % j)
-            product(bank, stationary, j, moving)
+        def result_tile(n, bank, rows, tag):
             sums = sb.tile([P, SLOTS], F32, name="sums%d" % n, tag=tag, align_bytes=64)
             nc.scalar.copy(out=sums[:], in_=bank[:])
             window = windows[n % WINDOWS]
@@ -154,20 +157,22 @@ def tile_attend_glin_kv_kernel(tc, kT, vT, cd, ce, do, qT, ts, offs, out_0, out_
         dv_rows = out_1.rearrange("(j p) n -> j p n", p=P)
         dk_rows = out_0.rearrange("(m t) n -> t m n", t=PACK)
         for j in range(2):
-            result_tile(j, sd_mx, j, k_mx, dv_rows[j], "sums%d" % j)
+            result_tile(j, dv_banks[j], dv_rows[j], "sums%d" % j)
 
         v_planes = sb.tile([P, PACK, SLOTS], BF16, name="v_planes", tag="k_woven", align_bytes=64)
         for t in range(PACK):
             if t in (1, 2):
-                v_bf = sb.tile([P, TOKENS], BF16, name="v_bf%d" % t)
+                v_bf = sb.tile([P, TOKENS], BF16, name="v_bf%d" % t, tag="sd%d_codes" % (t - 1), align_bytes=64)
                 nc.scalar.activation(out=v_bf[:], in_=v_raw[t][:], func=COPY)
                 nc.scalar.activation(out=v_planes[:, t, :], in_=v_bf[:].indirect(offsets[:]), func=COPY)
             else:
                 nc.vector.tensor_copy(out=v_planes[:, t, :], in_=v_raw[t][:].indirect(offsets[:]))
-        result_tile(2, sd_mx, 2, k_mx, dv_rows[2], "v_raw2")
+        result_tile(2, dv_banks[2], dv_rows[2], "v_raw2")
         v_woven = sb.tile([P, SLOTS, PACK], BF16, name="v_woven", align_bytes=64)
         weave(nc.scalar.copy, v_woven, v_planes)
         v_mx = quantise("v", v_woven, E4M3)
-        result_tile(3, sd_mx, 3, k_mx, dv_rows[3], "k_woven")
+        result_tile(3, dv_banks[3], dv_rows[3], "k_woven")
         for t in range(PACK):
-            result_tile(PACK + t, se_mx, t, v_mx, dk_rows[t], "sums%d" % (PACK + t))
+            bank = ps.tile([P, SLOTS], F32, name="dk_bank", tag="sum%d" % t)
+            product(bank, se_mx, t, v_mx)
+            result_tile(PACK + t, bank, dk_rows[t], "sums%d" % (PACK + t))

@@ -17,6 +17,8 @@ PACK = 4
 K = 512
 TOKENS = 2048
 SLOTS = 512
+HALF = SLOTS // 2
+SPLIT = 64
 WINDOWS = 3
 FLOPS = 3 * 2 * K * K * K
 
@@ -25,19 +27,20 @@ def tile_attend_glin_kv_kernel(tc, kT, vT, cd, ce, do, qT, ts, offs, out_0, out_
     nc = tc.nc
     with ExitStack() as ctx:
         sb = ctx.enter_context(tc.tile_pool(name="sb", bufs=1))
+        placed = ctx.enter_context(tc.tile_pool(name="placed", bufs=1))
         ps = ctx.enter_context(tc.psum_pool(name="ps", bufs=1))
 
-        def weave(engine_copy, woven, planes, first=0, last=K):
-            engine_copy(
-                out=woven[:, first:last, :].rearrange("p (c i) t -> p c t i", i=4),
-                in_=planes[:, :, first:last].rearrange("p t (c i) -> p c t i", i=4),
-            )
+        def weave(engine_copy, woven, planes):
+            engine_copy(out=woven.rearrange("p (c i) t -> p c t i", i=4), in_=planes.rearrange("p t (c i) -> p c t i", i=4))
 
-        def quantise(name, woven, fmt, tag="", first=0, last=K):
-            codes = sb.tile([P, last - first], U32, name=name + "_codes", align_bytes=64, tag=tag or name + "_codes")
-            scales = sb.tile([P, last - first], U8, name=name + "_scales", align_bytes=64)
-            nc.vector.quantize_mx(out=codes[:].bitcast(fmt), scales=scales[:], in_=woven[:, first:last, :].rearrange("p c t -> p (c t)"))
+        def operand(name, fmt, width=K, tag=""):
+            codes = sb.tile([P, width], U32, name=name + "_codes", align_bytes=64, tag=tag or name + "_codes")
+            scales = sb.tile([P, width], U8, name=name + "_scales", align_bytes=64)
             return codes, scales, fmt
+
+        def quantise(mx, woven, first=0):
+            cols = slice(first, first + woven.shape[1])
+            nc.vector.quantize_mx(out=mx[0][:, cols].bitcast(mx[2]), scales=mx[1][:, cols], in_=woven.rearrange("p c t -> p (c t)"))
 
         def product(bank, stationary, j, moving):
             cols = slice(P * j, P * (j + 1))
@@ -51,128 +54,165 @@ def tile_attend_glin_kv_kernel(tc, kT, vT, cd, ce, do, qT, ts, offs, out_0, out_
                 stop=True,
             )
 
-        def turn(woven, rows, ident):
-            woven_words = woven[:].rearrange("p c t -> p (c t)").bitcast(F32).rearrange("p (t m u) -> p t m u", t=PACK, u=2)
-            for half in range(2):
-                bank = ps.tile([P, 2, 2, P], F32, name="turn_bank", tag="turn%d" % half)
-                for tt in range(2):
-                    words = rows[2 * half + tt].bitcast(F32)
-                    for u in range(2):
-                        nc.tensor.transpose(bank[:, tt, u, :], words[:, u : K // 2 : 2], ident[:])
-                nc.scalar.copy(out=woven_words[:, 2 * half : 2 * half + 2], in_=bank[:].rearrange("p t u m -> p t m u"))
+        def turn(woven, rows, half, ident):
+            woven_words = woven.rearrange("p c t -> p (c t)").bitcast(F32).rearrange("p (t m u) -> p t m u", t=2, u=2)
+            bank = ps.tile([P, 2, 2, P], F32, name="turn_bank", tag="turn%d" % half)
+            for tt in range(2):
+                words = rows[:, tt, :].bitcast(F32)
+                for u in range(2):
+                    nc.tensor.transpose(bank[:, tt, u, :], words[:, u : K // 2 : 2], ident[:])
+            nc.scalar.copy(out=woven_words, in_=bank[:].rearrange("p t u m -> p t m u"))
 
         offsets = sb.tile([P, SLOTS // 16], U16, name="offsets")
-        q_raw = sb.tile([P, PACK, K], F32, name="q_raw")
+        q_raw = [sb.tile([P, 2, K], F32, name="q_raw%d" % h, align_bytes=64) for h in range(2)]
         do_raw = sb.tile([P, PACK, K], F32, name="do_raw")
-        cd_cols = sb.tile([P, PACK], F32, name="cd_cols")
+        shared = sb.tile([P, 5 * SLOTS], BF16, name="shared", align_bytes=64)
+        cd_cols = shared[:, 2 * SLOTS - 6 : 2 * SLOTS + 2].bitcast(F32)
         ce_cols = sb.tile([P, PACK], F32, name="ce_cols", align_bytes=64)
-        ts_pool = sb.tile([P, TOKENS], F32, name="ts_pool")
-        ts_cols = sb.tile([P, TOKENS // P], F32, name="ts_cols")
-        nc.sync.dma_start(out=ts_cols[:], in_=ts[0:1, :].rearrange("o (p j) -> (o p) j", p=P))
-        nc.sync.dma_start(out=q_raw[:], in_=qT.rearrange("(m t) r -> m t r", t=PACK))
+        ts_pool = sb.tile([P, TOKENS], F32, name="ts_pool", align_bytes=64)
+        q_rows = qT.rearrange("(m t) r -> m t r", t=PACK)
+        nc.sync.dma_start(out=q_raw[0][:], in_=q_rows[:, 0:2, :])
         nc.sync.dma_start(offsets[:], offs)
-        nc.sync.dma_start(out=do_raw[:], in_=do.rearrange("(p j) e -> p j e", j=PACK))
+        nc.sync.dma_start(out=ts_pool[P - 1 : P, :], in_=ts[0:1, :])
+        nc.sync.dma_start(out=q_raw[1][:], in_=q_rows[:, 2:4, :])
         nc.scalar.dma_start(out=ce_cols[:], in_=ce[0:1, :].rearrange("o (p j) -> (o p) j", j=PACK))
-        nc.scalar.dma_start(out=cd_cols[:], in_=cd.rearrange("(p t) o -> p (t o)", t=PACK))
+        nc.scalar.dma_start(out=cd_cols, in_=cd.rearrange("(p t) o -> p (t o)", t=PACK))
+        nc.sync.dma_start(out=do_raw[:], in_=do.rearrange("(p j) e -> p j e", j=PACK))
         k_rows = kT.rearrange("(p t) n -> t p n", t=PACK)
         v_rows = vT.rearrange("(p t) n -> t p n", t=PACK)
         k_raw = [sb.tile([P, TOKENS], F32, name="k_raw%d" % t, align_bytes=64) for t in range(PACK)]
         v_raw = [sb.tile([P, TOKENS], F32, name="v_raw%d" % t, align_bytes=64) for t in range(PACK)]
-        for t in range(PACK):
-            nc.sync.dma_start(out=k_raw[t][:], in_=k_rows[t])
+        for t in (1, 2, 3):
+            v_raw[t] = placed.tile([P, TOKENS], F32, name="v_placed%d" % t, offset=8192 * (t - 1), align_bytes=64)
+        k_raw[0] = placed.tile([P, TOKENS], F32, name="k_placed", offset=28672, align_bytes=64)
         for t in range(PACK):
             nc.sync.dma_start(out=v_raw[t][:], in_=v_rows[t])
+        for t in range(PACK):
+            nc.sync.dma_start(out=k_raw[t][:], in_=k_rows[t])
 
         ident = sb.tile([P, P], F32, name="ident")
-        zeros = sb.tile([P, P], F32, name="zeros", tag="window2")
-        nc.gpsimd.memset(zeros[:], 0.0)
-        nc.gpsimd.affine_select(out=ident[:], in_=zeros[:], compare_op=mybir.AluOpType.not_equal, fill=1.0, base=0,
+        nc.gpsimd.memset(ident[:], 0.0)
+        nc.gpsimd.affine_select(out=ident[:], in_=ident[:], compare_op=mybir.AluOpType.not_equal, fill=1.0, base=0,
                                 pattern=[[-1, P]], channel_multiplier=1)
-        windows = [sb.tile([P, TOKENS], F32, name="window%d" % w) for w in range(WINDOWS)]
-        for w in range(WINDOWS):
-            (nc.vector if w < 2 else nc.gpsimd).memset(windows[w][:], 0.0)
+        nc.vector.memset(ts_pool[0 : P - 1, :], 0.0)
 
-        ts_lines = ts_pool[:].rearrange("p (n b j) -> p n b j", b=PACK, j=PACK)
-        for b in range(PACK):
-            ts_bank = ps.tile([P, PACK, P], F32, name="ts_bank", tag="sum%d" % b)
-            for j in range(PACK):
-                col = PACK * b + j
-                nc.tensor.transpose(ts_bank[:, j, :], ts_cols[:, col : col + 1].to_broadcast([P, P]), ident[:])
-            nc.scalar.activation(out=ts_lines[:, :, b, :], in_=ts_bank[:].rearrange("p j n -> p n j"), func=COPY)
+        ts_row = sb.tile([P, SLOTS], F32, name="ts_row")
+        nc.vector.tensor_copy(out=ts_row[:], in_=ts_pool[:].indirect(offsets[:]))
 
-        q_bf = [sb.tile([P, K], BF16, name="q_bf%d" % t) for t in range(PACK)]
-        for t in range(PACK):
-            nc.vector.tensor_copy(out=q_bf[t][:], in_=q_raw[:, t, :])
-        q_woven = sb.tile([P, K, PACK], BF16, name="q_woven", align_bytes=64)
-        turn(q_woven, [q_bf[t][:] for t in range(PACK)], ident)
-        do_woven = sb.tile([P, K, PACK], BF16, name="do_woven", align_bytes=64)
-        weave(nc.vector.tensor_copy, do_woven, do_raw)
-        do_mx = quantise("do", do_woven, E5M2)
-        q_mx = quantise("q", q_woven, E4M3)
-        ts_rows = sb.tile([P, SLOTS], F32, name="ts_rows", tag="q_woven", align_bytes=64)
-        nc.vector.tensor_copy(out=ts_rows[:], in_=ts_pool[:].indirect(offsets[:]))
+        q_bf = [sb.tile([P, 2, K], BF16, name="q_bf%d" % h) for h in range(2)]
+        for h in range(2):
+            nc.vector.tensor_copy(out=q_bf[h][:], in_=q_raw[h][:])
+        q_woven = [sb.tile([P, HALF, PACK], BF16, name="q_woven%d" % h, align_bytes=64) for h in range(2)]
+        q_mx = [operand("q%d" % h, E4M3, HALF) for h in range(2)]
+        for h in range(2):
+            turn(q_woven[h][:], q_bf[h], h, ident)
+        quantise(q_mx[0], q_woven[0][:])
+        do_woven = sb.tile([P, K, PACK], BF16, name="do_woven", tag="q_woven0", align_bytes=64)
+        weave(nc.vector.tensor_copy, do_woven[:], do_raw[:])
+        quantise(q_mx[1], q_woven[1][:])
+        do_mx = operand("do", E5M2)
+        quantise(do_mx, do_woven[:])
+        windows = [sb.tile([P, TOKENS], F32, name="window0", tag="q_woven0", align_bytes=64)]
+        nc.gpsimd.memset(windows[0][:], 0.0)
 
-        ce_bank = ps.tile([P, PACK, P], F32, name="ce_bank", tag="turn0")
+        ce_bank = ps.tile([P, PACK, P], F32, name="ce_bank", tag="spread0")
         for j in range(PACK):
             nc.tensor.transpose(ce_bank[:, j, :], ce_cols[:, j : j + 1].to_broadcast([P, P]), ident[:])
         ce_rows = sb.tile([P, P, PACK], F32, name="ce_rows")
         nc.scalar.copy(out=ce_rows[:], in_=ce_bank[:].rearrange("p j n -> p n j"))
+        ts_turned = ps.tile([P, PACK, P], F32, name="ts_turned", tag="spread1")
+        for j in range(PACK):
+            nc.tensor.transpose(ts_turned[:, j, :], ts_row[:, P * j : P * (j + 1)], ident[:])
+        ts_cols = sb.tile([P, PACK], F32, name="ts_cols")
+        nc.scalar.copy(out=ts_cols[:], in_=ts_turned[:, :, P - 1])
+        ts_bank = ps.tile([P, PACK, P], F32, name="ts_bank", tag="spread1")
+        for j in range(PACK):
+            nc.tensor.transpose(ts_bank[:, j, :], ts_cols[:, j : j + 1].to_broadcast([P, P]), ident[:])
+        ts_rows = sb.tile([P, SLOTS], F32, name="ts_rows")
+        nc.scalar.copy(out=ts_rows[:], in_=ts_bank[:].rearrange("p j n -> p (j n)"))
 
-        k_bf = sb.tile([P, TOKENS], BF16, name="k_bf", tag="ce_cols", align_bytes=64)
-        nc.scalar.activation(out=k_bf[:], in_=k_raw[0][:], func=COPY)
-
+        v_planes = shared[:, 0 : PACK * SLOTS].rearrange("p (t s) -> p t s", t=PACK)
+        v_bf = sb.tile([P, TOKENS], BF16, name="v_bf", tag="q_woven1", align_bytes=64)
+        nc.scalar.activation(out=v_bf[:], in_=v_raw[0][:], func=COPY)
+        nc.scalar.activation(out=v_planes[:, 0, :], in_=v_bf[:].indirect(offsets[:]), func=COPY)
         s_planes = sb.tile([P, PACK, K], BF16, name="s_planes")
         for t in range(PACK):
             bank = ps.tile([P, K], F32, name="s_bank", tag="sum%d" % t)
-            product(bank, q_mx, t, do_mx)
+            product(bank, q_mx[t // 2], t % 2, do_mx)
             nc.vector.scalar_tensor_tensor(
                 out=s_planes[:, t, :], in0=bank[:], scalar=cd_cols[:, t : t + 1],
                 in1=ce_rows[:].rearrange("p n j -> p (n j)"), op0=MULT, op1=MULT)
-        k_planes = sb.tile([P, PACK, SLOTS], BF16, name="k_planes", tag="q_codes", align_bytes=64)
-        nc.scalar.activation(out=k_planes[:, 0, :], in_=k_bf[:].indirect(offsets[:]), func=COPY)
-        sd_woven = sb.tile([P, K, PACK], BF16, name="sd_woven", align_bytes=64)
-        weave(nc.scalar.copy, sd_woven, s_planes)
-        se_woven = sb.tile([P, K, PACK], BF16, name="se_woven", align_bytes=64)
-        turn(se_woven, [s_planes[:, t, :] for t in range(PACK)], ident)
+        se_woven1 = sb.tile([P, HALF, PACK], BF16, name="se_woven1", align_bytes=64)
+        se_woven = [shared[:, 3 * SLOTS : 5 * SLOTS].rearrange("p (c t) -> p c t", t=PACK), se_woven1[:]]
+        for h in range(2):
+            turn(se_woven[h], s_planes[:, 2 * h : 2 * h + 2, :], h, ident)
+        sd_woven = [placed.tile([P, HALF, PACK], BF16, name="sd_woven%d" % h, offset=(1024, 8192)[h], align_bytes=64) for h in range(2)]
+        for h in range(2):
+            weave(nc.scalar.copy, sd_woven[h][:], s_planes[:, :, HALF * h : HALF * (h + 1)])
+        se_mx = [(placed.tile([P, HALF], U32, name="se%d_codes" % h, offset=16384 * h, align_bytes=64),
+                  sb.tile([P, HALF], U8, name="se%d_scales" % h, align_bytes=64), E5M2) for h in range(2)]
+        nc.vector.tensor_copy(out=v_planes[:, 1, :], in_=v_raw[1][:].indirect(offsets[:]))
+        nc.vector.tensor_copy(out=v_planes[:, 2, :], in_=v_raw[2][:].indirect(offsets[:]))
+        quantise(se_mx[0], se_woven[0])
+        nc.vector.tensor_copy(out=v_planes[:, 3, :], in_=v_raw[3][:].indirect(offsets[:]))
+        v_woven = [sb.tile([P, HALF, PACK], BF16, name="v_woven%d" % i, align_bytes=64) for i in range(2)]
+        v_mx = operand("v", E4M3)
+        weave(nc.vector.tensor_copy, v_woven[0][:], v_planes[:, :, 0:HALF])
+        weave(nc.vector.tensor_copy, v_woven[1][:, 0:SPLIT, :], v_planes[:, :, HALF : HALF + SPLIT])
+        weave(nc.scalar.copy, v_woven[1][:, SPLIT:HALF, :], v_planes[:, :, HALF + SPLIT : SLOTS])
+        for i in range(2):
+            quantise(v_mx, v_woven[i][:], HALF * i)
+        quantise(se_mx[1], se_woven[1])
+        dk_banks = [ps.tile([P, SLOTS], F32, name="dk_bank%d" % t, tag="sum%d" % t) for t in range(PACK)]
+        for t in range(PACK):
+            product(dk_banks[t], se_mx[t // 2], t % 2, v_mx)
 
-        for t in range(1, PACK):
-            nc.vector.tensor_copy(out=k_planes[:, t, :], in_=k_raw[t][:].indirect(offsets[:]))
-        sd_mx = [quantise("sd%d" % h, sd_woven, E5M2, "", 256 * h, 256 * (h + 1)) for h in range(2)]
-        k_woven = sb.tile([P, SLOTS, PACK], BF16, name="k_woven", align_bytes=64)
-        weave(nc.vector.tensor_copy, k_woven, k_planes, 0, 352)
-        weave(nc.scalar.copy, k_woven, k_planes, 352, K)
-        k_mx = quantise("k", k_woven, E4M3)
-        dv_banks = [ps.tile([P, SLOTS], F32, name="dv_bank%d" % j, tag="sum%d" % j) for j in range(PACK)]
-        for j in range(PACK):
-            product(dv_banks[j], sd_mx[j // 2], j % 2, k_mx)
-        se_mx = quantise("se", se_woven, E5M2, "q_codes")
+        sd_mx = operand("sd", E5M2, K, "v_woven0")
+        for h in range(2):
+            quantise(sd_mx, sd_woven[h][:], HALF * h)
+        k_shared = sb.tile([P, 5 * SLOTS], BF16, name="k_shared", tag="v_woven1", align_bytes=64)
+        k_planes = k_shared[:, 0 : PACK * SLOTS].rearrange("p (t s) -> p t s", t=PACK)
+        nc.vector.tensor_copy(out=k_planes[:, 0, :], in_=k_raw[0][:].indirect(offsets[:]))
+        for w in (1, 2):
+            windows.append(placed.tile([P, TOKENS], F32, name="window%d" % w, offset=16384 + 8192 * w, align_bytes=64))
+            nc.gpsimd.memset(windows[w][:], 0.0)
+
+        def empty(n, bank, tag):
+            if n == 0:
+                sums = k_shared[:, 3 * SLOTS : 5 * SLOTS].bitcast(F32)
+            else:
+                sums = sb.tile([P, SLOTS], F32, name="sums%d" % n, tag=tag, align_bytes=64)[:]
+            nc.scalar.copy(out=sums, in_=bank[:])
+            return sums
+
+        def scatter(n, sums, rows):
+            window = windows[n % WINDOWS]
+            nc.vector.tensor_tensor(out=window[:].indirect(offsets[:]), in0=sums, in1=ts_rows[:], op=MULT)
+            nc.sync.dma_start(out=rows, in_=window[:])
 
         def result_tile(n, bank, rows, tag):
-            sums = sb.tile([P, SLOTS], F32, name="sums%d" % n, tag=tag, align_bytes=64)
-            nc.scalar.copy(out=sums[:], in_=bank[:])
-            window = windows[n % WINDOWS]
-            nc.vector.tensor_tensor(out=window[:].indirect(offsets[:]), in0=sums[:], in1=ts_rows[:], op=MULT)
-            nc.sync.dma_start(out=rows, in_=window[:])
+            scatter(n, empty(n, bank, tag), rows)
 
         dv_rows = out_1.rearrange("(j p) n -> j p n", p=P)
         dk_rows = out_0.rearrange("(m t) n -> t m n", t=PACK)
-        for j in range(2):
-            result_tile(j, dv_banks[j], dv_rows[j], "sums%d" % j)
+        for t in range(2):
+            result_tile(t, dk_banks[t], dk_rows[t], "sums%d" % t)
 
-        v_planes = sb.tile([P, PACK, SLOTS], BF16, name="v_planes", tag="k_woven", align_bytes=64)
-        for t in range(PACK):
-            if t in (1, 2):
-                v_bf = sb.tile([P, TOKENS], BF16, name="v_bf%d" % t, tag="sd%d_codes" % (t - 1), align_bytes=64)
-                nc.scalar.activation(out=v_bf[:], in_=v_raw[t][:], func=COPY)
-                nc.scalar.activation(out=v_planes[:, t, :], in_=v_bf[:].indirect(offsets[:]), func=COPY)
-            else:
-                nc.vector.tensor_copy(out=v_planes[:, t, :], in_=v_raw[t][:].indirect(offsets[:]))
-        result_tile(2, dv_banks[2], dv_rows[2], "v_raw2")
-        v_woven = sb.tile([P, SLOTS, PACK], BF16, name="v_woven", align_bytes=64)
-        weave(nc.scalar.copy, v_woven, v_planes)
-        v_mx = quantise("v", v_woven, E4M3)
-        result_tile(3, dv_banks[3], dv_rows[3], "k_woven")
-        for t in range(PACK):
-            bank = ps.tile([P, SLOTS], F32, name="dk_bank", tag="sum%d" % t)
-            product(bank, se_mx, t, v_mx)
-            result_tile(PACK + t, bank, dk_rows[t], "sums%d" % (PACK + t))
+        k_bf = [placed.tile([P, TOKENS], BF16, name="k_bf0", offset=0, align_bytes=64),
+                sb.tile([P, TOKENS], BF16, name="k_bf1", tag="v_codes", align_bytes=64)]
+        for t in range(2):
+            nc.scalar.activation(out=k_bf[t][:], in_=k_raw[t + 1][:], func=COPY)
+        nc.scalar.activation(out=k_planes[:, 1, :], in_=k_bf[0][:].indirect(offsets[:]), func=COPY)
+        sums2 = empty(2, dk_banks[2], "k_raw2")
+        nc.scalar.activation(out=k_planes[:, 2, :], in_=k_bf[1][:].indirect(offsets[:]), func=COPY)
+        nc.vector.tensor_copy(out=k_planes[:, 3, :], in_=k_raw[3][:].indirect(offsets[:]))
+        scatter(2, sums2, dk_rows[2])
+        k_woven = sb.tile([P, SLOTS, PACK], BF16, name="k_woven", align_bytes=64)
+        weave(nc.scalar.copy, k_woven[:], k_planes)
+        k_mx = operand("k", E4M3)
+        quantise(k_mx, k_woven[:])
+        result_tile(3, dk_banks[3], dk_rows[3], "v_woven1")
+        for j in range(PACK):
+            bank = ps.tile([P, SLOTS], F32, name="dv_bank", tag="sum%d" % j)
+            product(bank, sd_mx, j, k_mx)
+            result_tile(PACK + j, bank, dv_rows[j], "sums%d" % (PACK + j))

@@ -17,10 +17,20 @@ PACK = 4
 K = 512
 TOKENS = 2048
 SLOTS = 512
-HALF = SLOTS // 2
-SPLIT = 64
+HALF = 256
+VECTOR_SHARE = 64
 WINDOWS = 3
+ALIGN = 64
 FLOPS = 3 * 2 * K * K * K
+
+PLANE = 4 * TOKENS
+V1_AT = 0
+V2_AT = PLANE
+V3_AT = 2 * PLANE
+WINDOW1_AT = 3 * PLANE
+WINDOW2_AT = 4 * PLANE
+SD1_AT = WINDOW2_AT - 1024
+GATHERED_AT = WINDOW2_AT - 3072
 
 
 def tile_attend_glin_kv_kernel(tc, kT, vT, cd, ce, do, qT, ts, offs, out_0, out_1):
@@ -33,14 +43,17 @@ def tile_attend_glin_kv_kernel(tc, kT, vT, cd, ce, do, qT, ts, offs, out_0, out_
         def weave(engine_copy, woven, planes):
             engine_copy(out=woven.rearrange("p (c i) t -> p c t i", i=4), in_=planes.rearrange("p t (c i) -> p c t i", i=4))
 
-        def operand(name, fmt, width=K, tag=""):
-            codes = sb.tile([P, width], U32, name=name + "_codes", align_bytes=64, tag=tag or name + "_codes")
-            scales = sb.tile([P, width], U8, name=name + "_scales", align_bytes=64)
+        def operand(name, fmt, width, codes):
+            scales = sb.tile([P, width], U8, name=name + "_scales", align_bytes=ALIGN)
             return codes, scales, fmt
 
-        def quantise(mx, woven, first=0):
+        def words(name, width, tag):
+            return sb.tile([P, width], U32, name=name + "_codes", align_bytes=ALIGN, tag=tag)
+
+        def quantise(mx, woven, first):
+            codes, scales, fmt = mx
             cols = slice(first, first + woven.shape[1])
-            nc.vector.quantize_mx(out=mx[0][:, cols].bitcast(mx[2]), scales=mx[1][:, cols], in_=woven.rearrange("p c t -> p (c t)"))
+            nc.vector.quantize_mx(out=codes[:, cols].bitcast(fmt), scales=scales[:, cols], in_=woven.rearrange("p c t -> p (c t)"))
 
         def product(bank, stationary, j, moving):
             cols = slice(P * j, P * (j + 1))
@@ -55,21 +68,25 @@ def tile_attend_glin_kv_kernel(tc, kT, vT, cd, ce, do, qT, ts, offs, out_0, out_
             )
 
         def turn(woven, rows, half, ident):
-            woven_words = woven.rearrange("p c t -> p (c t)").bitcast(F32).rearrange("p (t m u) -> p t m u", t=2, u=2)
+            woven_words = woven.rearrange("p c t -> p (c t)").bitcast(F32).rearrange("p (a m u) -> p a m u", a=2, u=2)
             bank = ps.tile([P, 2, 2, P], F32, name="turn_bank", tag="turn%d" % half)
-            for tt in range(2):
-                words = rows[:, tt, :].bitcast(F32)
+            for a in range(2):
+                row_words = rows[:, a, :].bitcast(F32)
                 for u in range(2):
-                    nc.tensor.transpose(bank[:, tt, u, :], words[:, u : K // 2 : 2], ident[:])
-            nc.scalar.copy(out=woven_words, in_=bank[:].rearrange("p t u m -> p t m u"))
+                    nc.tensor.transpose(bank[:, a, u, :], row_words[:, u : K // 2 : 2], ident[:])
+            nc.scalar.copy(out=woven_words, in_=bank[:].rearrange("p a u m -> p a m u"))
+
+        def spread(bank, columns, ident):
+            for j in range(PACK):
+                nc.tensor.transpose(bank[:, j, :], columns[:, j : j + 1].to_broadcast([P, P]), ident[:])
 
         offsets = sb.tile([P, SLOTS // 16], U16, name="offsets")
-        q_raw = [sb.tile([P, 2, K], F32, name="q_raw%d" % h, align_bytes=64) for h in range(2)]
+        q_raw = [sb.tile([P, 2, K], F32, name="q_raw%d" % h, align_bytes=ALIGN) for h in range(2)]
         do_raw = sb.tile([P, PACK, K], F32, name="do_raw")
-        shared = sb.tile([P, 5 * SLOTS], BF16, name="shared", align_bytes=64)
-        cd_cols = shared[:, 2 * SLOTS - 6 : 2 * SLOTS + 2].bitcast(F32)
-        ce_cols = sb.tile([P, PACK], F32, name="ce_cols", align_bytes=64)
-        ts_pool = sb.tile([P, TOKENS], F32, name="ts_pool", align_bytes=64)
+        v_gathered = placed.tile([P, (PACK + 1) * SLOTS], BF16, name="v_gathered", offset=GATHERED_AT, align_bytes=ALIGN)
+        cd_cols = v_gathered[:, 2 * SLOTS - 6 : 2 * SLOTS + 2].bitcast(F32)
+        ce_cols = sb.tile([P, PACK], F32, name="ce_cols", align_bytes=ALIGN)
+        ts_pool = sb.tile([P, TOKENS], F32, name="ts_pool", align_bytes=ALIGN)
         q_rows = qT.rearrange("(m t) r -> m t r", t=PACK)
         nc.sync.dma_start(out=q_raw[0][:], in_=q_rows[:, 0:2, :])
         nc.sync.dma_start(offsets[:], offs)
@@ -77,14 +94,13 @@ def tile_attend_glin_kv_kernel(tc, kT, vT, cd, ce, do, qT, ts, offs, out_0, out_
         nc.sync.dma_start(out=q_raw[1][:], in_=q_rows[:, 2:4, :])
         nc.scalar.dma_start(out=ce_cols[:], in_=ce[0:1, :].rearrange("o (p j) -> (o p) j", j=PACK))
         nc.scalar.dma_start(out=cd_cols, in_=cd.rearrange("(p t) o -> p (t o)", t=PACK))
-        nc.sync.dma_start(out=do_raw[:], in_=do.rearrange("(p j) e -> p j e", j=PACK))
+        nc.sync.dma_start(out=do_raw[:], in_=do.rearrange("(p t) e -> p t e", t=PACK))
         k_rows = kT.rearrange("(p t) n -> t p n", t=PACK)
         v_rows = vT.rearrange("(p t) n -> t p n", t=PACK)
-        k_raw = [sb.tile([P, TOKENS], F32, name="k_raw%d" % t, align_bytes=64) for t in range(PACK)]
-        v_raw = [sb.tile([P, TOKENS], F32, name="v_raw%d" % t, align_bytes=64) for t in range(PACK)]
-        for t in (1, 2, 3):
-            v_raw[t] = placed.tile([P, TOKENS], F32, name="v_placed%d" % t, offset=8192 * (t - 1), align_bytes=64)
-        k_raw[0] = placed.tile([P, TOKENS], F32, name="k_placed", offset=28672, align_bytes=64)
+        k_raw = [sb.tile([P, TOKENS], F32, name="k_raw%d" % t, align_bytes=ALIGN) for t in range(PACK)]
+        v_raw = [sb.tile([P, TOKENS], F32, name="v_raw0", align_bytes=ALIGN)]
+        for t, at in ((1, V1_AT), (2, V2_AT), (3, V3_AT)):
+            v_raw.append(placed.tile([P, TOKENS], F32, name="v_raw%d" % t, offset=at, align_bytes=ALIGN))
         for t in range(PACK):
             nc.sync.dma_start(out=v_raw[t][:], in_=v_rows[t])
         for t in range(PACK):
@@ -94,125 +110,128 @@ def tile_attend_glin_kv_kernel(tc, kT, vT, cd, ce, do, qT, ts, offs, out_0, out_
         nc.gpsimd.memset(ident[:], 0.0)
         nc.gpsimd.affine_select(out=ident[:], in_=ident[:], compare_op=mybir.AluOpType.not_equal, fill=1.0, base=0,
                                 pattern=[[-1, P]], channel_multiplier=1)
-        nc.vector.memset(ts_pool[0 : P - 1, :], 0.0)
 
-        ts_row = sb.tile([P, SLOTS], F32, name="ts_row")
-        nc.vector.tensor_copy(out=ts_row[:], in_=ts_pool[:].indirect(offsets[:]))
+        nc.vector.memset(ts_pool[0 : P - 1, :], 0.0)
+        ts_gathered = sb.tile([P, SLOTS], F32, name="ts_gathered")
+        nc.vector.tensor_copy(out=ts_gathered[:], in_=ts_pool[:].indirect(offsets[:]))
 
         q_bf = [sb.tile([P, 2, K], BF16, name="q_bf%d" % h) for h in range(2)]
         for h in range(2):
             nc.vector.tensor_copy(out=q_bf[h][:], in_=q_raw[h][:])
-        q_woven = [sb.tile([P, HALF, PACK], BF16, name="q_woven%d" % h, align_bytes=64) for h in range(2)]
-        q_mx = [operand("q%d" % h, E4M3, HALF) for h in range(2)]
+        q_woven = [sb.tile([P, HALF, PACK], BF16, name="q_woven%d" % h, align_bytes=ALIGN) for h in range(2)]
+        q_mx = [operand("q%d" % h, E4M3, HALF, words("q%d" % h, HALF, "q%d_codes" % h)) for h in range(2)]
         for h in range(2):
             turn(q_woven[h][:], q_bf[h], h, ident)
-        quantise(q_mx[0], q_woven[0][:])
-        do_woven = sb.tile([P, K, PACK], BF16, name="do_woven", tag="q_woven0", align_bytes=64)
+        quantise(q_mx[0], q_woven[0][:], 0)
+        do_woven = sb.tile([P, K, PACK], BF16, name="do_woven", tag="q_woven0", align_bytes=ALIGN)
         weave(nc.vector.tensor_copy, do_woven[:], do_raw[:])
-        quantise(q_mx[1], q_woven[1][:])
-        do_mx = operand("do", E5M2)
-        quantise(do_mx, do_woven[:])
-        windows = [sb.tile([P, TOKENS], F32, name="window0", tag="q_woven0", align_bytes=64)]
+        quantise(q_mx[1], q_woven[1][:], 0)
+        do_mx = operand("do", E5M2, K, words("do", K, "do_codes"))
+        quantise(do_mx, do_woven[:], 0)
+        windows = [sb.tile([P, TOKENS], F32, name="window0", tag="q_woven0", align_bytes=ALIGN)]
         nc.gpsimd.memset(windows[0][:], 0.0)
 
         ce_bank = ps.tile([P, PACK, P], F32, name="ce_bank", tag="spread0")
-        for j in range(PACK):
-            nc.tensor.transpose(ce_bank[:, j, :], ce_cols[:, j : j + 1].to_broadcast([P, P]), ident[:])
+        spread(ce_bank, ce_cols, ident)
         ce_rows = sb.tile([P, P, PACK], F32, name="ce_rows")
         nc.scalar.copy(out=ce_rows[:], in_=ce_bank[:].rearrange("p j n -> p n j"))
         ts_turned = ps.tile([P, PACK, P], F32, name="ts_turned", tag="spread1")
         for j in range(PACK):
-            nc.tensor.transpose(ts_turned[:, j, :], ts_row[:, P * j : P * (j + 1)], ident[:])
+            nc.tensor.transpose(ts_turned[:, j, :], ts_gathered[:, P * j : P * (j + 1)], ident[:])
         ts_cols = sb.tile([P, PACK], F32, name="ts_cols")
         nc.scalar.copy(out=ts_cols[:], in_=ts_turned[:, :, P - 1])
         ts_bank = ps.tile([P, PACK, P], F32, name="ts_bank", tag="spread1")
-        for j in range(PACK):
-            nc.tensor.transpose(ts_bank[:, j, :], ts_cols[:, j : j + 1].to_broadcast([P, P]), ident[:])
+        spread(ts_bank, ts_cols, ident)
         ts_rows = sb.tile([P, SLOTS], F32, name="ts_rows")
         nc.scalar.copy(out=ts_rows[:], in_=ts_bank[:].rearrange("p j n -> p (j n)"))
 
-        v_planes = shared[:, 0 : PACK * SLOTS].rearrange("p (t s) -> p t s", t=PACK)
-        v_bf = sb.tile([P, TOKENS], BF16, name="v_bf", tag="q_woven1", align_bytes=64)
+        v_planes = v_gathered[:, 0 : PACK * SLOTS].rearrange("p (t s) -> p t s", t=PACK)
+        v_bf = sb.tile([P, TOKENS], BF16, name="v_bf", tag="q_woven1", align_bytes=ALIGN)
         nc.scalar.activation(out=v_bf[:], in_=v_raw[0][:], func=COPY)
         nc.scalar.activation(out=v_planes[:, 0, :], in_=v_bf[:].indirect(offsets[:]), func=COPY)
+
         s_planes = sb.tile([P, PACK, K], BF16, name="s_planes")
         for t in range(PACK):
-            bank = ps.tile([P, K], F32, name="s_bank", tag="sum%d" % t)
-            product(bank, q_mx[t // 2], t % 2, do_mx)
+            s_bank = ps.tile([P, K], F32, name="s_bank", tag="sum%d" % t)
+            product(s_bank, q_mx[t // 2], t % 2, do_mx)
             nc.vector.scalar_tensor_tensor(
-                out=s_planes[:, t, :], in0=bank[:], scalar=cd_cols[:, t : t + 1],
+                out=s_planes[:, t, :], in0=s_bank[:], scalar=cd_cols[:, t : t + 1],
                 in1=ce_rows[:].rearrange("p n j -> p (n j)"), op0=MULT, op1=MULT)
-        se_woven1 = sb.tile([P, HALF, PACK], BF16, name="se_woven1", align_bytes=64)
-        se_woven = [shared[:, 3 * SLOTS : 5 * SLOTS].rearrange("p (c t) -> p c t", t=PACK), se_woven1[:]]
+
+        se_woven_second = sb.tile([P, HALF, PACK], BF16, name="se_woven_second", align_bytes=ALIGN)
+        se_woven = [v_gathered[:, 3 * SLOTS : 5 * SLOTS].rearrange("p (c t) -> p c t", t=PACK), se_woven_second[:]]
         for h in range(2):
             turn(se_woven[h], s_planes[:, 2 * h : 2 * h + 2, :], h, ident)
-        sd_woven = [placed.tile([P, HALF, PACK], BF16, name="sd_woven%d" % h, offset=(1024, 8192)[h], align_bytes=64) for h in range(2)]
+        sd_woven = [placed.tile([P, HALF, PACK], BF16, name="sd_woven%d" % h, offset=at, align_bytes=ALIGN)
+                    for h, at in enumerate((V2_AT + 4 * HALF, SD1_AT))]
+        se_mx = [operand("se%d" % h, E5M2, HALF, placed.tile([P, HALF], U32, name="se%d_codes" % h, offset=at, align_bytes=ALIGN))
+                 for h, at in enumerate((V1_AT, V2_AT))]
+        for t in (1, 2):
+            nc.vector.tensor_copy(out=v_planes[:, t, :], in_=v_raw[t][:].indirect(offsets[:]))
+        quantise(se_mx[0], se_woven[0], 0)
+        weave(nc.scalar.copy, sd_woven[0][:], s_planes[:, :, 0:HALF])
+        quantise(se_mx[1], se_woven[1], 0)
+
         for h in range(2):
-            weave(nc.scalar.copy, sd_woven[h][:], s_planes[:, :, HALF * h : HALF * (h + 1)])
-        se_mx = [(placed.tile([P, HALF], U32, name="se%d_codes" % h, offset=16384 * h, align_bytes=64),
-                  sb.tile([P, HALF], U8, name="se%d_scales" % h, align_bytes=64), E5M2) for h in range(2)]
-        nc.vector.tensor_copy(out=v_planes[:, 1, :], in_=v_raw[1][:].indirect(offsets[:]))
-        nc.vector.tensor_copy(out=v_planes[:, 2, :], in_=v_raw[2][:].indirect(offsets[:]))
-        quantise(se_mx[0], se_woven[0])
-        nc.vector.tensor_copy(out=v_planes[:, 3, :], in_=v_raw[3][:].indirect(offsets[:]))
-        v_woven = [sb.tile([P, HALF, PACK], BF16, name="v_woven%d" % i, align_bytes=64) for i in range(2)]
-        v_mx = operand("v", E4M3)
-        weave(nc.vector.tensor_copy, v_woven[0][:], v_planes[:, :, 0:HALF])
-        weave(nc.vector.tensor_copy, v_woven[1][:, 0:SPLIT, :], v_planes[:, :, HALF : HALF + SPLIT])
-        weave(nc.scalar.copy, v_woven[1][:, SPLIT:HALF, :], v_planes[:, :, HALF + SPLIT : SLOTS])
-        for i in range(2):
-            quantise(v_mx, v_woven[i][:], HALF * i)
-        quantise(se_mx[1], se_woven[1])
+            nc.vector.tensor_copy(out=v_planes[:, 3, HALF * h : HALF * (h + 1)],
+                                  in_=v_raw[3][:].indirect(offsets[:, HALF // 16 * h : HALF // 16 * (h + 1)]))
+        v_woven = [sb.tile([P, HALF, PACK], BF16, name="v_woven%d" % h, align_bytes=ALIGN) for h in range(2)]
+        v_mx = operand("v", E4M3, SLOTS, words("v", SLOTS, "v_codes"))
+        weave(nc.scalar.copy, v_woven[0][:, VECTOR_SHARE:HALF, :], v_planes[:, :, VECTOR_SHARE:HALF])
+        weave(nc.vector.tensor_copy, v_woven[0][:, 0:VECTOR_SHARE, :], v_planes[:, :, 0:VECTOR_SHARE])
+        weave(nc.vector.tensor_copy, v_woven[1][:], v_planes[:, :, HALF:SLOTS])
+        for h in range(2):
+            quantise(v_mx, v_woven[h][:], HALF * h)
+        weave(nc.scalar.copy, sd_woven[1][:], s_planes[:, :, HALF:K])
+
         dk_banks = [ps.tile([P, SLOTS], F32, name="dk_bank%d" % t, tag="sum%d" % t) for t in range(PACK)]
         for t in range(PACK):
             product(dk_banks[t], se_mx[t // 2], t % 2, v_mx)
 
-        sd_mx = operand("sd", E5M2, K, "v_woven0")
-        for h in range(2):
-            quantise(sd_mx, sd_woven[h][:], HALF * h)
-        k_shared = sb.tile([P, 5 * SLOTS], BF16, name="k_shared", tag="v_woven1", align_bytes=64)
-        k_planes = k_shared[:, 0 : PACK * SLOTS].rearrange("p (t s) -> p t s", t=PACK)
+        sd_mx = operand("sd", E5M2, K, words("sd", K, "v_woven0"))
+        quantise(sd_mx, sd_woven[0][:], 0)
+        k_gathered = sb.tile([P, (PACK + 1) * SLOTS], BF16, name="k_gathered", tag="v_woven1", align_bytes=ALIGN)
+        k_planes = k_gathered[:, 0 : PACK * SLOTS].rearrange("p (t s) -> p t s", t=PACK)
         nc.vector.tensor_copy(out=k_planes[:, 0, :], in_=k_raw[0][:].indirect(offsets[:]))
-        for w in (1, 2):
-            windows.append(placed.tile([P, TOKENS], F32, name="window%d" % w, offset=16384 + 8192 * w, align_bytes=64))
+        quantise(sd_mx, sd_woven[1][:], HALF)
+        for w, at in ((1, WINDOW1_AT), (2, WINDOW2_AT)):
+            windows.append(placed.tile([P, TOKENS], F32, name="window%d" % w, offset=at, align_bytes=ALIGN))
             nc.gpsimd.memset(windows[w][:], 0.0)
 
-        def empty(n, bank, tag):
-            if n == 0:
-                sums = k_shared[:, 3 * SLOTS : 5 * SLOTS].bitcast(F32)
-            else:
-                sums = sb.tile([P, SLOTS], F32, name="sums%d" % n, tag=tag, align_bytes=64)[:]
-            nc.scalar.copy(out=sums, in_=bank[:])
-            return sums
+        def sums_tile(n, tag):
+            return sb.tile([P, SLOTS], F32, name="sums%d" % n, tag=tag, align_bytes=ALIGN)[:]
 
         def scatter(n, sums, rows):
             window = windows[n % WINDOWS]
             nc.vector.tensor_tensor(out=window[:].indirect(offsets[:]), in0=sums, in1=ts_rows[:], op=MULT)
             nc.sync.dma_start(out=rows, in_=window[:])
 
-        def result_tile(n, bank, rows, tag):
-            scatter(n, empty(n, bank, tag), rows)
+        def result_tile(n, bank, sums, rows):
+            nc.scalar.copy(out=sums, in_=bank[:])
+            scatter(n, sums, rows)
 
-        dv_rows = out_1.rearrange("(j p) n -> j p n", p=P)
         dk_rows = out_0.rearrange("(m t) n -> t m n", t=PACK)
-        for t in range(2):
-            result_tile(t, dk_banks[t], dk_rows[t], "sums%d" % t)
+        dv_rows = out_1.rearrange("(j m) n -> j m n", m=P)
+        result_tile(0, dk_banks[0], k_gathered[:, 3 * SLOTS : 5 * SLOTS].bitcast(F32), dk_rows[0])
+        result_tile(1, dk_banks[1], sums_tile(1, "sums1"), dk_rows[1])
 
-        k_bf = [placed.tile([P, TOKENS], BF16, name="k_bf0", offset=0, align_bytes=64),
-                sb.tile([P, TOKENS], BF16, name="k_bf1", tag="v_codes", align_bytes=64)]
-        for t in range(2):
-            nc.scalar.activation(out=k_bf[t][:], in_=k_raw[t + 1][:], func=COPY)
+        k_bf = [placed.tile([P, TOKENS], BF16, name="k_bf1", offset=V1_AT, align_bytes=ALIGN),
+                sb.tile([P, TOKENS], BF16, name="k_bf2", tag="v_codes", align_bytes=ALIGN)]
+        for i in range(2):
+            nc.scalar.activation(out=k_bf[i][:], in_=k_raw[i + 1][:], func=COPY)
         nc.scalar.activation(out=k_planes[:, 1, :], in_=k_bf[0][:].indirect(offsets[:]), func=COPY)
-        sums2 = empty(2, dk_banks[2], "k_raw2")
+        third_sums = sums_tile(2, "k_raw2")
+        nc.scalar.copy(out=third_sums, in_=dk_banks[2][:])
         nc.scalar.activation(out=k_planes[:, 2, :], in_=k_bf[1][:].indirect(offsets[:]), func=COPY)
         nc.vector.tensor_copy(out=k_planes[:, 3, :], in_=k_raw[3][:].indirect(offsets[:]))
-        scatter(2, sums2, dk_rows[2])
-        k_woven = sb.tile([P, SLOTS, PACK], BF16, name="k_woven", align_bytes=64)
+        scatter(2, third_sums, dk_rows[2])
+        k_woven = sb.tile([P, SLOTS, PACK], BF16, name="k_woven", align_bytes=ALIGN)
         weave(nc.scalar.copy, k_woven[:], k_planes)
-        k_mx = operand("k", E4M3)
-        quantise(k_mx, k_woven[:])
-        result_tile(3, dk_banks[3], dk_rows[3], "v_woven1")
+        k_mx = operand("k", E4M3, SLOTS, words("k", SLOTS, "k_codes"))
+        quantise(k_mx, k_woven[:], 0)
+        result_tile(3, dk_banks[3], sums_tile(3, "v_woven1"), dk_rows[3])
+
         for j in range(PACK):
-            bank = ps.tile([P, SLOTS], F32, name="dv_bank", tag="sum%d" % j)
-            product(bank, sd_mx, j, k_mx)
-            result_tile(PACK + j, bank, dv_rows[j], "sums%d" % (PACK + j))
+            dv_bank = ps.tile([P, SLOTS], F32, name="dv_bank", tag="sum%d" % j)
+            product(dv_bank, sd_mx, j, k_mx)
+            result_tile(PACK + j, dv_bank, sums_tile(PACK + j, "sums%d" % (PACK + j)), dv_rows[j])

@@ -18,18 +18,17 @@ K = 512
 TOKENS = 2048
 SLOTS = 512
 HALF = 256
-VECTOR_SHARE = 64
 WINDOWS = 3
 ALIGN = 64
 FLOPS = 3 * 2 * K * K * K
 
 PLANE = 4 * TOKENS
-V1_AT = 0
-V2_AT = PLANE
-V3_AT = 2 * PLANE
-WINDOW1_AT = 3 * PLANE
-WINDOW2_AT = 4 * PLANE
+WINDOW1_AT = 0
+WINDOW2_AT = PLANE
 SD1_AT = WINDOW2_AT - 1024
+K_PAIRS_AT = 2 * PLANE
+V_WOVEN1_AT = K_PAIRS_AT + 3072
+K_LAST_AT = K_PAIRS_AT + 4096
 GATHERED_AT = WINDOW2_AT - 3072
 
 
@@ -42,6 +41,13 @@ def tile_attend_glin_kv_kernel(tc, kT, vT, cd, ce, do, qT, ts, offs, out_0, out_
 
         def weave(engine_copy, woven, planes):
             engine_copy(out=woven.rearrange("p (c i) t -> p c t i", i=4), in_=planes.rearrange("p t (c i) -> p c t i", i=4))
+
+        def place(pairs, t):
+            return pairs.rearrange("p (u s j) -> p u s j", u=2, j=2)[:, t // 2, :, t % 2]
+
+        def weave_pairs(woven, pairs, slots):
+            nc.scalar.copy(out=woven.rearrange("p c t -> p (c t)").bitcast(U32).rearrange("p (s u) -> p s u", u=2),
+                           in_=pairs.bitcast(U32).rearrange("p (u s) -> p s u", u=2)[:, slots, :])
 
         def operand(name, fmt, width, codes):
             scales = sb.tile([P, width], U8, name=name + "_scales", align_bytes=ALIGN)
@@ -82,9 +88,12 @@ def tile_attend_glin_kv_kernel(tc, kT, vT, cd, ce, do, qT, ts, offs, out_0, out_
 
         offsets = sb.tile([P, SLOTS // 16], U16, name="offsets")
         q_raw = [sb.tile([P, 2, K], F32, name="q_raw%d" % h, align_bytes=ALIGN) for h in range(2)]
-        do_raw = sb.tile([P, PACK, K], F32, name="do_raw")
-        v_gathered = placed.tile([P, (PACK + 1) * SLOTS], BF16, name="v_gathered", offset=GATHERED_AT, align_bytes=ALIGN)
-        cd_cols = v_gathered[:, 2 * SLOTS - 6 : 2 * SLOTS + 2].bitcast(F32)
+        do_raw = sb.tile([P, PACK, K], F32, name="do_raw", align_bytes=ALIGN)
+        v_tile = placed.tile([P, PACK * SLOTS], BF16, name="v_tile", offset=GATHERED_AT, align_bytes=ALIGN)
+        v_pairs = v_tile[:]
+        v_early = sb.tile([P, 4 * SLOTS + 8], BF16, name="v_early", align_bytes=ALIGN)
+        v_first = v_early[:, 2 * SLOTS - 32 : 4 * SLOTS - 32]
+        cd_cols = v_early[:, 4 * SLOTS - 34 : 4 * SLOTS - 26].bitcast(F32)
         ce_cols = sb.tile([P, PACK], F32, name="ce_cols", align_bytes=ALIGN)
         ts_pool = sb.tile([P, TOKENS], F32, name="ts_pool", align_bytes=ALIGN)
         q_rows = qT.rearrange("(m t) r -> m t r", t=PACK)
@@ -97,16 +106,14 @@ def tile_attend_glin_kv_kernel(tc, kT, vT, cd, ce, do, qT, ts, offs, out_0, out_
         nc.sync.dma_start(out=do_raw[:], in_=do.rearrange("(p t) e -> p t e", t=PACK))
         k_rows = kT.rearrange("(p t) n -> t p n", t=PACK)
         v_rows = vT.rearrange("(p t) n -> t p n", t=PACK)
-        k_raw = [sb.tile([P, TOKENS], F32, name="k_raw%d" % t, align_bytes=ALIGN) for t in range(PACK)]
-        v_raw = [sb.tile([P, TOKENS], F32, name="v_raw0", align_bytes=ALIGN)]
-        for t, at in ((1, V1_AT), (2, V2_AT), (3, V3_AT)):
-            v_raw.append(placed.tile([P, TOKENS], F32, name="v_raw%d" % t, offset=at, align_bytes=ALIGN))
+        k_raw = {t: sb.tile([P, TOKENS], F32, name="k_raw%d" % t, align_bytes=ALIGN) for t in (0, 2, 3)}
+        v_raw = [sb.tile([P, TOKENS], F32, name="v_raw%d" % t, align_bytes=ALIGN) for t in range(PACK)]
         for t in range(PACK):
             nc.sync.dma_start(out=v_raw[t][:], in_=v_rows[t])
-        for t in range(PACK):
+        for t in (0, 2, 3):
             nc.sync.dma_start(out=k_raw[t][:], in_=k_rows[t])
 
-        ident = sb.tile([P, P], F32, name="ident")
+        ident = sb.tile([P, P], F32, name="ident", align_bytes=ALIGN)
         nc.gpsimd.memset(ident[:], 0.0)
         nc.gpsimd.affine_select(out=ident[:], in_=ident[:], compare_op=mybir.AluOpType.not_equal, fill=1.0, base=0,
                                 pattern=[[-1, P]], channel_multiplier=1)
@@ -115,17 +122,18 @@ def tile_attend_glin_kv_kernel(tc, kT, vT, cd, ce, do, qT, ts, offs, out_0, out_
         ts_gathered = sb.tile([P, SLOTS], F32, name="ts_gathered")
         nc.vector.tensor_copy(out=ts_gathered[:], in_=ts_pool[:].indirect(offsets[:]))
 
-        q_bf = [sb.tile([P, 2, K], BF16, name="q_bf%d" % h) for h in range(2)]
+        q_bf = [sb.tile([P, 2, K], BF16, name="q_bf%d" % h, align_bytes=ALIGN) for h in range(2)]
         for h in range(2):
             nc.vector.tensor_copy(out=q_bf[h][:], in_=q_raw[h][:])
-        q_woven = [sb.tile([P, HALF, PACK], BF16, name="q_woven%d" % h, align_bytes=ALIGN) for h in range(2)]
+        q_woven_first = sb.tile([P, HALF, PACK], BF16, name="q_woven0", align_bytes=ALIGN)
+        q_woven = [q_woven_first[:], v_early[:, 0 : 2 * SLOTS].rearrange("p (c t) -> p c t", t=PACK)]
         q_mx = [operand("q%d" % h, E4M3, HALF, words("q%d" % h, HALF, "q%d_codes" % h)) for h in range(2)]
         for h in range(2):
-            turn(q_woven[h][:], q_bf[h], h, ident)
-        quantise(q_mx[0], q_woven[0][:], 0)
+            turn(q_woven[h], q_bf[h], h, ident)
+        quantise(q_mx[0], q_woven[0], 0)
         do_woven = sb.tile([P, K, PACK], BF16, name="do_woven", tag="q_woven0", align_bytes=ALIGN)
         weave(nc.vector.tensor_copy, do_woven[:], do_raw[:])
-        quantise(q_mx[1], q_woven[1][:], 0)
+        quantise(q_mx[1], q_woven[1], 0)
         do_mx = operand("do", E5M2, K, words("do", K, "do_codes"))
         quantise(do_mx, do_woven[:], 0)
         windows = [sb.tile([P, TOKENS], F32, name="window0", tag="q_woven0", align_bytes=ALIGN)]
@@ -145,10 +153,10 @@ def tile_attend_glin_kv_kernel(tc, kT, vT, cd, ce, do, qT, ts, offs, out_0, out_
         ts_rows = sb.tile([P, SLOTS], F32, name="ts_rows")
         nc.scalar.copy(out=ts_rows[:], in_=ts_bank[:].rearrange("p j n -> p (j n)"))
 
-        v_planes = v_gathered[:, 0 : PACK * SLOTS].rearrange("p (t s) -> p t s", t=PACK)
-        v_bf = sb.tile([P, TOKENS], BF16, name="v_bf", tag="q_woven1", align_bytes=ALIGN)
+        v_bf = sb.tile([P, TOKENS], BF16, name="v_bf", tag="q_bf1", align_bytes=ALIGN)
         nc.scalar.activation(out=v_bf[:], in_=v_raw[0][:], func=COPY)
-        nc.scalar.activation(out=v_planes[:, 0, :], in_=v_bf[:].indirect(offsets[:]), func=COPY)
+        nc.scalar.activation(out=v_first[:, HALF:SLOTS], in_=v_bf[:].indirect(offsets[:, HALF // 16 :]), func=COPY)
+        nc.vector.tensor_copy(out=v_first[:, 0:HALF], in_=v_raw[0][:].indirect(offsets[:, 0 : HALF // 16]))
 
         s_planes = sb.tile([P, PACK, K], BF16, name="s_planes")
         for t in range(PACK):
@@ -158,28 +166,30 @@ def tile_attend_glin_kv_kernel(tc, kT, vT, cd, ce, do, qT, ts, offs, out_0, out_
                 out=s_planes[:, t, :], in0=s_bank[:], scalar=cd_cols[:, t : t + 1],
                 in1=ce_rows[:].rearrange("p n j -> p (n j)"), op0=MULT, op1=MULT)
 
-        se_woven_second = sb.tile([P, HALF, PACK], BF16, name="se_woven_second", align_bytes=ALIGN)
-        se_woven = [v_gathered[:, 3 * SLOTS : 5 * SLOTS].rearrange("p (c t) -> p c t", t=PACK), se_woven_second[:]]
+        se_woven = [v_tile[:, at : at + 2 * SLOTS].rearrange("p (c t) -> p c t", t=PACK) for at in (2 * SLOTS, 0)]
         for h in range(2):
             turn(se_woven[h], s_planes[:, 2 * h : 2 * h + 2, :], h, ident)
-        sd_woven = [placed.tile([P, HALF, PACK], BF16, name="sd_woven%d" % h, offset=at, align_bytes=ALIGN)
-                    for h, at in enumerate((V2_AT + 4 * HALF, SD1_AT))]
-        se_mx = [operand("se%d" % h, E5M2, HALF, placed.tile([P, HALF], U32, name="se%d_codes" % h, offset=at, align_bytes=ALIGN))
-                 for h, at in enumerate((V1_AT, V2_AT))]
-        for t in (1, 2):
-            nc.vector.tensor_copy(out=v_planes[:, t, :], in_=v_raw[t][:].indirect(offsets[:]))
-        quantise(se_mx[0], se_woven[0], 0)
-        weave(nc.scalar.copy, sd_woven[0][:], s_planes[:, :, 0:HALF])
-        quantise(se_mx[1], se_woven[1], 0)
+        sd_woven = [sb.tile([P, HALF, PACK], BF16, name="sd_woven0", tag="ident", align_bytes=ALIGN)[:],
+                    placed.tile([P, HALF, PACK], BF16, name="sd_woven1", offset=SD1_AT, align_bytes=ALIGN)]
+        se_mx = [operand("se%d" % h, E5M2, HALF, words("se%d" % h, HALF, "se%d_codes" % h)) for h in range(2)]
+        nc.vector.tensor_copy(out=v_first[:, SLOTS : 2 * SLOTS], in_=v_raw[1][:].indirect(offsets[:]))
+        for h in range(2):
+            quantise(se_mx[h], se_woven[h], 0)
+        weave(nc.scalar.copy, sd_woven[0], s_planes[:, :, 0:HALF])
+        nc.scalar.copy(out=v_pairs[:, 0 : 2 * SLOTS].rearrange("p (c i j) -> p c j i", i=4, j=2),
+                       in_=v_first[:, 0 : 2 * SLOTS].rearrange("p (j c i) -> p c j i", i=4, j=2))
+        nc.vector.tensor_copy(out=place(v_pairs, 2), in_=v_raw[2][:].indirect(offsets[:]))
 
         for h in range(2):
-            nc.vector.tensor_copy(out=v_planes[:, 3, HALF * h : HALF * (h + 1)],
+            nc.vector.tensor_copy(out=place(v_pairs, 3)[:, HALF * h : HALF * (h + 1)],
                                   in_=v_raw[3][:].indirect(offsets[:, HALF // 16 * h : HALF // 16 * (h + 1)]))
-        v_woven = [sb.tile([P, HALF, PACK], BF16, name="v_woven%d" % h, align_bytes=ALIGN) for h in range(2)]
+        sd_mx = operand("sd", E5M2, K, words("sd", K, "sd_codes"))
+        quantise(sd_mx, sd_woven[0], 0)
+        v_woven = [sb.tile([P, HALF, PACK], BF16, name="v_woven0", align_bytes=ALIGN),
+                   placed.tile([P, HALF, PACK], BF16, name="v_woven1", offset=V_WOVEN1_AT, align_bytes=ALIGN)]
         v_mx = operand("v", E4M3, SLOTS, words("v", SLOTS, "v_codes"))
-        weave(nc.scalar.copy, v_woven[0][:, VECTOR_SHARE:HALF, :], v_planes[:, :, VECTOR_SHARE:HALF])
-        weave(nc.vector.tensor_copy, v_woven[0][:, 0:VECTOR_SHARE, :], v_planes[:, :, 0:VECTOR_SHARE])
-        weave(nc.vector.tensor_copy, v_woven[1][:], v_planes[:, :, HALF:SLOTS])
+        for h in range(2):
+            weave_pairs(v_woven[h][:], v_pairs, slice(HALF * h, HALF * (h + 1)))
         for h in range(2):
             quantise(v_mx, v_woven[h][:], HALF * h)
         weave(nc.scalar.copy, sd_woven[1][:], s_planes[:, :, HALF:K])
@@ -188,11 +198,10 @@ def tile_attend_glin_kv_kernel(tc, kT, vT, cd, ce, do, qT, ts, offs, out_0, out_
         for t in range(PACK):
             product(dk_banks[t], se_mx[t // 2], t % 2, v_mx)
 
-        sd_mx = operand("sd", E5M2, K, words("sd", K, "v_woven0"))
-        quantise(sd_mx, sd_woven[0][:], 0)
-        k_gathered = sb.tile([P, (PACK + 1) * SLOTS], BF16, name="k_gathered", tag="v_woven1", align_bytes=ALIGN)
-        k_planes = k_gathered[:, 0 : PACK * SLOTS].rearrange("p (t s) -> p t s", t=PACK)
-        nc.vector.tensor_copy(out=k_planes[:, 0, :], in_=k_raw[0][:].indirect(offsets[:]))
+        k_pairs = placed.tile([P, PACK * SLOTS], BF16, name="k_pairs", offset=K_PAIRS_AT, align_bytes=ALIGN)
+        nc.vector.tensor_copy(out=place(k_pairs[:], 0), in_=k_raw[0][:].indirect(offsets[:]))
+        k_raw[1] = placed.tile([P, TOKENS], F32, name="k_raw1", offset=K_LAST_AT, align_bytes=ALIGN)
+        nc.sync.dma_start(out=k_raw[1][:], in_=k_rows[1])
         quantise(sd_mx, sd_woven[1][:], HALF)
         for w, at in ((1, WINDOW1_AT), (2, WINDOW2_AT)):
             windows.append(placed.tile([P, TOKENS], F32, name="window%d" % w, offset=at, align_bytes=ALIGN))
@@ -212,24 +221,25 @@ def tile_attend_glin_kv_kernel(tc, kT, vT, cd, ce, do, qT, ts, offs, out_0, out_
 
         dk_rows = out_0.rearrange("(m t) n -> t m n", t=PACK)
         dv_rows = out_1.rearrange("(j m) n -> j m n", m=P)
-        result_tile(0, dk_banks[0], k_gathered[:, 3 * SLOTS : 5 * SLOTS].bitcast(F32), dk_rows[0])
-        result_tile(1, dk_banks[1], sums_tile(1, "sums1"), dk_rows[1])
+        for t in range(2):
+            result_tile(t, dk_banks[t], sums_tile(t, "sums%d" % t), dk_rows[t])
 
-        k_bf = [placed.tile([P, TOKENS], BF16, name="k_bf1", offset=V1_AT, align_bytes=ALIGN),
-                sb.tile([P, TOKENS], BF16, name="k_bf2", tag="v_codes", align_bytes=ALIGN)]
-        for i in range(2):
-            nc.scalar.activation(out=k_bf[i][:], in_=k_raw[i + 1][:], func=COPY)
-        nc.scalar.activation(out=k_planes[:, 1, :], in_=k_bf[0][:].indirect(offsets[:]), func=COPY)
-        third_sums = sums_tile(2, "k_raw2")
+        k_bf = {2: sb.tile([P, TOKENS], BF16, name="k_bf2", tag="se0_codes", align_bytes=ALIGN),
+                3: sb.tile([P, TOKENS], BF16, name="k_bf3", tag="v_codes", align_bytes=ALIGN)}
+        for t in (2, 3):
+            nc.scalar.activation(out=k_bf[t][:], in_=k_raw[t][:], func=COPY)
+        nc.scalar.activation(out=place(k_pairs[:], 2), in_=k_bf[2][:].indirect(offsets[:]), func=COPY)
+        third_sums = sums_tile(2, "k_raw3")
         nc.scalar.copy(out=third_sums, in_=dk_banks[2][:])
-        nc.scalar.activation(out=k_planes[:, 2, :], in_=k_bf[1][:].indirect(offsets[:]), func=COPY)
-        nc.vector.tensor_copy(out=k_planes[:, 3, :], in_=k_raw[3][:].indirect(offsets[:]))
+        nc.scalar.activation(out=place(k_pairs[:], 3), in_=k_bf[3][:].indirect(offsets[:]), func=COPY)
+        nc.vector.tensor_copy(out=place(k_pairs[:], 1), in_=k_raw[1][:].indirect(offsets[:]))
         scatter(2, third_sums, dk_rows[2])
         k_woven = sb.tile([P, SLOTS, PACK], BF16, name="k_woven", align_bytes=ALIGN)
-        weave(nc.scalar.copy, k_woven[:], k_planes)
+        weave_pairs(k_woven[:], k_pairs[:], slice(0, SLOTS))
         k_mx = operand("k", E4M3, SLOTS, words("k", SLOTS, "k_codes"))
         quantise(k_mx, k_woven[:], 0)
-        result_tile(3, dk_banks[3], sums_tile(3, "v_woven1"), dk_rows[3])
+        fourth_sums = placed.tile([P, SLOTS], F32, name="sums3", offset=K_PAIRS_AT, align_bytes=ALIGN)
+        result_tile(3, dk_banks[3], fourth_sums[:], dk_rows[3])
 
         for j in range(PACK):
             dv_bank = ps.tile([P, SLOTS], F32, name="dv_bank", tag="sum%d" % j)

@@ -25,11 +25,14 @@ FLOPS = 3 * 2 * K * K * K
 PLANE = 4 * TOKENS
 WINDOW1_AT = 0
 WINDOW2_AT = PLANE
-SD1_AT = WINDOW2_AT - 1024
-K_PAIRS_AT = 2 * PLANE
-V_WOVEN1_AT = K_PAIRS_AT + 3072
-K_LAST_AT = K_PAIRS_AT + 4096
-GATHERED_AT = WINDOW2_AT - 3072
+SD_AT = WINDOW2_AT - 2048
+SE0_AT = WINDOW2_AT - 1024
+K_GATHERED_AT = 2 * PLANE
+V_WOVEN0_AT = K_GATHERED_AT + 5120 - ALIGN
+SE1_SCALES_AT = V_WOVEN0_AT + 256
+SD_SCALES_AT = V_WOVEN0_AT + 512
+IDENT_AT = V_WOVEN0_AT + 2048
+V_WOVEN1_AT = IDENT_AT + 512 - ALIGN
 
 
 def tile_attend_glin_kv_kernel(tc, kT, vT, cd, ce, do, qT, ts, offs, out_0, out_1):
@@ -42,15 +45,11 @@ def tile_attend_glin_kv_kernel(tc, kT, vT, cd, ce, do, qT, ts, offs, out_0, out_
         def weave(engine_copy, woven, planes):
             engine_copy(out=woven.rearrange("p (c i) t -> p c t i", i=4), in_=planes.rearrange("p t (c i) -> p c t i", i=4))
 
-        def place(pairs, t):
-            return pairs.rearrange("p (u s j) -> p u s j", u=2, j=2)[:, t // 2, :, t % 2]
-
-        def weave_pairs(woven, pairs, slots):
-            nc.scalar.copy(out=woven.rearrange("p c t -> p (c t)").bitcast(U32).rearrange("p (s u) -> p s u", u=2),
-                           in_=pairs.bitcast(U32).rearrange("p (u s) -> p s u", u=2)[:, slots, :])
-
-        def operand(name, fmt, width, codes):
-            scales = sb.tile([P, width], U8, name=name + "_scales", align_bytes=ALIGN)
+        def operand(name, fmt, width, codes, scales_at=None):
+            if scales_at is None:
+                scales = sb.tile([P, width], U8, name=name + "_scales", align_bytes=ALIGN)
+            else:
+                scales = placed.tile([P, width], U8, name=name + "_scales", offset=scales_at, align_bytes=ALIGN)
             return codes, scales, fmt
 
         def words(name, width, tag):
@@ -89,8 +88,6 @@ def tile_attend_glin_kv_kernel(tc, kT, vT, cd, ce, do, qT, ts, offs, out_0, out_
         offsets = sb.tile([P, SLOTS // 16], U16, name="offsets")
         q_raw = [sb.tile([P, 2, K], F32, name="q_raw%d" % h, align_bytes=ALIGN) for h in range(2)]
         do_raw = sb.tile([P, PACK, K], F32, name="do_raw", align_bytes=ALIGN)
-        v_tile = placed.tile([P, PACK * SLOTS], BF16, name="v_tile", offset=GATHERED_AT, align_bytes=ALIGN)
-        v_pairs = v_tile[:]
         v_early = sb.tile([P, 4 * SLOTS + 8], BF16, name="v_early", align_bytes=ALIGN)
         v_first = v_early[:, 2 * SLOTS - 32 : 4 * SLOTS - 32]
         cd_cols = v_early[:, 4 * SLOTS - 34 : 4 * SLOTS - 26].bitcast(F32)
@@ -106,14 +103,14 @@ def tile_attend_glin_kv_kernel(tc, kT, vT, cd, ce, do, qT, ts, offs, out_0, out_
         nc.sync.dma_start(out=do_raw[:], in_=do.rearrange("(p t) e -> p t e", t=PACK))
         k_rows = kT.rearrange("(p t) n -> t p n", t=PACK)
         v_rows = vT.rearrange("(p t) n -> t p n", t=PACK)
-        k_raw = {t: sb.tile([P, TOKENS], F32, name="k_raw%d" % t, align_bytes=ALIGN) for t in (0, 2, 3)}
+        k_raw = [sb.tile([P, TOKENS], F32, name="k_raw%d" % t, align_bytes=ALIGN) for t in range(PACK)]
         v_raw = [sb.tile([P, TOKENS], F32, name="v_raw%d" % t, align_bytes=ALIGN) for t in range(PACK)]
         for t in range(PACK):
             nc.sync.dma_start(out=v_raw[t][:], in_=v_rows[t])
-        for t in (0, 2, 3):
+        for t in range(PACK):
             nc.sync.dma_start(out=k_raw[t][:], in_=k_rows[t])
 
-        ident = sb.tile([P, P], F32, name="ident", align_bytes=ALIGN)
+        ident = placed.tile([P, P], F32, name="ident", offset=IDENT_AT, align_bytes=ALIGN)
         nc.gpsimd.memset(ident[:], 0.0)
         nc.gpsimd.affine_select(out=ident[:], in_=ident[:], compare_op=mybir.AluOpType.not_equal, fill=1.0, base=0,
                                 pattern=[[-1, P]], channel_multiplier=1)
@@ -166,43 +163,43 @@ def tile_attend_glin_kv_kernel(tc, kT, vT, cd, ce, do, qT, ts, offs, out_0, out_
                 out=s_planes[:, t, :], in0=s_bank[:], scalar=cd_cols[:, t : t + 1],
                 in1=ce_rows[:].rearrange("p n j -> p (n j)"), op0=MULT, op1=MULT)
 
-        se_woven = [v_tile[:, at : at + 2 * SLOTS].rearrange("p (c t) -> p c t", t=PACK) for at in (2 * SLOTS, 0)]
+        se_woven = [placed.tile([P, HALF, PACK], BF16, name="se_woven0", offset=SE0_AT, align_bytes=ALIGN),
+                    sb.tile([P, HALF, PACK], BF16, name="se_woven1", align_bytes=ALIGN)]
         for h in range(2):
-            turn(se_woven[h], s_planes[:, 2 * h : 2 * h + 2, :], h, ident)
-        sd_woven = [sb.tile([P, HALF, PACK], BF16, name="sd_woven0", tag="ident", align_bytes=ALIGN)[:],
-                    placed.tile([P, HALF, PACK], BF16, name="sd_woven1", offset=SD1_AT, align_bytes=ALIGN)]
-        se_mx = [operand("se%d" % h, E5M2, HALF, words("se%d" % h, HALF, "se%d_codes" % h)) for h in range(2)]
+            turn(se_woven[h][:], s_planes[:, 2 * h : 2 * h + 2, :], h, ident)
         nc.vector.tensor_copy(out=v_first[:, SLOTS : 2 * SLOTS], in_=v_raw[1][:].indirect(offsets[:]))
-        for h in range(2):
-            quantise(se_mx[h], se_woven[h], 0)
-        weave(nc.scalar.copy, sd_woven[0], s_planes[:, :, 0:HALF])
-        nc.scalar.copy(out=v_pairs[:, 0 : 2 * SLOTS].rearrange("p (c i j) -> p c j i", i=4, j=2),
-                       in_=v_first[:, 0 : 2 * SLOTS].rearrange("p (j c i) -> p c j i", i=4, j=2))
-        nc.vector.tensor_copy(out=place(v_pairs, 2), in_=v_raw[2][:].indirect(offsets[:]))
+        se_mx = [operand("se0", E5M2, HALF, words("se0", HALF, "se0_codes"))]
+        quantise(se_mx[0], se_woven[0][:], 0)
 
+        v_tiles = [placed.tile([P, HALF * PACK + ALIGN // 2], BF16, name="v_woven%d" % h, offset=at, align_bytes=ALIGN)
+                   for h, at in enumerate((V_WOVEN0_AT, V_WOVEN1_AT))]
+        v_woven = [v_tiles[h][:, ALIGN // 2 * h : ALIGN // 2 * h + HALF * PACK].rearrange("p (c t) -> p c t", t=PACK) for h in range(2)]
         for h in range(2):
-            nc.vector.tensor_copy(out=place(v_pairs, 3)[:, HALF * h : HALF * (h + 1)],
-                                  in_=v_raw[3][:].indirect(offsets[:, HALF // 16 * h : HALF // 16 * (h + 1)]))
-        sd_mx = operand("sd", E5M2, K, words("sd", K, "sd_codes"))
-        quantise(sd_mx, sd_woven[0], 0)
-        v_woven = [sb.tile([P, HALF, PACK], BF16, name="v_woven0", align_bytes=ALIGN),
-                   placed.tile([P, HALF, PACK], BF16, name="v_woven1", offset=V_WOVEN1_AT, align_bytes=ALIGN)]
+            nc.scalar.copy(out=v_woven[h][:, :, 0:2],
+                           in_=v_first.rearrange("p (j s) -> p s j", j=2)[:, HALF * h : HALF * (h + 1), :])
+        for t in (2, 3):
+            for h in range(2):
+                nc.vector.tensor_copy(out=v_woven[h][:, :, t],
+                                      in_=v_raw[t][:].indirect(offsets[:, HALF // 16 * h : HALF // 16 * (h + 1)]))
         v_mx = operand("v", E4M3, SLOTS, words("v", SLOTS, "v_codes"))
         for h in range(2):
-            weave_pairs(v_woven[h][:], v_pairs, slice(HALF * h, HALF * (h + 1)))
+            quantise(v_mx, v_woven[h], HALF * h)
+        sd_woven = placed.tile([P, K, PACK], BF16, name="sd_woven", offset=SD_AT, align_bytes=ALIGN)
         for h in range(2):
-            quantise(v_mx, v_woven[h][:], HALF * h)
-        weave(nc.scalar.copy, sd_woven[1][:], s_planes[:, :, HALF:K])
+            weave(nc.scalar.copy, sd_woven[:, HALF * h : HALF * (h + 1), :], s_planes[:, :, HALF * h : HALF * (h + 1)])
+        se_mx.append(operand("se1", E5M2, HALF, words("se1", HALF, "se1_codes"), SE1_SCALES_AT))
+        quantise(se_mx[1], se_woven[1][:], 0)
+        sd_mx = operand("sd", E5M2, K, words("sd", K, "sd_codes"), SD_SCALES_AT)
+        quantise(sd_mx, sd_woven[:, 0:HALF, :], 0)
 
         dk_banks = [ps.tile([P, SLOTS], F32, name="dk_bank%d" % t, tag="sum%d" % t) for t in range(PACK)]
         for t in range(PACK):
             product(dk_banks[t], se_mx[t // 2], t % 2, v_mx)
 
-        k_pairs = placed.tile([P, PACK * SLOTS], BF16, name="k_pairs", offset=K_PAIRS_AT, align_bytes=ALIGN)
-        nc.vector.tensor_copy(out=place(k_pairs[:], 0), in_=k_raw[0][:].indirect(offsets[:]))
-        k_raw[1] = placed.tile([P, TOKENS], F32, name="k_raw1", offset=K_LAST_AT, align_bytes=ALIGN)
-        nc.sync.dma_start(out=k_raw[1][:], in_=k_rows[1])
-        quantise(sd_mx, sd_woven[1][:], HALF)
+        k_gathered = placed.tile([P, (PACK + 1) * SLOTS], BF16, name="k_gathered", offset=K_GATHERED_AT, align_bytes=ALIGN)
+        k_planes = k_gathered[:, 0 : PACK * SLOTS].rearrange("p (t s) -> p t s", t=PACK)
+        nc.vector.tensor_copy(out=k_planes[:, 0, :], in_=k_raw[0][:].indirect(offsets[:]))
+        quantise(sd_mx, sd_woven[:, HALF:K, :], HALF)
         for w, at in ((1, WINDOW1_AT), (2, WINDOW2_AT)):
             windows.append(placed.tile([P, TOKENS], F32, name="window%d" % w, offset=at, align_bytes=ALIGN))
             nc.gpsimd.memset(windows[w][:], 0.0)
@@ -221,24 +218,24 @@ def tile_attend_glin_kv_kernel(tc, kT, vT, cd, ce, do, qT, ts, offs, out_0, out_
 
         dk_rows = out_0.rearrange("(m t) n -> t m n", t=PACK)
         dv_rows = out_1.rearrange("(j m) n -> j m n", m=P)
-        for t in range(2):
-            result_tile(t, dk_banks[t], sums_tile(t, "sums%d" % t), dk_rows[t])
+        result_tile(0, dk_banks[0], k_gathered[:, 3 * SLOTS : 5 * SLOTS].bitcast(F32), dk_rows[0])
+        result_tile(1, dk_banks[1], sums_tile(1, "sums1"), dk_rows[1])
 
-        k_bf = {2: sb.tile([P, TOKENS], BF16, name="k_bf2", tag="se0_codes", align_bytes=ALIGN),
-                3: sb.tile([P, TOKENS], BF16, name="k_bf3", tag="v_codes", align_bytes=ALIGN)}
-        for t in (2, 3):
-            nc.scalar.activation(out=k_bf[t][:], in_=k_raw[t][:], func=COPY)
-        nc.scalar.activation(out=place(k_pairs[:], 2), in_=k_bf[2][:].indirect(offsets[:]), func=COPY)
-        third_sums = sums_tile(2, "k_raw3")
+        k_bf = [sb.tile([P, TOKENS], BF16, name="k_bf1", tag="se0_codes", align_bytes=ALIGN),
+                sb.tile([P, TOKENS], BF16, name="k_bf2", tag="v_codes", align_bytes=ALIGN)]
+        for i in range(2):
+            nc.scalar.activation(out=k_bf[i][:], in_=k_raw[i + 1][:], func=COPY)
+        nc.scalar.activation(out=k_planes[:, 1, :], in_=k_bf[0][:].indirect(offsets[:]), func=COPY)
+        third_sums = sums_tile(2, "k_raw2")
         nc.scalar.copy(out=third_sums, in_=dk_banks[2][:])
-        nc.scalar.activation(out=place(k_pairs[:], 3), in_=k_bf[3][:].indirect(offsets[:]), func=COPY)
-        nc.vector.tensor_copy(out=place(k_pairs[:], 1), in_=k_raw[1][:].indirect(offsets[:]))
+        nc.scalar.activation(out=k_planes[:, 2, :], in_=k_bf[1][:].indirect(offsets[:]), func=COPY)
+        nc.vector.tensor_copy(out=k_planes[:, 3, :], in_=k_raw[3][:].indirect(offsets[:]))
         scatter(2, third_sums, dk_rows[2])
         k_woven = sb.tile([P, SLOTS, PACK], BF16, name="k_woven", align_bytes=ALIGN)
-        weave_pairs(k_woven[:], k_pairs[:], slice(0, SLOTS))
+        weave(nc.scalar.copy, k_woven[:], k_planes)
         k_mx = operand("k", E4M3, SLOTS, words("k", SLOTS, "k_codes"))
         quantise(k_mx, k_woven[:], 0)
-        fourth_sums = placed.tile([P, SLOTS], F32, name="sums3", offset=K_PAIRS_AT, align_bytes=ALIGN)
+        fourth_sums = placed.tile([P, SLOTS], F32, name="sums3", offset=K_GATHERED_AT, align_bytes=ALIGN)
         result_tile(3, dk_banks[3], fourth_sums[:], dk_rows[3])
 
         for j in range(PACK):

@@ -18,6 +18,8 @@ K = 512
 TOKENS = 2048
 SLOTS = 512
 HALF = 256
+DO_VECTOR = 336
+Q_WOVEN_AT = 288
 WINDOWS = 3
 ALIGN = 64
 FLOPS = 3 * 2 * K * K * K
@@ -88,9 +90,9 @@ def tile_attend_glin_kv_kernel(tc, kT, vT, cd, ce, do, qT, ts, offs, out_0, out_
         offsets = sb.tile([P, SLOTS // 16], U16, name="offsets")
         q_raw = [sb.tile([P, 2, K], F32, name="q_raw%d" % h, align_bytes=ALIGN) for h in range(2)]
         do_raw = sb.tile([P, PACK, K], F32, name="do_raw", align_bytes=ALIGN)
-        v_early = sb.tile([P, 4 * SLOTS + 8], BF16, name="v_early", align_bytes=ALIGN)
-        v_first = v_early[:, 2 * SLOTS - 32 : 4 * SLOTS - 32]
-        cd_cols = v_early[:, 4 * SLOTS - 34 : 4 * SLOTS - 26].bitcast(F32)
+        early = sb.tile([P, 6 * SLOTS + 8], BF16, name="early", align_bytes=ALIGN)
+        v_first = early[:, 4 * SLOTS - 32 : 6 * SLOTS - 32]
+        cd_cols = early[:, 6 * SLOTS - 34 : 6 * SLOTS - 26].bitcast(F32)
         ce_cols = sb.tile([P, PACK], F32, name="ce_cols", align_bytes=ALIGN)
         ts_pool = sb.tile([P, TOKENS], F32, name="ts_pool", align_bytes=ALIGN)
         q_rows = qT.rearrange("(m t) r -> m t r", t=PACK)
@@ -115,31 +117,26 @@ def tile_attend_glin_kv_kernel(tc, kT, vT, cd, ce, do, qT, ts, offs, out_0, out_
         nc.gpsimd.affine_select(out=ident[:], in_=ident[:], compare_op=mybir.AluOpType.not_equal, fill=1.0, base=0,
                                 pattern=[[-1, P]], channel_multiplier=1)
 
+        ce_bank = ps.tile([P, PACK, P], F32, name="ce_bank", tag="spread0")
+        spread(ce_bank, ce_cols, ident)
+        ce_rows = sb.tile([P, P, PACK], F32, name="ce_rows")
+        nc.scalar.copy(out=ce_rows[:], in_=ce_bank[:].rearrange("p j n -> p n j"))
+
         nc.vector.memset(ts_pool[0 : P - 1, :], 0.0)
+        windows = [sb.tile([P, TOKENS], F32, name="window0", align_bytes=ALIGN)]
+        nc.vector.memset(windows[0][:], 0.0)
         ts_gathered = sb.tile([P, SLOTS], F32, name="ts_gathered")
         nc.vector.tensor_copy(out=ts_gathered[:], in_=ts_pool[:].indirect(offsets[:]))
 
         q_bf = [sb.tile([P, 2, K], BF16, name="q_bf%d" % h, align_bytes=ALIGN) for h in range(2)]
         for h in range(2):
             nc.vector.tensor_copy(out=q_bf[h][:], in_=q_raw[h][:])
-        q_woven_first = sb.tile([P, HALF, PACK], BF16, name="q_woven0", align_bytes=ALIGN)
-        q_woven = [q_woven_first[:], v_early[:, 0 : 2 * SLOTS].rearrange("p (c t) -> p c t", t=PACK)]
-        q_mx = [operand("q%d" % h, E4M3, HALF, words("q%d" % h, HALF, "q%d_codes" % h)) for h in range(2)]
+        q_woven_second = sb.tile([P, HALF, PACK], BF16, name="q_woven1", align_bytes=ALIGN)
+        q_woven = [early[:, Q_WOVEN_AT : Q_WOVEN_AT + HALF * PACK].rearrange("p (c t) -> p c t", t=PACK), q_woven_second[:]]
         for h in range(2):
             turn(q_woven[h], q_bf[h], h, ident)
+        q_mx = [operand("q0", E4M3, HALF, words("q0", HALF, "q0_codes"))]
         quantise(q_mx[0], q_woven[0], 0)
-        do_woven = sb.tile([P, K, PACK], BF16, name="do_woven", tag="q_woven0", align_bytes=ALIGN)
-        weave(nc.vector.tensor_copy, do_woven[:], do_raw[:])
-        quantise(q_mx[1], q_woven[1], 0)
-        do_mx = operand("do", E5M2, K, words("do", K, "do_codes"))
-        quantise(do_mx, do_woven[:], 0)
-        windows = [sb.tile([P, TOKENS], F32, name="window0", tag="q_woven0", align_bytes=ALIGN)]
-        nc.gpsimd.memset(windows[0][:], 0.0)
-
-        ce_bank = ps.tile([P, PACK, P], F32, name="ce_bank", tag="spread0")
-        spread(ce_bank, ce_cols, ident)
-        ce_rows = sb.tile([P, P, PACK], F32, name="ce_rows")
-        nc.scalar.copy(out=ce_rows[:], in_=ce_bank[:].rearrange("p j n -> p n j"))
         ts_turned = ps.tile([P, PACK, P], F32, name="ts_turned", tag="spread1")
         for j in range(PACK):
             nc.tensor.transpose(ts_turned[:, j, :], ts_gathered[:, P * j : P * (j + 1)], ident[:])
@@ -150,7 +147,17 @@ def tile_attend_glin_kv_kernel(tc, kT, vT, cd, ce, do, qT, ts, offs, out_0, out_
         ts_rows = sb.tile([P, SLOTS], F32, name="ts_rows")
         nc.scalar.copy(out=ts_rows[:], in_=ts_bank[:].rearrange("p j n -> p (j n)"))
 
-        v_bf = sb.tile([P, TOKENS], BF16, name="v_bf", tag="q_bf1", align_bytes=ALIGN)
+        do_woven = [early[:, at : at + HALF * PACK].rearrange("p (c t) -> p c t", t=PACK) for at in (HALF * PACK, 0)]
+        weave(nc.scalar.copy, do_woven[1][:, DO_VECTOR - HALF : HALF, :], do_raw[:, :, DO_VECTOR:K])
+        weave(nc.vector.tensor_copy, do_woven[0], do_raw[:, :, 0:HALF])
+        weave(nc.vector.tensor_copy, do_woven[1][:, 0 : DO_VECTOR - HALF, :], do_raw[:, :, HALF:DO_VECTOR])
+        do_mx = operand("do", E5M2, K, words("do", K, "do_codes"))
+        for h in range(2):
+            quantise(do_mx, do_woven[h], HALF * h)
+        q_mx.append(operand("q1", E4M3, HALF, words("q1", HALF, "do_raw")))
+        quantise(q_mx[1], q_woven[1], 0)
+
+        v_bf = sb.tile([P, TOKENS], BF16, name="v_bf", tag="q_woven1", align_bytes=ALIGN)
         nc.scalar.activation(out=v_bf[:], in_=v_raw[0][:], func=COPY)
         nc.scalar.activation(out=v_first[:, HALF:SLOTS], in_=v_bf[:].indirect(offsets[:, HALF // 16 :]), func=COPY)
         nc.vector.tensor_copy(out=v_first[:, 0:HALF], in_=v_raw[0][:].indirect(offsets[:, 0 : HALF // 16]))

@@ -26,13 +26,13 @@ FLOPS = 3 * 2 * K * K * K
 
 PLANE = 4 * TOKENS
 WINDOW1_AT = 0
-WINDOW2_AT = PLANE
-SD_AT = WINDOW2_AT - 2048
-SE0_AT = WINDOW2_AT - 1024
-K_GATHERED_AT = 2 * PLANE
-V_WOVEN0_AT = K_GATHERED_AT + 5120 - ALIGN
-SE1_SCALES_AT = V_WOVEN0_AT + 256
-SD_SCALES_AT = V_WOVEN0_AT + 512
+K0_AT = PLANE - ALIGN
+WINDOW2_AT = K0_AT + PLANE - ALIGN
+SUMS0_AT = PLANE
+SUMS1_AT = SUMS0_AT + 2048
+SD_SCALES_AT = SUMS1_AT + 2048
+K_GATHERED_AT = 3 * PLANE
+V_WOVEN0_AT = K_GATHERED_AT + 4096 - ALIGN
 IDENT_AT = V_WOVEN0_AT + 2048
 V_WOVEN1_AT = IDENT_AT + 512 - ALIGN
 
@@ -105,7 +105,8 @@ def tile_attend_glin_kv_kernel(tc, kT, vT, cd, ce, do, qT, ts, offs, out_0, out_
         nc.sync.dma_start(out=do_raw[:], in_=do.rearrange("(p t) e -> p t e", t=PACK))
         k_rows = kT.rearrange("(p t) n -> t p n", t=PACK)
         v_rows = vT.rearrange("(p t) n -> t p n", t=PACK)
-        k_raw = [sb.tile([P, TOKENS], F32, name="k_raw%d" % t, align_bytes=ALIGN) for t in range(PACK)]
+        k_raw = [placed.tile([P, TOKENS], F32, name="k_raw0", offset=K0_AT, align_bytes=ALIGN)]
+        k_raw.extend(sb.tile([P, TOKENS], F32, name="k_raw%d" % t, align_bytes=ALIGN) for t in range(1, PACK))
         v_raw = [sb.tile([P, TOKENS], F32, name="v_raw%d" % t, align_bytes=ALIGN) for t in range(PACK)]
         for t in range(PACK):
             nc.sync.dma_start(out=v_raw[t][:], in_=v_rows[t])
@@ -170,13 +171,14 @@ def tile_attend_glin_kv_kernel(tc, kT, vT, cd, ce, do, qT, ts, offs, out_0, out_
                 out=s_planes[:, t, :], in0=s_bank[:], scalar=cd_cols[:, t : t + 1],
                 in1=ce_rows[:].rearrange("p n j -> p (n j)"), op0=MULT, op1=MULT)
 
-        se_woven = [placed.tile([P, HALF, PACK], BF16, name="se_woven0", offset=SE0_AT, align_bytes=ALIGN),
+        se_woven = [sb.tile([P, HALF, PACK], BF16, name="se_woven0", align_bytes=ALIGN),
                     sb.tile([P, HALF, PACK], BF16, name="se_woven1", align_bytes=ALIGN)]
         for h in range(2):
             turn(se_woven[h][:], s_planes[:, 2 * h : 2 * h + 2, :], h, ident)
         nc.vector.tensor_copy(out=v_first[:, SLOTS : 2 * SLOTS], in_=v_raw[1][:].indirect(offsets[:]))
-        se_mx = [operand("se0", E5M2, HALF, words("se0", HALF, "se0_codes"))]
-        quantise(se_mx[0], se_woven[0][:], 0)
+        se_mx = [operand("se%d" % h, E5M2, HALF, words("se%d" % h, HALF, "se%d_codes" % h)) for h in range(2)]
+        for h in range(2):
+            quantise(se_mx[h], se_woven[h][:], 0)
 
         v_tiles = [placed.tile([P, HALF * PACK + ALIGN // 2], BF16, name="v_woven%d" % h, offset=at, align_bytes=ALIGN)
                    for h, at in enumerate((V_WOVEN0_AT, V_WOVEN1_AT))]
@@ -191,22 +193,18 @@ def tile_attend_glin_kv_kernel(tc, kT, vT, cd, ce, do, qT, ts, offs, out_0, out_
         v_mx = operand("v", E4M3, SLOTS, words("v", SLOTS, "v_codes"))
         for h in range(2):
             quantise(v_mx, v_woven[h], HALF * h)
-        sd_woven = placed.tile([P, K, PACK], BF16, name="sd_woven", offset=SD_AT, align_bytes=ALIGN)
-        for h in range(2):
-            weave(nc.scalar.copy, sd_woven[:, HALF * h : HALF * (h + 1), :], s_planes[:, :, HALF * h : HALF * (h + 1)])
-        se_mx.append(operand("se1", E5M2, HALF, words("se1", HALF, "se1_codes"), SE1_SCALES_AT))
-        quantise(se_mx[1], se_woven[1][:], 0)
-        sd_mx = operand("sd", E5M2, K, words("sd", K, "sd_codes"), SD_SCALES_AT)
-        quantise(sd_mx, sd_woven[:, 0:HALF, :], 0)
+        sd_woven = sb.tile([P, K, PACK], BF16, name="sd_woven", tag="se_woven0", align_bytes=ALIGN)
+        weave(nc.scalar.copy, sd_woven[:], s_planes[:])
 
         dk_banks = [ps.tile([P, SLOTS], F32, name="dk_bank%d" % t, tag="sum%d" % t) for t in range(PACK)]
         for t in range(PACK):
             product(dk_banks[t], se_mx[t // 2], t % 2, v_mx)
 
-        k_gathered = placed.tile([P, (PACK + 1) * SLOTS], BF16, name="k_gathered", offset=K_GATHERED_AT, align_bytes=ALIGN)
-        k_planes = k_gathered[:, 0 : PACK * SLOTS].rearrange("p (t s) -> p t s", t=PACK)
+        k_gathered = placed.tile([P, PACK, SLOTS], BF16, name="k_gathered", offset=K_GATHERED_AT, align_bytes=ALIGN)
+        k_planes = k_gathered[:]
         nc.vector.tensor_copy(out=k_planes[:, 0, :], in_=k_raw[0][:].indirect(offsets[:]))
-        quantise(sd_mx, sd_woven[:, HALF:K, :], HALF)
+        sd_mx = operand("sd", E5M2, K, words("sd", K, "sd_codes"), SD_SCALES_AT)
+        quantise(sd_mx, sd_woven[:], 0)
         for w, at in ((1, WINDOW1_AT), (2, WINDOW2_AT)):
             windows.append(placed.tile([P, TOKENS], F32, name="window%d" % w, offset=at, align_bytes=ALIGN))
             nc.gpsimd.memset(windows[w][:], 0.0)
@@ -225,8 +223,9 @@ def tile_attend_glin_kv_kernel(tc, kT, vT, cd, ce, do, qT, ts, offs, out_0, out_
 
         dk_rows = out_0.rearrange("(m t) n -> t m n", t=PACK)
         dv_rows = out_1.rearrange("(j m) n -> j m n", m=P)
-        result_tile(0, dk_banks[0], k_gathered[:, 3 * SLOTS : 5 * SLOTS].bitcast(F32), dk_rows[0])
-        result_tile(1, dk_banks[1], sums_tile(1, "sums1"), dk_rows[1])
+        for t, at in enumerate((SUMS0_AT, SUMS1_AT)):
+            early_sums = placed.tile([P, SLOTS], F32, name="sums%d" % t, offset=at, align_bytes=ALIGN)
+            result_tile(t, dk_banks[t], early_sums[:], dk_rows[t])
 
         k_bf = [sb.tile([P, TOKENS], BF16, name="k_bf1", tag="se0_codes", align_bytes=ALIGN),
                 sb.tile([P, TOKENS], BF16, name="k_bf2", tag="v_codes", align_bytes=ALIGN)]

@@ -26,9 +26,11 @@ FLOPS = 3 * 2 * K * K * K
 
 PLANE = 4 * TOKENS
 WINDOW1_AT = 0
-K0_AT = PLANE - ALIGN
-WINDOW2_AT = K0_AT + PLANE - ALIGN
-SUMS0_AT = PLANE
+WINDOW2_AT = PLANE
+SD_AT = WINDOW2_AT - 2048
+SE0_AT = WINDOW2_AT - 1024
+K0_AT = 2 * PLANE
+SUMS0_AT = K0_AT
 SUMS1_AT = SUMS0_AT + 2048
 SD_SCALES_AT = SUMS1_AT + 2048
 K_GATHERED_AT = 3 * PLANE
@@ -171,7 +173,7 @@ def tile_attend_glin_kv_kernel(tc, kT, vT, cd, ce, do, qT, ts, offs, out_0, out_
                 out=s_planes[:, t, :], in0=s_bank[:], scalar=cd_cols[:, t : t + 1],
                 in1=ce_rows[:].rearrange("p n j -> p (n j)"), op0=MULT, op1=MULT)
 
-        se_woven = [sb.tile([P, HALF, PACK], BF16, name="se_woven0", align_bytes=ALIGN),
+        se_woven = [placed.tile([P, HALF, PACK], BF16, name="se_woven0", offset=SE0_AT, align_bytes=ALIGN),
                     sb.tile([P, HALF, PACK], BF16, name="se_woven1", align_bytes=ALIGN)]
         for h in range(2):
             turn(se_woven[h][:], s_planes[:, 2 * h : 2 * h + 2, :], h, ident)
@@ -193,7 +195,7 @@ def tile_attend_glin_kv_kernel(tc, kT, vT, cd, ce, do, qT, ts, offs, out_0, out_
         v_mx = operand("v", E4M3, SLOTS, words("v", SLOTS, "v_codes"))
         for h in range(2):
             quantise(v_mx, v_woven[h], HALF * h)
-        sd_woven = sb.tile([P, K, PACK], BF16, name="sd_woven", tag="se_woven0", align_bytes=ALIGN)
+        sd_woven = placed.tile([P, K, PACK], BF16, name="sd_woven", offset=SD_AT, align_bytes=ALIGN)
         weave(nc.scalar.copy, sd_woven[:], s_planes[:])
 
         dk_banks = [ps.tile([P, SLOTS], F32, name="dk_bank%d" % t, tag="sum%d" % t) for t in range(PACK)]

@@ -32,7 +32,8 @@ SE0_AT = WINDOW2_AT - 1024
 K0_AT = 2 * PLANE
 SUMS0_AT = K0_AT
 SUMS1_AT = SUMS0_AT + 2048
-SD_SCALES_AT = SUMS1_AT + 2048
+SE1_SCALES_AT = SUMS1_AT + 2048
+SD_SCALES_AT = SE1_SCALES_AT + HALF
 K_GATHERED_AT = 3 * PLANE
 V_WOVEN0_AT = K_GATHERED_AT + 4096 - ALIGN
 IDENT_AT = V_WOVEN0_AT + 2048
@@ -178,9 +179,8 @@ def tile_attend_glin_kv_kernel(tc, kT, vT, cd, ce, do, qT, ts, offs, out_0, out_
         for h in range(2):
             turn(se_woven[h][:], s_planes[:, 2 * h : 2 * h + 2, :], h, ident)
         nc.vector.tensor_copy(out=v_first[:, SLOTS : 2 * SLOTS], in_=v_raw[1][:].indirect(offsets[:]))
-        se_mx = [operand("se%d" % h, E5M2, HALF, words("se%d" % h, HALF, "se%d_codes" % h)) for h in range(2)]
-        for h in range(2):
-            quantise(se_mx[h], se_woven[h][:], 0)
+        se_mx = [operand("se0", E5M2, HALF, words("se0", HALF, "se0_codes"))]
+        quantise(se_mx[0], se_woven[0][:], 0)
 
         v_tiles = [placed.tile([P, HALF * PACK + ALIGN // 2], BF16, name="v_woven%d" % h, offset=at, align_bytes=ALIGN)
                    for h, at in enumerate((V_WOVEN0_AT, V_WOVEN1_AT))]
@@ -199,12 +199,16 @@ def tile_attend_glin_kv_kernel(tc, kT, vT, cd, ce, do, qT, ts, offs, out_0, out_
         weave(nc.scalar.copy, sd_woven[:], s_planes[:])
 
         dk_banks = [ps.tile([P, SLOTS], F32, name="dk_bank%d" % t, tag="sum%d" % t) for t in range(PACK)]
-        for t in range(PACK):
-            product(dk_banks[t], se_mx[t // 2], t % 2, v_mx)
+        for t in range(2):
+            product(dk_banks[t], se_mx[0], t, v_mx)
 
         k_gathered = placed.tile([P, PACK, SLOTS], BF16, name="k_gathered", offset=K_GATHERED_AT, align_bytes=ALIGN)
         k_planes = k_gathered[:]
         nc.vector.tensor_copy(out=k_planes[:, 0, :], in_=k_raw[0][:].indirect(offsets[:]))
+        se_mx.append(operand("se1", E5M2, HALF, words("se1", HALF, "se1_codes"), SE1_SCALES_AT))
+        quantise(se_mx[1], se_woven[1][:], 0)
+        for t in range(2):
+            product(dk_banks[2 + t], se_mx[1], t, v_mx)
         sd_mx = operand("sd", E5M2, K, words("sd", K, "sd_codes"), SD_SCALES_AT)
         quantise(sd_mx, sd_woven[:], 0)
         for w, at in ((1, WINDOW1_AT), (2, WINDOW2_AT)):
@@ -236,11 +240,14 @@ def tile_attend_glin_kv_kernel(tc, kT, vT, cd, ce, do, qT, ts, offs, out_0, out_
         nc.scalar.activation(out=k_planes[:, 1, :], in_=k_bf[0][:].indirect(offsets[:]), func=COPY)
         third_sums = sums_tile(2, "k_raw2")
         nc.scalar.copy(out=third_sums, in_=dk_banks[2][:])
-        nc.scalar.activation(out=k_planes[:, 2, :], in_=k_bf[1][:].indirect(offsets[:]), func=COPY)
+        for h in range(2):
+            nc.scalar.activation(out=k_planes[:, 2, HALF * h : HALF * (h + 1)],
+                                 in_=k_bf[1][:].indirect(offsets[:, HALF // 16 * h : HALF // 16 * (h + 1)]), func=COPY)
         nc.vector.tensor_copy(out=k_planes[:, 3, :], in_=k_raw[3][:].indirect(offsets[:]))
         scatter(2, third_sums, dk_rows[2])
         k_woven = sb.tile([P, SLOTS, PACK], BF16, name="k_woven", align_bytes=ALIGN)
-        weave(nc.scalar.copy, k_woven[:], k_planes)
+        for h in range(2):
+            weave(nc.scalar.copy, k_woven[:, HALF * h : HALF * (h + 1), :], k_planes[:, :, HALF * h : HALF * (h + 1)])
         k_mx = operand("k", E4M3, SLOTS, words("k", SLOTS, "k_codes"))
         quantise(k_mx, k_woven[:], 0)
         fourth_sums = placed.tile([P, SLOTS], F32, name="sums3", offset=K_GATHERED_AT, align_bytes=ALIGN)

@@ -19,25 +19,19 @@ TOKENS = 2048
 SLOTS = 512
 HALF = 256
 DO_VECTOR = 336
-Q_WOVEN_AT = 288
-WINDOWS = 3
 ALIGN = 64
 FLOPS = 3 * 2 * K * K * K
 
 PLANE = 4 * TOKENS
+TILE = 4 * SLOTS
 WINDOW1_AT = 0
 WINDOW2_AT = PLANE
-SD_AT = WINDOW2_AT - 2048
-SE0_AT = WINDOW2_AT - 1024
-K0_AT = 2 * PLANE
-SUMS0_AT = K0_AT
-SUMS1_AT = SUMS0_AT + 2048
-SE1_SCALES_AT = SUMS1_AT + 2048
-SD_SCALES_AT = SE1_SCALES_AT + HALF
-K_GATHERED_AT = 3 * PLANE
-V_WOVEN0_AT = K_GATHERED_AT + 4096 - ALIGN
-IDENT_AT = V_WOVEN0_AT + 2048
-V_WOVEN1_AT = IDENT_AT + 512 - ALIGN
+V_WOVEN_AT = WINDOW2_AT - 2048
+WINDOW3_AT = 2 * PLANE
+DO_WOVEN_AT = WINDOW3_AT
+SUMS6_AT = 3 * PLANE
+SUMS7_AT = SUMS6_AT + TILE
+SUMS4_AT = SUMS7_AT - TILE // 2
 
 
 def tile_attend_glin_kv_kernel(tc, kT, vT, cd, ce, do, qT, ts, offs, out_0, out_1):
@@ -47,18 +41,16 @@ def tile_attend_glin_kv_kernel(tc, kT, vT, cd, ce, do, qT, ts, offs, out_0, out_
         placed = ctx.enter_context(tc.tile_pool(name="placed", bufs=1))
         ps = ctx.enter_context(tc.psum_pool(name="ps", bufs=1))
 
+        def tile(name, shape, dtype, at=None):
+            if at is None:
+                return sb.tile(shape, dtype, name=name, align_bytes=ALIGN)
+            return placed.tile(shape, dtype, name=name, offset=at, align_bytes=ALIGN)
+
         def weave(engine_copy, woven, planes):
             engine_copy(out=woven.rearrange("p (c i) t -> p c t i", i=4), in_=planes.rearrange("p t (c i) -> p c t i", i=4))
 
-        def operand(name, fmt, width, codes, scales_at=None):
-            if scales_at is None:
-                scales = sb.tile([P, width], U8, name=name + "_scales", align_bytes=ALIGN)
-            else:
-                scales = placed.tile([P, width], U8, name=name + "_scales", offset=scales_at, align_bytes=ALIGN)
-            return codes, scales, fmt
-
-        def words(name, width, tag):
-            return sb.tile([P, width], U32, name=name + "_codes", align_bytes=ALIGN, tag=tag)
+        def operand(name, fmt):
+            return tile(name + "_codes", [P, K], U32), tile(name + "_scales", [P, K], U8), fmt
 
         def quantise(mx, woven, first):
             codes, scales, fmt = mx
@@ -77,183 +69,168 @@ def tile_attend_glin_kv_kernel(tc, kT, vT, cd, ce, do, qT, ts, offs, out_0, out_
                 stop=True,
             )
 
-        def turn(woven, rows, half, ident):
+        def turn(woven, rows, tag):
             woven_words = woven.rearrange("p c t -> p (c t)").bitcast(F32).rearrange("p (a m u) -> p a m u", a=2, u=2)
-            bank = ps.tile([P, 2, 2, P], F32, name="turn_bank", tag="turn%d" % half)
+            bank = ps.tile([P, 2, 2, P], F32, name="turn_bank", tag=tag)
             for a in range(2):
                 row_words = rows[:, a, :].bitcast(F32)
                 for u in range(2):
                     nc.tensor.transpose(bank[:, a, u, :], row_words[:, u : K // 2 : 2], ident[:])
             nc.scalar.copy(out=woven_words, in_=bank[:].rearrange("p a u m -> p a m u"))
 
-        def spread(bank, columns, ident):
+        def spread(bank, columns):
             for j in range(PACK):
                 nc.tensor.transpose(bank[:, j, :], columns[:, j : j + 1].to_broadcast([P, P]), ident[:])
 
+        def part(first, last):
+            return offsets[:, first // 16 : last // 16]
+
+        def gather_vector(planes, raw, t, first, last):
+            nc.vector.tensor_copy(out=planes[:, t, first:last], in_=raw[t][:].indirect(part(first, last)))
+
+        def gather_scalar(planes, raw, t, first, last):
+            nc.scalar.activation(out=planes[:, t, first:last], in_=raw[t][:].indirect(part(first, last)), func=COPY)
+
         offsets = sb.tile([P, SLOTS // 16], U16, name="offsets")
-        q_raw = [sb.tile([P, 2, K], F32, name="q_raw%d" % h, align_bytes=ALIGN) for h in range(2)]
-        do_raw = sb.tile([P, PACK, K], F32, name="do_raw", align_bytes=ALIGN)
-        early = sb.tile([P, 6 * SLOTS + 8], BF16, name="early", align_bytes=ALIGN)
-        v_first = early[:, 4 * SLOTS - 32 : 6 * SLOTS - 32]
-        cd_cols = early[:, 6 * SLOTS - 34 : 6 * SLOTS - 26].bitcast(F32)
-        ce_cols = sb.tile([P, PACK], F32, name="ce_cols", align_bytes=ALIGN)
-        ts_pool = sb.tile([P, TOKENS], F32, name="ts_pool", align_bytes=ALIGN)
+        q_raw = [tile("q_raw%d" % h, [P, 2, K], F32) for h in range(2)]
+        do_raw = tile("do_raw", [P, PACK, K], F32)
+        cd_cols = tile("cd_cols", [P, PACK], F32)
+        ce_cols = tile("ce_cols", [P, PACK], F32)
+        ts_pool = tile("ts_pool", [P, TOKENS], F32)
+        v_raw = [tile("v_raw%d" % t, [P, TOKENS], F32) for t in range(PACK)]
+        k_raw = [tile("k_raw%d" % t, [P, TOKENS], F32) for t in range(PACK)]
         q_rows = qT.rearrange("(m t) r -> m t r", t=PACK)
         nc.sync.dma_start(out=q_raw[0][:], in_=q_rows[:, 0:2, :])
         nc.sync.dma_start(offsets[:], offs)
         nc.sync.dma_start(out=ts_pool[P - 1 : P, :], in_=ts[0:1, :])
         nc.sync.dma_start(out=q_raw[1][:], in_=q_rows[:, 2:4, :])
         nc.scalar.dma_start(out=ce_cols[:], in_=ce[0:1, :].rearrange("o (p j) -> (o p) j", j=PACK))
-        nc.scalar.dma_start(out=cd_cols, in_=cd.rearrange("(p t) o -> p (t o)", t=PACK))
+        nc.scalar.dma_start(out=cd_cols[:], in_=cd.rearrange("(p t) o -> p (t o)", t=PACK))
         nc.sync.dma_start(out=do_raw[:], in_=do.rearrange("(p t) e -> p t e", t=PACK))
-        k_rows = kT.rearrange("(p t) n -> t p n", t=PACK)
-        v_rows = vT.rearrange("(p t) n -> t p n", t=PACK)
-        k_raw = [placed.tile([P, TOKENS], F32, name="k_raw0", offset=K0_AT, align_bytes=ALIGN)]
-        k_raw.extend(sb.tile([P, TOKENS], F32, name="k_raw%d" % t, align_bytes=ALIGN) for t in range(1, PACK))
-        v_raw = [sb.tile([P, TOKENS], F32, name="v_raw%d" % t, align_bytes=ALIGN) for t in range(PACK)]
-        for t in range(PACK):
-            nc.sync.dma_start(out=v_raw[t][:], in_=v_rows[t])
-        for t in range(PACK):
-            nc.sync.dma_start(out=k_raw[t][:], in_=k_rows[t])
+        for raw, table in ((v_raw, vT), (k_raw, kT)):
+            rows = table.rearrange("(p t) n -> t p n", t=PACK)
+            for t in range(PACK):
+                nc.sync.dma_start(out=raw[t][:], in_=rows[t])
 
-        ident = placed.tile([P, P], F32, name="ident", offset=IDENT_AT, align_bytes=ALIGN)
+        ident = tile("ident", [P, P], F32)
         nc.gpsimd.memset(ident[:], 0.0)
         nc.gpsimd.affine_select(out=ident[:], in_=ident[:], compare_op=mybir.AluOpType.not_equal, fill=1.0, base=0,
                                 pattern=[[-1, P]], channel_multiplier=1)
 
-        ce_bank = ps.tile([P, PACK, P], F32, name="ce_bank", tag="spread0")
-        spread(ce_bank, ce_cols, ident)
-        ce_rows = sb.tile([P, P, PACK], F32, name="ce_rows")
+        nc.vector.memset(ts_pool[0 : P - 1, :], 0.0)
+        window0 = tile("window0", [P, TOKENS], F32)
+        nc.vector.memset(window0[:], 0.0)
+
+        ce_bank = ps.tile([P, PACK, P], F32, name="ce_bank", tag="b2")
+        spread(ce_bank, ce_cols)
+        ce_rows = tile("ce_rows", [P, P, PACK], F32)
         nc.scalar.copy(out=ce_rows[:], in_=ce_bank[:].rearrange("p j n -> p n j"))
 
-        nc.vector.memset(ts_pool[0 : P - 1, :], 0.0)
-        windows = [sb.tile([P, TOKENS], F32, name="window0", align_bytes=ALIGN)]
-        nc.vector.memset(windows[0][:], 0.0)
-        ts_gathered = sb.tile([P, SLOTS], F32, name="ts_gathered")
-        nc.vector.tensor_copy(out=ts_gathered[:], in_=ts_pool[:].indirect(offsets[:]))
-
-        q_bf = [sb.tile([P, 2, K], BF16, name="q_bf%d" % h, align_bytes=ALIGN) for h in range(2)]
+        q_bf = [tile("q_bf%d" % h, [P, 2, K], BF16) for h in range(2)]
+        q_woven = [tile("q_woven%d" % h, [P, HALF, PACK], BF16) for h in range(2)]
+        q_mx = operand("q", E4M3)
         for h in range(2):
             nc.vector.tensor_copy(out=q_bf[h][:], in_=q_raw[h][:])
-        q_woven_second = sb.tile([P, HALF, PACK], BF16, name="q_woven1", align_bytes=ALIGN)
-        q_woven = [early[:, Q_WOVEN_AT : Q_WOVEN_AT + HALF * PACK].rearrange("p (c t) -> p c t", t=PACK), q_woven_second[:]]
+            turn(q_woven[h][:], q_bf[h], "b%d" % h)
+        ts_gathered = tile("ts_gathered", [P, SLOTS], F32)
+        nc.vector.tensor_copy(out=ts_gathered[:], in_=ts_pool[:].indirect(offsets[:]))
         for h in range(2):
-            turn(q_woven[h], q_bf[h], h, ident)
-        q_mx = [operand("q0", E4M3, HALF, words("q0", HALF, "q0_codes"))]
-        quantise(q_mx[0], q_woven[0], 0)
-        ts_turned = ps.tile([P, PACK, P], F32, name="ts_turned", tag="spread1")
+            quantise(q_mx, q_woven[h][:], HALF * h)
+
+        do_woven = tile("do_woven", [P, K, PACK], BF16, DO_WOVEN_AT)
+        weave(nc.scalar.copy, do_woven[:, DO_VECTOR:K, :], do_raw[:, :, DO_VECTOR:K])
+        weave(nc.vector.tensor_copy, do_woven[:, 0:HALF, :], do_raw[:, :, 0:HALF])
+        weave(nc.vector.tensor_copy, do_woven[:, HALF:DO_VECTOR, :], do_raw[:, :, HALF:DO_VECTOR])
+        do_mx = operand("do", E5M2)
+        for h in range(2):
+            quantise(do_mx, do_woven[:, HALF * h : HALF * (h + 1), :], HALF * h)
+        window3 = tile("window3", [P, TOKENS], F32, WINDOW3_AT)
+        nc.gpsimd.memset(window3[:], 0.0)
+
+        ts_turned = ps.tile([P, PACK, P], F32, name="ts_turned", tag="b3")
         for j in range(PACK):
             nc.tensor.transpose(ts_turned[:, j, :], ts_gathered[:, P * j : P * (j + 1)], ident[:])
-        ts_cols = sb.tile([P, PACK], F32, name="ts_cols")
+        ts_cols = tile("ts_cols", [P, PACK], F32)
         nc.scalar.copy(out=ts_cols[:], in_=ts_turned[:, :, P - 1])
-        ts_bank = ps.tile([P, PACK, P], F32, name="ts_bank", tag="spread1")
-        spread(ts_bank, ts_cols, ident)
-        ts_rows = sb.tile([P, SLOTS], F32, name="ts_rows")
+        ts_bank = ps.tile([P, PACK, P], F32, name="ts_bank", tag="b3")
+        spread(ts_bank, ts_cols)
+        ts_rows = tile("ts_rows", [P, SLOTS], F32)
         nc.scalar.copy(out=ts_rows[:], in_=ts_bank[:].rearrange("p j n -> p (j n)"))
 
-        do_woven = [early[:, at : at + HALF * PACK].rearrange("p (c t) -> p c t", t=PACK) for at in (HALF * PACK, 0)]
-        weave(nc.scalar.copy, do_woven[1][:, DO_VECTOR - HALF : HALF, :], do_raw[:, :, DO_VECTOR:K])
-        weave(nc.vector.tensor_copy, do_woven[0], do_raw[:, :, 0:HALF])
-        weave(nc.vector.tensor_copy, do_woven[1][:, 0 : DO_VECTOR - HALF, :], do_raw[:, :, HALF:DO_VECTOR])
-        do_mx = operand("do", E5M2, K, words("do", K, "do_codes"))
-        for h in range(2):
-            quantise(do_mx, do_woven[h], HALF * h)
-        q_mx.append(operand("q1", E4M3, HALF, words("q1", HALF, "do_raw")))
-        quantise(q_mx[1], q_woven[1], 0)
-
-        v_bf = sb.tile([P, TOKENS], BF16, name="v_bf", tag="q_woven1", align_bytes=ALIGN)
-        nc.scalar.activation(out=v_bf[:], in_=v_raw[0][:], func=COPY)
-        nc.scalar.activation(out=v_first[:, HALF:SLOTS], in_=v_bf[:].indirect(offsets[:, HALF // 16 :]), func=COPY)
-        nc.vector.tensor_copy(out=v_first[:, 0:HALF], in_=v_raw[0][:].indirect(offsets[:, 0 : HALF // 16]))
-
-        s_planes = sb.tile([P, PACK, K], BF16, name="s_planes")
+        s_planes = tile("s_planes", [P, PACK, K], BF16)
         for t in range(PACK):
-            s_bank = ps.tile([P, K], F32, name="s_bank", tag="sum%d" % t)
-            product(s_bank, q_mx[t // 2], t % 2, do_mx)
+            s_bank = ps.tile([P, K], F32, name="s_bank", tag="b%d" % (4 + t))
+            product(s_bank, q_mx, t, do_mx)
             nc.vector.scalar_tensor_tensor(
                 out=s_planes[:, t, :], in0=s_bank[:], scalar=cd_cols[:, t : t + 1],
                 in1=ce_rows[:].rearrange("p n j -> p (n j)"), op0=MULT, op1=MULT)
-
-        se_woven = [placed.tile([P, HALF, PACK], BF16, name="se_woven0", offset=SE0_AT, align_bytes=ALIGN),
-                    sb.tile([P, HALF, PACK], BF16, name="se_woven1", align_bytes=ALIGN)]
+        se_woven = [tile("se_woven%d" % h, [P, HALF, PACK], BF16) for h in range(2)]
+        se_mx = operand("se", E5M2)
         for h in range(2):
-            turn(se_woven[h][:], s_planes[:, 2 * h : 2 * h + 2, :], h, ident)
-        nc.vector.tensor_copy(out=v_first[:, SLOTS : 2 * SLOTS], in_=v_raw[1][:].indirect(offsets[:]))
-        se_mx = [operand("se0", E5M2, HALF, words("se0", HALF, "se0_codes"))]
-        quantise(se_mx[0], se_woven[0][:], 0)
-
-        v_tiles = [placed.tile([P, HALF * PACK + ALIGN // 2], BF16, name="v_woven%d" % h, offset=at, align_bytes=ALIGN)
-                   for h, at in enumerate((V_WOVEN0_AT, V_WOVEN1_AT))]
-        v_woven = [v_tiles[h][:, ALIGN // 2 * h : ALIGN // 2 * h + HALF * PACK].rearrange("p (c t) -> p c t", t=PACK) for h in range(2)]
-        for h in range(2):
-            nc.scalar.copy(out=v_woven[h][:, :, 0:2],
-                           in_=v_first.rearrange("p (j s) -> p s j", j=2)[:, HALF * h : HALF * (h + 1), :])
-        for t in (2, 3):
-            for h in range(2):
-                nc.vector.tensor_copy(out=v_woven[h][:, :, t],
-                                      in_=v_raw[t][:].indirect(offsets[:, HALF // 16 * h : HALF // 16 * (h + 1)]))
-        v_mx = operand("v", E4M3, SLOTS, words("v", SLOTS, "v_codes"))
-        for h in range(2):
-            quantise(v_mx, v_woven[h], HALF * h)
-        sd_woven = placed.tile([P, K, PACK], BF16, name="sd_woven", offset=SD_AT, align_bytes=ALIGN)
-        weave(nc.scalar.copy, sd_woven[:], s_planes[:])
-
-        dk_banks = [ps.tile([P, SLOTS], F32, name="dk_bank%d" % t, tag="sum%d" % t) for t in range(PACK)]
-        for t in range(2):
-            product(dk_banks[t], se_mx[0], t, v_mx)
-
-        k_gathered = placed.tile([P, PACK, SLOTS], BF16, name="k_gathered", offset=K_GATHERED_AT, align_bytes=ALIGN)
-        k_planes = k_gathered[:]
-        nc.vector.tensor_copy(out=k_planes[:, 0, :], in_=k_raw[0][:].indirect(offsets[:]))
-        se_mx.append(operand("se1", E5M2, HALF, words("se1", HALF, "se1_codes"), SE1_SCALES_AT))
-        quantise(se_mx[1], se_woven[1][:], 0)
-        for t in range(2):
-            product(dk_banks[2 + t], se_mx[1], t, v_mx)
-        sd_mx = operand("sd", E5M2, K, words("sd", K, "sd_codes"), SD_SCALES_AT)
+            turn(se_woven[h][:], s_planes[:, 2 * h : 2 * h + 2, :], "b%d" % h)
+            quantise(se_mx, se_woven[h][:], HALF * h)
+        sd_woven = tile("sd_woven", [P, K, PACK], BF16)
+        weave(nc.vector.tensor_copy, sd_woven[:], s_planes[:])
+        sd_mx = operand("sd", E5M2)
         quantise(sd_mx, sd_woven[:], 0)
-        for w, at in ((1, WINDOW1_AT), (2, WINDOW2_AT)):
-            windows.append(placed.tile([P, TOKENS], F32, name="window%d" % w, offset=at, align_bytes=ALIGN))
+
+        v_planes = tile("v_planes", [P, PACK, SLOTS], BF16)
+        for t in range(PACK - 1):
+            gather_scalar(v_planes, v_raw, t, 0, SLOTS)
+        v_woven = tile("v_woven", [P, SLOTS, PACK], BF16, V_WOVEN_AT)
+        v_mx = operand("v", E4M3)
+        gather_vector(v_planes, v_raw, PACK - 1, 0, HALF)
+        gather_scalar(v_planes, v_raw, PACK - 1, HALF, SLOTS)
+        weave(nc.vector.tensor_copy, v_woven[:, 0:HALF, :], v_planes[:, :, 0:HALF])
+        weave(nc.scalar.copy, v_woven[:, HALF:SLOTS, :], v_planes[:, :, HALF:SLOTS])
+        for h in range(2):
+            quantise(v_mx, v_woven[:, HALF * h : HALF * (h + 1), :], HALF * h)
+        windows = [window0, tile("window1", [P, TOKENS], F32, WINDOW1_AT), tile("window2", [P, TOKENS], F32, WINDOW2_AT), window3]
+        for w in (1, 2):
             nc.gpsimd.memset(windows[w][:], 0.0)
 
-        def sums_tile(n, tag):
-            return sb.tile([P, SLOTS], F32, name="sums%d" % n, tag=tag, align_bytes=ALIGN)[:]
+        def scaled(n, stationary, moving, tag, at=None):
+            bank = ps.tile([P, SLOTS], F32, name="result_bank", tag=tag)
+            product(bank, stationary, n % PACK, moving)
+            sums = tile("sums%d" % n, [P, SLOTS], F32, at)
+            nc.vector.tensor_tensor(out=sums[:], in0=bank[:], in1=ts_rows[:], op=MULT)
+            return sums
 
-        def scatter(n, sums, rows):
-            window = windows[n % WINDOWS]
-            nc.vector.tensor_tensor(out=window[:].indirect(offsets[:]), in0=sums, in1=ts_rows[:], op=MULT)
-            nc.sync.dma_start(out=rows, in_=window[:])
+        def scatter_scalar(n, sums, first, last):
+            nc.scalar.activation(out=windows[n % PACK][:].indirect(part(first, last)), in_=sums[:, first:last], func=COPY)
 
-        def result_tile(n, bank, sums, rows):
-            nc.scalar.copy(out=sums, in_=bank[:])
-            scatter(n, sums, rows)
+        def scatter_vector(n, sums, first, last):
+            nc.vector.tensor_copy(out=windows[n % PACK][:].indirect(part(first, last)), in_=sums[:, first:last])
 
         dk_rows = out_0.rearrange("(m t) n -> t m n", t=PACK)
         dv_rows = out_1.rearrange("(j m) n -> j m n", m=P)
-        for t, at in enumerate((SUMS0_AT, SUMS1_AT)):
-            early_sums = placed.tile([P, SLOTS], F32, name="sums%d" % t, offset=at, align_bytes=ALIGN)
-            result_tile(t, dk_banks[t], early_sums[:], dk_rows[t])
 
-        k_bf = [sb.tile([P, TOKENS], BF16, name="k_bf1", tag="se0_codes", align_bytes=ALIGN),
-                sb.tile([P, TOKENS], BF16, name="k_bf2", tag="v_codes", align_bytes=ALIGN)]
-        for i in range(2):
-            nc.scalar.activation(out=k_bf[i][:], in_=k_raw[i + 1][:], func=COPY)
-        nc.scalar.activation(out=k_planes[:, 1, :], in_=k_bf[0][:].indirect(offsets[:]), func=COPY)
-        third_sums = sums_tile(2, "k_raw2")
-        nc.scalar.copy(out=third_sums, in_=dk_banks[2][:])
-        for h in range(2):
-            nc.scalar.activation(out=k_planes[:, 2, HALF * h : HALF * (h + 1)],
-                                 in_=k_bf[1][:].indirect(offsets[:, HALF // 16 * h : HALF // 16 * (h + 1)]), func=COPY)
-        nc.vector.tensor_copy(out=k_planes[:, 3, :], in_=k_raw[3][:].indirect(offsets[:]))
-        scatter(2, third_sums, dk_rows[2])
-        k_woven = sb.tile([P, SLOTS, PACK], BF16, name="k_woven", align_bytes=ALIGN)
-        for h in range(2):
-            weave(nc.scalar.copy, k_woven[:, HALF * h : HALF * (h + 1), :], k_planes[:, :, HALF * h : HALF * (h + 1)])
-        k_mx = operand("k", E4M3, SLOTS, words("k", SLOTS, "k_codes"))
+        def store(n):
+            rows = dk_rows[n] if n < PACK else dv_rows[n - PACK]
+            nc.sync.dma_start(out=rows, in_=windows[n % PACK][:])
+
+        k_planes = tile("k_planes", [P, PACK, SLOTS], BF16)
+        gather_scalar(k_planes, k_raw, 0, 0, SLOTS)
+        dk = [scaled(n, se_mx, v_mx, "b%d" % (4 + n)) for n in range(PACK)]
+        scatter_vector(3, dk[3], HALF, SLOTS)
+        for n in range(PACK - 1):
+            for h in range(2):
+                scatter_scalar(n, dk[n], HALF * h, HALF * (h + 1))
+            store(n)
+        scatter_scalar(3, dk[3], 0, HALF)
+        store(3)
+
+        for t in range(1, PACK):
+            gather_vector(k_planes, k_raw, t, 0, SLOTS)
+        k_woven = tile("k_woven", [P, SLOTS, PACK], BF16)
+        weave(nc.vector.tensor_copy, k_woven[:], k_planes[:])
+        k_mx = operand("k", E4M3)
         quantise(k_mx, k_woven[:], 0)
-        fourth_sums = placed.tile([P, SLOTS], F32, name="sums3", offset=K_GATHERED_AT, align_bytes=ALIGN)
-        result_tile(3, dk_banks[3], fourth_sums[:], dk_rows[3])
 
-        for j in range(PACK):
-            dv_bank = ps.tile([P, SLOTS], F32, name="dv_bank", tag="sum%d" % j)
-            product(dv_bank, sd_mx, j, k_mx)
-            result_tile(PACK + j, dv_bank, sums_tile(PACK + j, "sums%d" % (PACK + j)), dv_rows[j])
+        for pair, places in ((4, (SUMS4_AT, None)), (6, (SUMS6_AT, SUMS7_AT))):
+            dv = [scaled(pair + i, sd_mx, k_mx, "b%d" % (pair + i - PACK), places[i]) for i in range(2)]
+            scatter_vector(pair, dv[0], 0, SLOTS)
+            store(pair)
+            for h in range(2):
+                scatter_scalar(pair + 1, dv[1], HALF * h, HALF * (h + 1))
+            store(pair + 1)

@@ -24,14 +24,16 @@ FLOPS = 3 * 2 * K * K * K
 
 PLANE = 4 * TOKENS
 TILE = 4 * SLOTS
-WINDOW1_AT = 0
-WINDOW2_AT = PLANE
-V_WOVEN_AT = WINDOW2_AT - 2048
-WINDOW3_AT = 2 * PLANE
-DO_WOVEN_AT = WINDOW3_AT
-SUMS6_AT = 3 * PLANE
-SUMS7_AT = SUMS6_AT + TILE
-SUMS4_AT = SUMS7_AT - TILE // 2
+V_VECTOR = 320
+TAIL = 256
+WINDOW2_AT = 0
+WINDOW3_AT = PLANE
+V_WOVEN_AT = WINDOW3_AT - ALIGN
+WINDOW4_AT = 2 * PLANE
+WINDOW1_AT = 3 * PLANE
+DO_WOVEN_AT = WINDOW1_AT
+SUMS4_AT = 4 * PLANE
+SUMS6_AT = SUMS4_AT + TILE
 
 
 def tile_attend_glin_kv_kernel(tc, kT, vT, cd, ce, do, qT, ts, offs, out_0, out_1):
@@ -49,22 +51,22 @@ def tile_attend_glin_kv_kernel(tc, kT, vT, cd, ce, do, qT, ts, offs, out_0, out_
         def weave(engine_copy, woven, planes):
             engine_copy(out=woven.rearrange("p (c i) t -> p c t i", i=4), in_=planes.rearrange("p t (c i) -> p c t i", i=4))
 
-        def operand(name, fmt):
-            return tile(name + "_codes", [P, K], U32), tile(name + "_scales", [P, K], U8), fmt
+        def operand(name, fmt, at=None):
+            return tile(name + "_codes", [P, K], U32, at), tile(name + "_scales", [P, K], U8), fmt
 
         def quantise(mx, woven, first):
             codes, scales, fmt = mx
             cols = slice(first, first + woven.shape[1])
             nc.vector.quantize_mx(out=codes[:, cols].bitcast(fmt), scales=scales[:, cols], in_=woven.rearrange("p c t -> p (c t)"))
 
-        def product(bank, stationary, j, moving):
+        def product(bank, stationary, j, moving, first=0, last=K):
             cols = slice(P * j, P * (j + 1))
             nc.tensor.matmul_mx(
-                out=bank[:],
+                out=bank[:, first:last],
                 lhsT=stationary[0][:, cols].bitcast(stationary[2]),
                 lhsT_scale=stationary[1][:, cols],
-                rhs=moving[0][:].bitcast(moving[2]),
-                rhs_scale=moving[1][:],
+                rhs=moving[0][:, first:last].bitcast(moving[2]),
+                rhs_scale=moving[1][:, first:last],
                 start=True,
                 stop=True,
             )
@@ -119,7 +121,7 @@ def tile_attend_glin_kv_kernel(tc, kT, vT, cd, ce, do, qT, ts, offs, out_0, out_
 
         nc.vector.memset(ts_pool[0 : P - 1, :], 0.0)
         window0 = tile("window0", [P, TOKENS], F32)
-        nc.vector.memset(window0[:], 0.0)
+        nc.gpsimd.memset(window0[:], 0.0)
 
         ce_bank = ps.tile([P, PACK, P], F32, name="ce_bank", tag="b2")
         spread(ce_bank, ce_cols)
@@ -144,8 +146,8 @@ def tile_attend_glin_kv_kernel(tc, kT, vT, cd, ce, do, qT, ts, offs, out_0, out_
         do_mx = operand("do", E5M2)
         for h in range(2):
             quantise(do_mx, do_woven[:, HALF * h : HALF * (h + 1), :], HALF * h)
-        window3 = tile("window3", [P, TOKENS], F32, WINDOW3_AT)
-        nc.gpsimd.memset(window3[:], 0.0)
+        window1 = tile("window1", [P, TOKENS], F32, WINDOW1_AT)
+        nc.gpsimd.memset(window1[:], 0.0)
 
         ts_turned = ps.tile([P, PACK, P], F32, name="ts_turned", tag="b3")
         for j in range(PACK):
@@ -177,60 +179,91 @@ def tile_attend_glin_kv_kernel(tc, kT, vT, cd, ce, do, qT, ts, offs, out_0, out_
         v_planes = tile("v_planes", [P, PACK, SLOTS], BF16)
         for t in range(PACK - 1):
             gather_scalar(v_planes, v_raw, t, 0, SLOTS)
-        v_woven = tile("v_woven", [P, SLOTS, PACK], BF16, V_WOVEN_AT)
+        v_span = tile("v_woven", [P, PLANE // 2 + ALIGN], BF16, V_WOVEN_AT)
+        v_woven = v_span[:, 0 : SLOTS * PACK].rearrange("p (c t) -> p c t", t=PACK)
         v_mx = operand("v", E4M3)
-        gather_vector(v_planes, v_raw, PACK - 1, 0, HALF)
-        gather_scalar(v_planes, v_raw, PACK - 1, HALF, SLOTS)
+        gather_scalar(v_planes, v_raw, PACK - 1, 0, HALF)
+        gather_vector(v_planes, v_raw, PACK - 1, HALF, SLOTS)
         weave(nc.vector.tensor_copy, v_woven[:, 0:HALF, :], v_planes[:, :, 0:HALF])
-        weave(nc.scalar.copy, v_woven[:, HALF:SLOTS, :], v_planes[:, :, HALF:SLOTS])
+        weave(nc.vector.tensor_copy, v_woven[:, HALF:V_VECTOR, :], v_planes[:, :, HALF:V_VECTOR])
+        weave(nc.scalar.copy, v_woven[:, V_VECTOR:SLOTS, :], v_planes[:, :, V_VECTOR:SLOTS])
         for h in range(2):
             quantise(v_mx, v_woven[:, HALF * h : HALF * (h + 1), :], HALF * h)
-        windows = [window0, tile("window1", [P, TOKENS], F32, WINDOW1_AT), tile("window2", [P, TOKENS], F32, WINDOW2_AT), window3]
-        for w in (1, 2):
-            nc.gpsimd.memset(windows[w][:], 0.0)
+        windows = [window0, window1, tile("window2", [P, TOKENS], F32, WINDOW2_AT), tile("window3", [P, TOKENS], F32, WINDOW3_AT),
+                   tile("window4", [P, TOKENS], F32, WINDOW4_AT)]
+        nc.gpsimd.memset(windows[4][:, 0 : TOKENS // 4], 0.0)
+        for cols in (slice(0, TOKENS - TAIL), slice(TOKENS - TAIL, TOKENS)):
+            for w in (2, 3):
+                nc.gpsimd.memset(windows[w][:, cols], 0.0)
+        nc.gpsimd.memset(windows[4][:, TOKENS // 4 : TOKENS], 0.0)
+        window_of = [windows[w] for w in (0, 1, 2, 3, 0, 4, 2, 1)]
 
-        def scaled(n, stationary, moving, tag, at=None):
-            bank = ps.tile([P, SLOTS], F32, name="result_bank", tag=tag)
-            product(bank, stationary, n % PACK, moving)
-            sums = tile("sums%d" % n, [P, SLOTS], F32, at)
-            nc.vector.tensor_tensor(out=sums[:], in0=bank[:], in1=ts_rows[:], op=MULT)
+        def scaled(tiles, stationary, moving, places):
+            sums = [tile("sums%d" % n, [P, SLOTS], F32, at) for n, at in zip(tiles, places)]
+            for h in range(2):
+                cols = slice(HALF * h, HALF * (h + 1))
+                for i, n in enumerate(tiles):
+                    bank = ps.tile([P, SLOTS], F32, name="result_bank", tag="b%d" % (2 * (n % PACK) + h))
+                    product(bank, stationary, n % PACK, moving, cols.start, cols.stop)
+                    nc.vector.tensor_tensor(out=sums[i][:, cols], in0=bank[:, cols], in1=ts_rows[:, cols], op=MULT)
             return sums
 
-        def scatter_scalar(n, sums, first, last):
-            nc.scalar.activation(out=windows[n % PACK][:].indirect(part(first, last)), in_=sums[:, first:last], func=COPY)
+        def scatter_scalar(n, sums, h):
+            first, last = HALF * h, HALF * (h + 1)
+            nc.scalar.activation(out=window_of[n][:].indirect(part(first, last)), in_=sums[:, first:last], func=COPY)
 
-        def scatter_vector(n, sums, first, last):
-            nc.vector.tensor_copy(out=windows[n % PACK][:].indirect(part(first, last)), in_=sums[:, first:last])
+        def scatter_vector(n, sums):
+            nc.vector.tensor_copy(out=window_of[n][:].indirect(offsets[:]), in_=sums[:])
 
         dk_rows = out_0.rearrange("(m t) n -> t m n", t=PACK)
         dv_rows = out_1.rearrange("(j m) n -> j m n", m=P)
 
         def store(n):
             rows = dk_rows[n] if n < PACK else dv_rows[n - PACK]
-            nc.sync.dma_start(out=rows, in_=windows[n % PACK][:])
+            nc.sync.dma_start(out=rows, in_=window_of[n][:])
 
         k_planes = tile("k_planes", [P, PACK, SLOTS], BF16)
         gather_scalar(k_planes, k_raw, 0, 0, SLOTS)
-        dk = [scaled(n, se_mx, v_mx, "b%d" % (4 + n)) for n in range(PACK)]
-        scatter_vector(3, dk[3], HALF, SLOTS)
-        for n in range(PACK - 1):
-            for h in range(2):
-                scatter_scalar(n, dk[n], HALF * h, HALF * (h + 1))
+        dk = scaled(range(PACK), se_mx, v_mx, [None] * PACK)
+        for h in range(2):
+            scatter_scalar(0, dk[0], h)
+        store(0)
+        scatter_vector(1, dk[1])
+        store(1)
+        gather_scalar(k_planes, k_raw, 1, 0, SLOTS)
+        for h in range(2):
+            for n in (2, 3):
+                scatter_scalar(n, dk[n], h)
+        for n in (2, 3):
             store(n)
-        scatter_scalar(3, dk[3], 0, HALF)
-        store(3)
 
-        for t in range(1, PACK):
-            gather_vector(k_planes, k_raw, t, 0, SLOTS)
+        gather_vector(k_planes, k_raw, 2, 0, SLOTS)
         k_woven = tile("k_woven", [P, SLOTS, PACK], BF16)
-        weave(nc.vector.tensor_copy, k_woven[:], k_planes[:])
         k_mx = operand("k", E4M3)
-        quantise(k_mx, k_woven[:], 0)
+        for h in range(2):
+            gather_vector(k_planes, k_raw, 3, HALF * h, HALF * (h + 1))
+        for h in range(2):
+            weave(nc.vector.tensor_copy, k_woven[:, HALF * h : HALF * (h + 1), :], k_planes[:, :, HALF * h : HALF * (h + 1)])
+        for h in range(2):
+            quantise(k_mx, k_woven[:, HALF * h : HALF * (h + 1), :], HALF * h)
 
-        for pair, places in ((4, (SUMS4_AT, None)), (6, (SUMS6_AT, SUMS7_AT))):
-            dv = [scaled(pair + i, sd_mx, k_mx, "b%d" % (pair + i - PACK), places[i]) for i in range(2)]
-            scatter_vector(pair, dv[0], 0, SLOTS)
-            store(pair)
-            for h in range(2):
-                scatter_scalar(pair + 1, dv[1], HALF * h, HALF * (h + 1))
-            store(pair + 1)
+        dv = scaled((4, 5), sd_mx, k_mx, (SUMS4_AT, None))
+        scatter_vector(4, dv[0])
+        store(4)
+        scatter_scalar(5, dv[1], 0)
+        bank6 = ps.tile([P, SLOTS], F32, name="result_bank", tag="b4")
+        product(bank6, sd_mx, 2, k_mx)
+        dv6 = tile("sums6", [P, SLOTS], F32, SUMS6_AT)
+        nc.scalar.copy(out=dv6[:], in_=bank6[:])
+        scatter_scalar(5, dv[1], 1)
+        store(5)
+        nc.vector.tensor_tensor(out=window_of[6][:].indirect(offsets[:]), in0=dv6[:], in1=ts_rows[:], op=MULT)
+        store(6)
+        for h, at in enumerate((SUMS4_AT, SUMS6_AT)):
+            cols = slice(HALF * h, HALF * (h + 1))
+            bank7 = ps.tile([P, SLOTS], F32, name="result_bank", tag="b%d" % (6 + h))
+            product(bank7, sd_mx, 3, k_mx, cols.start, cols.stop)
+            half7 = tile("sums7_%d" % h, [P, HALF], F32, at)
+            nc.vector.tensor_tensor(out=half7[:], in0=bank7[:, cols], in1=ts_rows[:, cols], op=MULT)
+            nc.scalar.activation(out=window_of[7][:].indirect(part(cols.start, cols.stop)), in_=half7[:], func=COPY)
+        store(7)

@@ -28,8 +28,9 @@ V_VECTOR = 320
 TAIL = 256
 WINDOW2_AT = 0
 WINDOW3_AT = PLANE
-V_WOVEN_AT = WINDOW3_AT - ALIGN
+V_WOVEN_AT = WINDOW3_AT - 2048
 WINDOW4_AT = 2 * PLANE
+K_WOVEN_AT = WINDOW4_AT
 WINDOW1_AT = 3 * PLANE
 DO_WOVEN_AT = WINDOW1_AT
 SUMS4_AT = 4 * PLANE
@@ -179,8 +180,7 @@ def tile_attend_glin_kv_kernel(tc, kT, vT, cd, ce, do, qT, ts, offs, out_0, out_
         v_planes = tile("v_planes", [P, PACK, SLOTS], BF16)
         for t in range(PACK - 1):
             gather_scalar(v_planes, v_raw, t, 0, SLOTS)
-        v_span = tile("v_woven", [P, PLANE // 2 + ALIGN], BF16, V_WOVEN_AT)
-        v_woven = v_span[:, 0 : SLOTS * PACK].rearrange("p (c t) -> p c t", t=PACK)
+        v_woven = tile("v_woven", [P, SLOTS, PACK], BF16, V_WOVEN_AT)
         v_mx = operand("v", E4M3)
         gather_scalar(v_planes, v_raw, PACK - 1, 0, HALF)
         gather_vector(v_planes, v_raw, PACK - 1, HALF, SLOTS)
@@ -189,14 +189,11 @@ def tile_attend_glin_kv_kernel(tc, kT, vT, cd, ce, do, qT, ts, offs, out_0, out_
         weave(nc.scalar.copy, v_woven[:, V_VECTOR:SLOTS, :], v_planes[:, :, V_VECTOR:SLOTS])
         for h in range(2):
             quantise(v_mx, v_woven[:, HALF * h : HALF * (h + 1), :], HALF * h)
-        windows = [window0, window1, tile("window2", [P, TOKENS], F32, WINDOW2_AT), tile("window3", [P, TOKENS], F32, WINDOW3_AT),
-                   tile("window4", [P, TOKENS], F32, WINDOW4_AT)]
-        nc.gpsimd.memset(windows[4][:, 0 : TOKENS // 4], 0.0)
+        windows = [window0, window1, tile("window2", [P, TOKENS], F32, WINDOW2_AT), tile("window3", [P, TOKENS], F32, WINDOW3_AT)]
         for cols in (slice(0, TOKENS - TAIL), slice(TOKENS - TAIL, TOKENS)):
             for w in (2, 3):
                 nc.gpsimd.memset(windows[w][:, cols], 0.0)
-        nc.gpsimd.memset(windows[4][:, TOKENS // 4 : TOKENS], 0.0)
-        window_of = [windows[w] for w in (0, 1, 2, 3, 0, 4, 2, 1)]
+        window_of = [windows[w] for w in (0, 1, 2, 3, 1, 0, 2)]
 
         def scaled(tiles, stationary, moving, places):
             sums = [tile("sums%d" % n, [P, SLOTS], F32, at) for n, at in zip(tiles, places)]
@@ -205,7 +202,10 @@ def tile_attend_glin_kv_kernel(tc, kT, vT, cd, ce, do, qT, ts, offs, out_0, out_
                 for i, n in enumerate(tiles):
                     bank = ps.tile([P, SLOTS], F32, name="result_bank", tag="b%d" % (2 * (n % PACK) + h))
                     product(bank, stationary, n % PACK, moving, cols.start, cols.stop)
-                    nc.vector.tensor_tensor(out=sums[i][:, cols], in0=bank[:, cols], in1=ts_rows[:, cols], op=MULT)
+                    if n in (1, 4):
+                        nc.vector.tensor_copy(out=sums[i][:, cols], in_=bank[:, cols])
+                    else:
+                        nc.vector.tensor_tensor(out=sums[i][:, cols], in0=bank[:, cols], in1=ts_rows[:, cols], op=MULT)
             return sums
 
         def scatter_scalar(n, sums, h):
@@ -213,7 +213,7 @@ def tile_attend_glin_kv_kernel(tc, kT, vT, cd, ce, do, qT, ts, offs, out_0, out_
             nc.scalar.activation(out=window_of[n][:].indirect(part(first, last)), in_=sums[:, first:last], func=COPY)
 
         def scatter_vector(n, sums):
-            nc.vector.tensor_copy(out=window_of[n][:].indirect(offsets[:]), in_=sums[:])
+            nc.vector.tensor_tensor(out=window_of[n][:].indirect(offsets[:]), in0=sums[:], in1=ts_rows[:], op=MULT)
 
         dk_rows = out_0.rearrange("(m t) n -> t m n", t=PACK)
         dv_rows = out_1.rearrange("(j m) n -> j m n", m=P)
@@ -238,7 +238,7 @@ def tile_attend_glin_kv_kernel(tc, kT, vT, cd, ce, do, qT, ts, offs, out_0, out_
             store(n)
 
         gather_vector(k_planes, k_raw, 2, 0, SLOTS)
-        k_woven = tile("k_woven", [P, SLOTS, PACK], BF16)
+        k_woven = tile("k_woven", [P, SLOTS, PACK], BF16, K_WOVEN_AT)
         k_mx = operand("k", E4M3)
         for h in range(2):
             gather_vector(k_planes, k_raw, 3, HALF * h, HALF * (h + 1))
@@ -247,6 +247,8 @@ def tile_attend_glin_kv_kernel(tc, kT, vT, cd, ce, do, qT, ts, offs, out_0, out_
         for h in range(2):
             quantise(k_mx, k_woven[:, HALF * h : HALF * (h + 1), :], HALF * h)
 
+        window_of.append(tile("window4", [P, TOKENS], F32, WINDOW4_AT))
+        nc.gpsimd.memset(window_of[7][:], 0.0)
         dv = scaled((4, 5), sd_mx, k_mx, (SUMS4_AT, None))
         scatter_vector(4, dv[0])
         store(4)
@@ -257,7 +259,7 @@ def tile_attend_glin_kv_kernel(tc, kT, vT, cd, ce, do, qT, ts, offs, out_0, out_
         nc.scalar.copy(out=dv6[:], in_=bank6[:])
         scatter_scalar(5, dv[1], 1)
         store(5)
-        nc.vector.tensor_tensor(out=window_of[6][:].indirect(offsets[:]), in0=dv6[:], in1=ts_rows[:], op=MULT)
+        scatter_vector(6, dv6)
         store(6)
         for h, at in enumerate((SUMS4_AT, SUMS6_AT)):
             cols = slice(HALF * h, HALF * (h + 1))

@@ -122,7 +122,7 @@ def tile_attend_glin_kv_kernel(tc, kT, vT, cd, ce, do, qT, ts, offs, out_0, out_
 
         nc.vector.memset(ts_pool[0 : P - 1, :], 0.0)
         window0 = tile("window0", [P, TOKENS], F32)
-        nc.gpsimd.memset(window0[:], 0.0)
+        nc.vector.memset(window0[:], 0.0)
 
         ce_bank = ps.tile([P, PACK, P], F32, name="ce_bank", tag="b2")
         spread(ce_bank, ce_cols)

@@ -25,16 +25,16 @@ FLOPS = 3 * 2 * K * K * K
 PLANE = 4 * TOKENS
 TILE = 4 * SLOTS
 V_VECTOR = 320
-TAIL = 256
-WINDOW2_AT = 0
-WINDOW3_AT = PLANE
-V_WOVEN_AT = WINDOW3_AT - 2048
-WINDOW4_AT = 2 * PLANE
+WINDOW1_AT = 0
+WINDOW2_AT = PLANE
+WINDOW3_AT = 2 * PLANE
+V_WOVEN_AT = WINDOW2_AT - ALIGN
+WINDOW4_AT = 3 * PLANE
 K_WOVEN_AT = WINDOW4_AT
-WINDOW1_AT = 3 * PLANE
-DO_WOVEN_AT = WINDOW1_AT
-SUMS4_AT = 4 * PLANE
-SUMS6_AT = SUMS4_AT + TILE
+WINDOW0_AT = 4 * PLANE
+DO_WOVEN_AT = WINDOW0_AT
+Q_WOVEN_AT = DO_WOVEN_AT + 4096
+SUMS4_AT = 5 * PLANE
 
 
 def tile_attend_glin_kv_kernel(tc, kT, vT, cd, ce, do, qT, ts, offs, out_0, out_1):
@@ -72,14 +72,13 @@ def tile_attend_glin_kv_kernel(tc, kT, vT, cd, ce, do, qT, ts, offs, out_0, out_
                 stop=True,
             )
 
-        def turn(woven, rows, tag):
+        def turn(woven, word_runs, tag, engine_copy):
             woven_words = woven.rearrange("p c t -> p (c t)").bitcast(F32).rearrange("p (a m u) -> p a m u", a=2, u=2)
             bank = ps.tile([P, 2, 2, P], F32, name="turn_bank", tag=tag)
             for a in range(2):
-                row_words = rows[:, a, :].bitcast(F32)
                 for u in range(2):
-                    nc.tensor.transpose(bank[:, a, u, :], row_words[:, u : K // 2 : 2], ident[:])
-            nc.scalar.copy(out=woven_words, in_=bank[:].rearrange("p a u m -> p a m u"))
+                    nc.tensor.transpose(bank[:, a, u, :], word_runs(a, u), ident[:])
+            engine_copy(out=woven_words, in_=bank[:].rearrange("p a u m -> p a m u"))
 
         def spread(bank, columns):
             for j in range(PACK):
@@ -103,10 +102,10 @@ def tile_attend_glin_kv_kernel(tc, kT, vT, cd, ce, do, qT, ts, offs, out_0, out_
         v_raw = [tile("v_raw%d" % t, [P, TOKENS], F32) for t in range(PACK)]
         k_raw = [tile("k_raw%d" % t, [P, TOKENS], F32) for t in range(PACK)]
         q_rows = qT.rearrange("(m t) r -> m t r", t=PACK)
-        nc.sync.dma_start(out=q_raw[0][:], in_=q_rows[:, 0:2, :])
         nc.sync.dma_start(offsets[:], offs)
         nc.sync.dma_start(out=ts_pool[P - 1 : P, :], in_=ts[0:1, :])
-        nc.sync.dma_start(out=q_raw[1][:], in_=q_rows[:, 2:4, :])
+        for h in range(2):
+            nc.sync.dma_start(out=q_raw[h][:], in_=q_rows[:, 2 * h : 2 * h + 2, :])
         nc.scalar.dma_start(out=ce_cols[:], in_=ce[0:1, :].rearrange("o (p j) -> (o p) j", j=PACK))
         nc.scalar.dma_start(out=cd_cols[:], in_=cd.rearrange("(p t) o -> p (t o)", t=PACK))
         nc.sync.dma_start(out=do_raw[:], in_=do.rearrange("(p t) e -> p t e", t=PACK))
@@ -121,35 +120,14 @@ def tile_attend_glin_kv_kernel(tc, kT, vT, cd, ce, do, qT, ts, offs, out_0, out_
                                 pattern=[[-1, P]], channel_multiplier=1)
 
         nc.vector.memset(ts_pool[0 : P - 1, :], 0.0)
-        window0 = tile("window0", [P, TOKENS], F32)
-        nc.vector.memset(window0[:], 0.0)
 
         ce_bank = ps.tile([P, PACK, P], F32, name="ce_bank", tag="b2")
         spread(ce_bank, ce_cols)
         ce_rows = tile("ce_rows", [P, P, PACK], F32)
         nc.scalar.copy(out=ce_rows[:], in_=ce_bank[:].rearrange("p j n -> p n j"))
 
-        q_bf = [tile("q_bf%d" % h, [P, 2, K], BF16) for h in range(2)]
-        q_woven = [tile("q_woven%d" % h, [P, HALF, PACK], BF16) for h in range(2)]
-        q_mx = operand("q", E4M3)
-        for h in range(2):
-            nc.vector.tensor_copy(out=q_bf[h][:], in_=q_raw[h][:])
-            turn(q_woven[h][:], q_bf[h], "b%d" % h)
         ts_gathered = tile("ts_gathered", [P, SLOTS], F32)
         nc.vector.tensor_copy(out=ts_gathered[:], in_=ts_pool[:].indirect(offsets[:]))
-        for h in range(2):
-            quantise(q_mx, q_woven[h][:], HALF * h)
-
-        do_woven = tile("do_woven", [P, K, PACK], BF16, DO_WOVEN_AT)
-        weave(nc.scalar.copy, do_woven[:, DO_VECTOR:K, :], do_raw[:, :, DO_VECTOR:K])
-        weave(nc.vector.tensor_copy, do_woven[:, 0:HALF, :], do_raw[:, :, 0:HALF])
-        weave(nc.vector.tensor_copy, do_woven[:, HALF:DO_VECTOR, :], do_raw[:, :, HALF:DO_VECTOR])
-        do_mx = operand("do", E5M2)
-        for h in range(2):
-            quantise(do_mx, do_woven[:, HALF * h : HALF * (h + 1), :], HALF * h)
-        window1 = tile("window1", [P, TOKENS], F32, WINDOW1_AT)
-        nc.gpsimd.memset(window1[:], 0.0)
-
         ts_turned = ps.tile([P, PACK, P], F32, name="ts_turned", tag="b3")
         for j in range(PACK):
             nc.tensor.transpose(ts_turned[:, j, :], ts_gathered[:, P * j : P * (j + 1)], ident[:])
@@ -160,7 +138,29 @@ def tile_attend_glin_kv_kernel(tc, kT, vT, cd, ce, do, qT, ts, offs, out_0, out_
         ts_rows = tile("ts_rows", [P, SLOTS], F32)
         nc.scalar.copy(out=ts_rows[:], in_=ts_bank[:].rearrange("p j n -> p (j n)"))
 
-        s_planes = tile("s_planes", [P, PACK, K], BF16)
+        q_bf = [tile("q_bf%d" % h, [P, 2 * K], BF16) for h in range(2)]
+        q_woven = [tile("q_woven%d" % h, [P, HALF, PACK], BF16, at) for h, at in enumerate((None, Q_WOVEN_AT))]
+        q_mx = operand("q", E4M3)
+        for h in range(2):
+            nc.vector.tensor_copy(out=q_bf[h][:].rearrange("p (a u w i) -> p a w u i", a=2, u=2, i=2),
+                                  in_=q_raw[h][:].rearrange("p a (w u i) -> p a w u i", u=2, i=2))
+            q_words = q_bf[h][:].bitcast(F32)
+            turn(q_woven[h][:], lambda a, u: q_words[:, P * (2 * a + u) : P * (2 * a + u + 1)], "b%d" % h, nc.scalar.copy)
+        for h in range(2):
+            quantise(q_mx, q_woven[h][:], HALF * h)
+
+        do_woven = tile("do_woven", [P, K, PACK], BF16, DO_WOVEN_AT)
+        weave(nc.scalar.copy, do_woven[:, DO_VECTOR:K, :], do_raw[:, :, DO_VECTOR:K])
+        weave(nc.vector.tensor_copy, do_woven[:, 0:HALF, :], do_raw[:, :, 0:HALF])
+        weave(nc.vector.tensor_copy, do_woven[:, HALF:DO_VECTOR, :], do_raw[:, :, HALF:DO_VECTOR])
+        do_mx = operand("do", E5M2)
+        for h in range(2):
+            quantise(do_mx, do_woven[:, HALF * h : HALF * (h + 1), :], HALF * h)
+        window0 = tile("window0", [P, TOKENS], F32, WINDOW0_AT)
+        nc.gpsimd.memset(window0[:], 0.0)
+
+        s_row = tile("s_planes", [P, PACK * K], BF16)
+        s_planes = s_row[:].rearrange("p (t e) -> p t e", t=PACK)
         for t in range(PACK):
             s_bank = ps.tile([P, K], F32, name="s_bank", tag="b%d" % (4 + t))
             product(s_bank, q_mx, t, do_mx)
@@ -169,18 +169,21 @@ def tile_attend_glin_kv_kernel(tc, kT, vT, cd, ce, do, qT, ts, offs, out_0, out_
                 in1=ce_rows[:].rearrange("p n j -> p (n j)"), op0=MULT, op1=MULT)
         se_woven = [tile("se_woven%d" % h, [P, HALF, PACK], BF16) for h in range(2)]
         se_mx = operand("se", E5M2)
+        s_words = s_row[:].bitcast(F32)
         for h in range(2):
-            turn(se_woven[h][:], s_planes[:, 2 * h : 2 * h + 2, :], "b%d" % h)
+            turn(se_woven[h][:], lambda a, u: s_words[:, HALF * (2 * h + a) + u : HALF * (2 * h + a + 1) : 2], "b%d" % h,
+                 (nc.scalar.copy, nc.vector.tensor_copy)[h])
             quantise(se_mx, se_woven[h][:], HALF * h)
         sd_woven = tile("sd_woven", [P, K, PACK], BF16)
-        weave(nc.vector.tensor_copy, sd_woven[:], s_planes[:])
+        weave(nc.vector.tensor_copy, sd_woven[:], s_planes)
         sd_mx = operand("sd", E5M2)
         quantise(sd_mx, sd_woven[:], 0)
 
         v_planes = tile("v_planes", [P, PACK, SLOTS], BF16)
         for t in range(PACK - 1):
             gather_scalar(v_planes, v_raw, t, 0, SLOTS)
-        v_woven = tile("v_woven", [P, SLOTS, PACK], BF16, V_WOVEN_AT)
+        v_span = tile("v_woven", [P, PLANE // 2 + ALIGN], BF16, V_WOVEN_AT)
+        v_woven = v_span[:, 0 : SLOTS * PACK].rearrange("p (c t) -> p c t", t=PACK)
         v_mx = operand("v", E4M3)
         gather_scalar(v_planes, v_raw, PACK - 1, 0, HALF)
         gather_vector(v_planes, v_raw, PACK - 1, HALF, SLOTS)
@@ -189,10 +192,10 @@ def tile_attend_glin_kv_kernel(tc, kT, vT, cd, ce, do, qT, ts, offs, out_0, out_
         weave(nc.scalar.copy, v_woven[:, V_VECTOR:SLOTS, :], v_planes[:, :, V_VECTOR:SLOTS])
         for h in range(2):
             quantise(v_mx, v_woven[:, HALF * h : HALF * (h + 1), :], HALF * h)
-        windows = [window0, window1, tile("window2", [P, TOKENS], F32, WINDOW2_AT), tile("window3", [P, TOKENS], F32, WINDOW3_AT)]
-        for cols in (slice(0, TOKENS - TAIL), slice(TOKENS - TAIL, TOKENS)):
-            for w in (2, 3):
-                nc.gpsimd.memset(windows[w][:, cols], 0.0)
+        windows = [window0]
+        for w, at in ((1, WINDOW1_AT), (2, WINDOW2_AT), (3, WINDOW3_AT)):
+            windows.append(tile("window%d" % w, [P, TOKENS], F32, at))
+            nc.gpsimd.memset(windows[w][:], 0.0)
         window_of = [windows[w] for w in (0, 1, 2, 3, 1, 0, 2)]
 
         def scaled(tiles, stationary, moving, places):
@@ -230,13 +233,13 @@ def tile_attend_glin_kv_kernel(tc, kT, vT, cd, ce, do, qT, ts, offs, out_0, out_
         store(0)
         scatter_vector(1, dk[1])
         store(1)
-        gather_scalar(k_planes, k_raw, 1, 0, SLOTS)
-        for h in range(2):
-            for n in (2, 3):
-                scatter_scalar(n, dk[n], h)
+        gather_scalar(k_planes, k_raw, 1, 0, HALF)
         for n in (2, 3):
+            for h in range(2):
+                scatter_scalar(n, dk[n], h)
             store(n)
 
+        gather_vector(k_planes, k_raw, 1, HALF, SLOTS)
         gather_vector(k_planes, k_raw, 2, 0, SLOTS)
         k_woven = tile("k_woven", [P, SLOTS, PACK], BF16, K_WOVEN_AT)
         k_mx = operand("k", E4M3)
@@ -255,17 +258,16 @@ def tile_attend_glin_kv_kernel(tc, kT, vT, cd, ce, do, qT, ts, offs, out_0, out_
         scatter_scalar(5, dv[1], 0)
         bank6 = ps.tile([P, SLOTS], F32, name="result_bank", tag="b4")
         product(bank6, sd_mx, 2, k_mx)
-        dv6 = tile("sums6", [P, SLOTS], F32, SUMS6_AT)
+        dv6 = tile("sums6", [P, SLOTS], F32)
         nc.scalar.copy(out=dv6[:], in_=bank6[:])
         scatter_scalar(5, dv[1], 1)
         store(5)
+        bank7 = ps.tile([P, SLOTS], F32, name="result_bank", tag="b6")
+        product(bank7, sd_mx, 3, k_mx)
+        dv7 = tile("sums7", [P, SLOTS], F32, SUMS4_AT)
+        nc.vector.tensor_tensor(out=dv7[:], in0=bank7[:], in1=ts_rows[:], op=MULT)
         scatter_vector(6, dv6)
         store(6)
-        for h, at in enumerate((SUMS4_AT, SUMS6_AT)):
-            cols = slice(HALF * h, HALF * (h + 1))
-            bank7 = ps.tile([P, SLOTS], F32, name="result_bank", tag="b%d" % (6 + h))
-            product(bank7, sd_mx, 3, k_mx, cols.start, cols.stop)
-            half7 = tile("sums7_%d" % h, [P, HALF], F32, at)
-            nc.vector.tensor_tensor(out=half7[:], in0=bank7[:, cols], in1=ts_rows[:, cols], op=MULT)
-            nc.scalar.activation(out=window_of[7][:].indirect(part(cols.start, cols.stop)), in_=half7[:], func=COPY)
+        for h in range(2):
+            scatter_scalar(7, dv7, h)
         store(7)

@@ -23,18 +23,15 @@ ALIGN = 64
 FLOPS = 3 * 2 * K * K * K
 
 PLANE = 4 * TOKENS
-TILE = 4 * SLOTS
-V_VECTOR = 320
-WINDOW1_AT = 0
-WINDOW2_AT = PLANE
-WINDOW3_AT = 2 * PLANE
-V_WOVEN_AT = WINDOW2_AT - ALIGN
-WINDOW4_AT = 3 * PLANE
-K_WOVEN_AT = WINDOW4_AT
-WINDOW0_AT = 4 * PLANE
+WINDOW0_AT = 0
 DO_WOVEN_AT = WINDOW0_AT
-Q_WOVEN_AT = DO_WOVEN_AT + 4096
-SUMS4_AT = 5 * PLANE
+WINDOW4_AT = PLANE
+DK0_AT = 2 * PLANE
+V_WOVEN1_AT = DK0_AT - ALIGN
+V_WOVEN1_SPAN = 2048 + 2 * ALIGN
+WINDOW2_AT = DK0_AT + 2048
+WINDOW3_AT = WINDOW2_AT + PLANE
+V_CODES1_AT = WINDOW3_AT
 
 
 def tile_attend_glin_kv_kernel(tc, kT, vT, cd, ce, do, qT, ts, offs, out_0, out_1):
@@ -52,46 +49,51 @@ def tile_attend_glin_kv_kernel(tc, kT, vT, cd, ce, do, qT, ts, offs, out_0, out_
         def weave(engine_copy, woven, planes):
             engine_copy(out=woven.rearrange("p (c i) t -> p c t i", i=4), in_=planes.rearrange("p t (c i) -> p c t i", i=4))
 
-        def operand(name, fmt, at=None):
-            return tile(name + "_codes", [P, K], U32, at), tile(name + "_scales", [P, K], U8), fmt
+        def operand(name, fmt, width=K, at=None):
+            return tile(name + "_codes", [P, width], U32, at), tile(name + "_scales", [P, width], U8), fmt
 
-        def quantise(mx, woven, first):
+        def quantise(mx, woven, first=0):
             codes, scales, fmt = mx
             cols = slice(first, first + woven.shape[1])
             nc.vector.quantize_mx(out=codes[:, cols].bitcast(fmt), scales=scales[:, cols], in_=woven.rearrange("p c t -> p (c t)"))
 
-        def product(bank, stationary, j, moving, first=0, last=K):
+        def product(sums, stationary, j, moving):
             cols = slice(P * j, P * (j + 1))
             nc.tensor.matmul_mx(
-                out=bank[:, first:last],
+                out=sums,
                 lhsT=stationary[0][:, cols].bitcast(stationary[2]),
                 lhsT_scale=stationary[1][:, cols],
-                rhs=moving[0][:, first:last].bitcast(moving[2]),
-                rhs_scale=moving[1][:, first:last],
+                rhs=moving[0][:].bitcast(moving[2]),
+                rhs_scale=moving[1][:],
                 start=True,
                 stop=True,
             )
 
-        def turn(woven, word_runs, tag, engine_copy):
+        def turn(woven, word_runs, tag):
             woven_words = woven.rearrange("p c t -> p (c t)").bitcast(F32).rearrange("p (a m u) -> p a m u", a=2, u=2)
             bank = ps.tile([P, 2, 2, P], F32, name="turn_bank", tag=tag)
             for a in range(2):
                 for u in range(2):
                     nc.tensor.transpose(bank[:, a, u, :], word_runs(a, u), ident[:])
-            engine_copy(out=woven_words, in_=bank[:].rearrange("p a u m -> p a m u"))
+            nc.scalar.copy(out=woven_words, in_=bank[:].rearrange("p a u m -> p a m u"))
 
         def spread(bank, columns):
             for j in range(PACK):
                 nc.tensor.transpose(bank[:, j, :], columns[:, j : j + 1].to_broadcast([P, P]), ident[:])
 
-        def part(first, last):
-            return offsets[:, first // 16 : last // 16]
+        def half(h):
+            return slice(HALF * h, HALF * (h + 1))
 
-        def gather_vector(planes, raw, t, first, last):
-            nc.vector.tensor_copy(out=planes[:, t, first:last], in_=raw[t][:].indirect(part(first, last)))
+        def part(cols):
+            return offsets[:, cols.start // 16 : cols.stop // 16]
 
-        def gather_scalar(planes, raw, t, first, last):
-            nc.scalar.activation(out=planes[:, t, first:last], in_=raw[t][:].indirect(part(first, last)), func=COPY)
+        whole = slice(0, SLOTS)
+
+        def gather_vector(out, raw, cols):
+            nc.vector.tensor_copy(out=out, in_=raw[:].indirect(part(cols)))
+
+        def gather_scalar(out, raw, cols):
+            nc.scalar.activation(out=out, in_=raw[:].indirect(part(cols)), func=COPY)
 
         offsets = sb.tile([P, SLOTS // 16], U16, name="offsets")
         q_raw = [tile("q_raw%d" % h, [P, 2, K], F32) for h in range(2)]
@@ -102,10 +104,10 @@ def tile_attend_glin_kv_kernel(tc, kT, vT, cd, ce, do, qT, ts, offs, out_0, out_
         v_raw = [tile("v_raw%d" % t, [P, TOKENS], F32) for t in range(PACK)]
         k_raw = [tile("k_raw%d" % t, [P, TOKENS], F32) for t in range(PACK)]
         q_rows = qT.rearrange("(m t) r -> m t r", t=PACK)
+        nc.sync.dma_start(out=q_raw[0][:], in_=q_rows[:, 0:2, :])
+        nc.sync.dma_start(out=q_raw[1][:], in_=q_rows[:, 2:4, :])
         nc.sync.dma_start(offsets[:], offs)
         nc.sync.dma_start(out=ts_pool[P - 1 : P, :], in_=ts[0:1, :])
-        for h in range(2):
-            nc.sync.dma_start(out=q_raw[h][:], in_=q_rows[:, 2 * h : 2 * h + 2, :])
         nc.scalar.dma_start(out=ce_cols[:], in_=ce[0:1, :].rearrange("o (p j) -> (o p) j", j=PACK))
         nc.scalar.dma_start(out=cd_cols[:], in_=cd.rearrange("(p t) o -> p (t o)", t=PACK))
         nc.sync.dma_start(out=do_raw[:], in_=do.rearrange("(p t) e -> p t e", t=PACK))
@@ -120,14 +122,56 @@ def tile_attend_glin_kv_kernel(tc, kT, vT, cd, ce, do, qT, ts, offs, out_0, out_
                                 pattern=[[-1, P]], channel_multiplier=1)
 
         nc.vector.memset(ts_pool[0 : P - 1, :], 0.0)
+        windows = {1: tile("window1", [P, TOKENS], F32)}
+        nc.vector.memset(windows[1][:], 0.0)
 
         ce_bank = ps.tile([P, PACK, P], F32, name="ce_bank", tag="b2")
         spread(ce_bank, ce_cols)
         ce_rows = tile("ce_rows", [P, P, PACK], F32)
         nc.scalar.copy(out=ce_rows[:], in_=ce_bank[:].rearrange("p j n -> p n j"))
 
+        q_bf = [tile("q_bf%d" % h, [P, 2 * K], BF16) for h in range(2)]
+        q_woven = [tile("q_woven%d" % h, [P, HALF, PACK], BF16) for h in range(2)]
+        q_mx = operand("q", E4M3)
+        for h, engine_copy in enumerate((nc.scalar.copy, nc.vector.tensor_copy)):
+            engine_copy(out=q_bf[h][:].rearrange("p (a u w i) -> p a u w i", a=2, u=2, i=2),
+                        in_=q_raw[h][:].rearrange("p a (w u i) -> p a u w i", u=2, i=2))
         ts_gathered = tile("ts_gathered", [P, SLOTS], F32)
-        nc.vector.tensor_copy(out=ts_gathered[:], in_=ts_pool[:].indirect(offsets[:]))
+        gather_vector(ts_gathered[:], ts_pool, whole)
+        for h in range(2):
+            q_words = q_bf[h][:].bitcast(F32)
+            turn(q_woven[h][:], lambda a, u: q_words[:, P * (2 * a + u) : P * (2 * a + u + 1)], "b%d" % h)
+            quantise(q_mx, q_woven[h][:], HALF * h)
+
+        do_woven = tile("do_woven", [P, K, PACK], BF16, DO_WOVEN_AT)
+        weave(nc.scalar.copy, do_woven[:, DO_VECTOR:K, :], do_raw[:, :, DO_VECTOR:K])
+        weave(nc.vector.tensor_copy, do_woven[:, 0:HALF, :], do_raw[:, :, 0:HALF])
+        weave(nc.vector.tensor_copy, do_woven[:, HALF:DO_VECTOR, :], do_raw[:, :, HALF:DO_VECTOR])
+        do_mx = operand("do", E5M2)
+        for h in range(2):
+            quantise(do_mx, do_woven[:, half(h), :], HALF * h)
+        windows[0] = tile("window0", [P, TOKENS], F32, WINDOW0_AT)
+        nc.gpsimd.memset(windows[0][:], 0.0)
+
+        s_row = tile("s_planes", [P, PACK * K], BF16)
+        s_planes = s_row[:].rearrange("p (t e) -> p t e", t=PACK)
+        for t in range(PACK):
+            s_bank = ps.tile([P, K], F32, name="s_bank", tag="b%d" % (4 + t))
+            product(s_bank[:], q_mx, t, do_mx)
+            nc.vector.scalar_tensor_tensor(
+                out=s_planes[:, t, :], in0=s_bank[:], scalar=cd_cols[:, t : t + 1],
+                in1=ce_rows[:].rearrange("p n j -> p (n j)"), op0=MULT, op1=MULT)
+        se_woven = [tile("se_woven%d" % h, [P, HALF, PACK], BF16) for h in range(2)]
+        se_mx = operand("se", E5M2)
+        s_words = s_row[:].bitcast(F32)
+        for h in range(2):
+            turn(se_woven[h][:], lambda a, u: s_words[:, HALF * (2 * h + a) + u : HALF * (2 * h + a + 1) : 2], "b%d" % h)
+            quantise(se_mx, se_woven[h][:], HALF * h)
+        sd_woven = tile("sd_woven", [P, K, PACK], BF16)
+        weave(nc.vector.tensor_copy, sd_woven[:], s_planes)
+        sd_mx = operand("sd", E5M2)
+        quantise(sd_mx, sd_woven[:])
+
         ts_turned = ps.tile([P, PACK, P], F32, name="ts_turned", tag="b3")
         for j in range(PACK):
             nc.tensor.transpose(ts_turned[:, j, :], ts_gathered[:, P * j : P * (j + 1)], ident[:])
@@ -138,136 +182,102 @@ def tile_attend_glin_kv_kernel(tc, kT, vT, cd, ce, do, qT, ts, offs, out_0, out_
         ts_rows = tile("ts_rows", [P, SLOTS], F32)
         nc.scalar.copy(out=ts_rows[:], in_=ts_bank[:].rearrange("p j n -> p (j n)"))
 
-        q_bf = [tile("q_bf%d" % h, [P, 2 * K], BF16) for h in range(2)]
-        q_woven = [tile("q_woven%d" % h, [P, HALF, PACK], BF16, at) for h, at in enumerate((None, Q_WOVEN_AT))]
-        q_mx = operand("q", E4M3)
-        for h in range(2):
-            nc.vector.tensor_copy(out=q_bf[h][:].rearrange("p (a u w i) -> p a w u i", a=2, u=2, i=2),
-                                  in_=q_raw[h][:].rearrange("p a (w u i) -> p a w u i", u=2, i=2))
-            q_words = q_bf[h][:].bitcast(F32)
-            turn(q_woven[h][:], lambda a, u: q_words[:, P * (2 * a + u) : P * (2 * a + u + 1)], "b%d" % h, nc.scalar.copy)
-        for h in range(2):
-            quantise(q_mx, q_woven[h][:], HALF * h)
-
-        do_woven = tile("do_woven", [P, K, PACK], BF16, DO_WOVEN_AT)
-        weave(nc.scalar.copy, do_woven[:, DO_VECTOR:K, :], do_raw[:, :, DO_VECTOR:K])
-        weave(nc.vector.tensor_copy, do_woven[:, 0:HALF, :], do_raw[:, :, 0:HALF])
-        weave(nc.vector.tensor_copy, do_woven[:, HALF:DO_VECTOR, :], do_raw[:, :, HALF:DO_VECTOR])
-        do_mx = operand("do", E5M2)
-        for h in range(2):
-            quantise(do_mx, do_woven[:, HALF * h : HALF * (h + 1), :], HALF * h)
-        window0 = tile("window0", [P, TOKENS], F32, WINDOW0_AT)
-        nc.gpsimd.memset(window0[:], 0.0)
-
-        s_row = tile("s_planes", [P, PACK * K], BF16)
-        s_planes = s_row[:].rearrange("p (t e) -> p t e", t=PACK)
-        for t in range(PACK):
-            s_bank = ps.tile([P, K], F32, name="s_bank", tag="b%d" % (4 + t))
-            product(s_bank, q_mx, t, do_mx)
-            nc.vector.scalar_tensor_tensor(
-                out=s_planes[:, t, :], in0=s_bank[:], scalar=cd_cols[:, t : t + 1],
-                in1=ce_rows[:].rearrange("p n j -> p (n j)"), op0=MULT, op1=MULT)
-        se_woven = [tile("se_woven%d" % h, [P, HALF, PACK], BF16) for h in range(2)]
-        se_mx = operand("se", E5M2)
-        s_words = s_row[:].bitcast(F32)
-        for h in range(2):
-            turn(se_woven[h][:], lambda a, u: s_words[:, HALF * (2 * h + a) + u : HALF * (2 * h + a + 1) : 2], "b%d" % h,
-                 (nc.scalar.copy, nc.vector.tensor_copy)[h])
-            quantise(se_mx, se_woven[h][:], HALF * h)
-        sd_woven = tile("sd_woven", [P, K, PACK], BF16)
-        weave(nc.vector.tensor_copy, sd_woven[:], s_planes)
-        sd_mx = operand("sd", E5M2)
-        quantise(sd_mx, sd_woven[:], 0)
-
+        last = PACK - 1
         v_planes = tile("v_planes", [P, PACK, SLOTS], BF16)
-        for t in range(PACK - 1):
-            gather_scalar(v_planes, v_raw, t, 0, SLOTS)
-        v_span = tile("v_woven", [P, PLANE // 2 + ALIGN], BF16, V_WOVEN_AT)
-        v_woven = v_span[:, 0 : SLOTS * PACK].rearrange("p (c t) -> p c t", t=PACK)
-        v_mx = operand("v", E4M3)
-        gather_scalar(v_planes, v_raw, PACK - 1, 0, HALF)
-        gather_vector(v_planes, v_raw, PACK - 1, HALF, SLOTS)
-        weave(nc.vector.tensor_copy, v_woven[:, 0:HALF, :], v_planes[:, :, 0:HALF])
-        weave(nc.vector.tensor_copy, v_woven[:, HALF:V_VECTOR, :], v_planes[:, :, HALF:V_VECTOR])
-        weave(nc.scalar.copy, v_woven[:, V_VECTOR:SLOTS, :], v_planes[:, :, V_VECTOR:SLOTS])
-        for h in range(2):
-            quantise(v_mx, v_woven[:, HALF * h : HALF * (h + 1), :], HALF * h)
-        windows = [window0]
-        for w, at in ((1, WINDOW1_AT), (2, WINDOW2_AT), (3, WINDOW3_AT)):
-            windows.append(tile("window%d" % w, [P, TOKENS], F32, at))
-            nc.gpsimd.memset(windows[w][:], 0.0)
-        window_of = [windows[w] for w in (0, 1, 2, 3, 1, 0, 2)]
+        for t in range(last):
+            gather_scalar(v_planes[:, t, :], v_raw[t], whole)
+        v_span = tile("v_woven1", [P, V_WOVEN1_SPAN // 2], BF16, V_WOVEN1_AT)
+        v_woven = [tile("v_woven0", [P, HALF, PACK], BF16), v_span[:, 0 : HALF * PACK].rearrange("p (c t) -> p c t", t=PACK)]
+        v_mx = [operand("v%d" % h, E4M3, HALF, at) for h, at in enumerate((None, V_CODES1_AT))]
+        weave(nc.vector.tensor_copy, v_woven[0][:, :, 0:last], v_planes[:, 0:last, half(0)])
+        weave(nc.vector.tensor_copy, v_woven[1][:, :, 0:2], v_planes[:, 0:2, half(1)])
+        gather_vector(v_woven[0][:, :, last], v_raw[last], half(0))
+        gather_scalar(v_planes[:, last, half(1)], v_raw[last], half(1))
+        weave(nc.scalar.copy, v_woven[1][:, :, 2:PACK], v_planes[:, 2:PACK, half(1)])
 
-        def scaled(tiles, stationary, moving, places):
-            sums = [tile("sums%d" % n, [P, SLOTS], F32, at) for n, at in zip(tiles, places)]
-            for h in range(2):
-                cols = slice(HALF * h, HALF * (h + 1))
-                for i, n in enumerate(tiles):
-                    bank = ps.tile([P, SLOTS], F32, name="result_bank", tag="b%d" % (2 * (n % PACK) + h))
-                    product(bank, stationary, n % PACK, moving, cols.start, cols.stop)
-                    if n in (1, 4):
-                        nc.vector.tensor_copy(out=sums[i][:, cols], in_=bank[:, cols])
-                    else:
-                        nc.vector.tensor_tensor(out=sums[i][:, cols], in0=bank[:, cols], in1=ts_rows[:, cols], op=MULT)
-            return sums
+        def bank(tag):
+            return ps.tile([P, SLOTS], F32, name="result_bank", tag="b%d" % tag)
 
-        def scatter_scalar(n, sums, h):
-            first, last = HALF * h, HALF * (h + 1)
-            nc.scalar.activation(out=window_of[n][:].indirect(part(first, last)), in_=sums[:, first:last], func=COPY)
+        def empty_scaled(sums, sums_bank, cols):
+            nc.vector.tensor_tensor(out=sums, in0=sums_bank, in1=ts_rows[:, cols], op=MULT)
 
-        def scatter_vector(n, sums):
-            nc.vector.tensor_tensor(out=window_of[n][:].indirect(offsets[:]), in0=sums[:], in1=ts_rows[:], op=MULT)
+        def scatter_scalar(window, sums, cols):
+            nc.scalar.activation(out=window[:].indirect(part(cols)), in_=sums, func=COPY)
+
+        def scatter_vector(window, sums, cols):
+            nc.vector.tensor_tensor(out=window[:].indirect(part(cols)), in0=sums, in1=ts_rows[:, cols], op=MULT)
 
         dk_rows = out_0.rearrange("(m t) n -> t m n", t=PACK)
         dv_rows = out_1.rearrange("(j m) n -> j m n", m=P)
 
-        def store(n):
+        def store(n, window):
             rows = dk_rows[n] if n < PACK else dv_rows[n - PACK]
-            nc.sync.dma_start(out=rows, in_=window_of[n][:])
+            nc.sync.dma_start(out=rows, in_=window[:])
+
+        for h in range(2):
+            quantise(v_mx[h], v_woven[h][:])
+        dk = [tile("dk%d" % n, [P, SLOTS], F32, DK0_AT if n == 0 else None) for n in range(PACK)]
+        dk0_banks = [bank(0), bank(4)]
+        dk_banks = {1: bank(1)}
+        for h in range(2):
+            product(dk0_banks[h][:, half(h)], se_mx, 0, v_mx[h])
+            product(dk_banks[1][:, half(h)], se_mx, 1, v_mx[h])
+        for h in range(2):
+            empty_scaled(dk[0][:, half(h)], dk0_banks[h][:, half(h)], half(h))
+            dk_banks[2 + h] = bank(PACK * h)
+            for g in range(2):
+                product(dk_banks[2 + h][:, half(g)], se_mx, 2 + h, v_mx[g])
+        for w, at in ((4, WINDOW4_AT), (2, WINDOW2_AT), (3, WINDOW3_AT)):
+            windows[w] = tile("window%d" % w, [P, TOKENS], F32, at)
+            nc.gpsimd.memset(windows[w][:], 0.0)
+        nc.vector.tensor_copy(out=dk[1][:], in_=dk_banks[1][:])
+        for n in (2, 3):
+            empty_scaled(dk[n][:], dk_banks[n][:], whole)
 
         k_planes = tile("k_planes", [P, PACK, SLOTS], BF16)
-        gather_scalar(k_planes, k_raw, 0, 0, SLOTS)
-        dk = scaled(range(PACK), se_mx, v_mx, [None] * PACK)
+        scatter_scalar(windows[0], dk[0][:, half(0)], half(0))
+        gather_scalar(k_planes[:, 0, :], k_raw[0], whole)
+        scatter_scalar(windows[0], dk[0][:, half(1)], half(1))
+        store(0, windows[0])
+        scatter_vector(windows[1], dk[1][:], whole)
+        store(1, windows[1])
+        scatter_scalar(windows[2], dk[2][:, half(0)], half(0))
+        gather_scalar(k_planes[:, 1, :], k_raw[1], whole)
+        scatter_scalar(windows[2], dk[2][:, half(1)], half(1))
+        store(2, windows[2])
         for h in range(2):
-            scatter_scalar(0, dk[0], h)
-        store(0)
-        scatter_vector(1, dk[1])
-        store(1)
-        gather_scalar(k_planes, k_raw, 1, 0, HALF)
-        for n in (2, 3):
+            scatter_scalar(windows[3], dk[3][:, half(h)], half(h))
+        store(3, windows[3])
+
+        k_woven = [tile("k_woven%d" % h, [P, HALF, PACK], BF16) for h in range(2)]
+        k_mx = [operand("k%d" % h, E4M3, HALF) for h in range(2)]
+        gather_vector(k_planes[:, 2, :], k_raw[2], whole)
+        for h in range(2):
+            gather_vector(k_planes[:, last, half(h)], k_raw[last], half(h))
+        for h in range(2):
+            weave(nc.vector.tensor_copy, k_woven[h][:], k_planes[:, :, half(h)])
+        for h in range(2):
+            quantise(k_mx[h], k_woven[h][:])
+
+        dv = [tile("dv%d" % j, [P, SLOTS], F32) for j in range(PACK)]
+
+        def dv_bank(j, tag):
+            sums_bank = bank(tag)
             for h in range(2):
-                scatter_scalar(n, dk[n], h)
-            store(n)
+                product(sums_bank[:, half(h)], sd_mx, j, k_mx[h])
+            return sums_bank
 
-        gather_vector(k_planes, k_raw, 1, HALF, SLOTS)
-        gather_vector(k_planes, k_raw, 2, 0, SLOTS)
-        k_woven = tile("k_woven", [P, SLOTS, PACK], BF16, K_WOVEN_AT)
-        k_mx = operand("k", E4M3)
+        nc.vector.tensor_copy(out=dv[0][:], in_=dv_bank(0, 0)[:])
+        empty_scaled(dv[1][:], dv_bank(1, 1)[:], whole)
+        scatter_vector(windows[4], dv[0][:], whole)
+        store(4, windows[4])
+        scatter_scalar(windows[0], dv[1][:, half(0)], half(0))
+        nc.scalar.copy(out=dv[2][:], in_=dv_bank(2, 1)[:])
+        scatter_scalar(windows[0], dv[1][:, half(1)], half(1))
+        store(5, windows[0])
+        empty_scaled(dv[3][:], dv_bank(3, 2)[:], whole)
+        scatter_vector(windows[1], dv[2][:], whole)
+        store(6, windows[1])
         for h in range(2):
-            gather_vector(k_planes, k_raw, 3, HALF * h, HALF * (h + 1))
-        for h in range(2):
-            weave(nc.vector.tensor_copy, k_woven[:, HALF * h : HALF * (h + 1), :], k_planes[:, :, HALF * h : HALF * (h + 1)])
-        for h in range(2):
-            quantise(k_mx, k_woven[:, HALF * h : HALF * (h + 1), :], HALF * h)
-
-        window_of.append(tile("window4", [P, TOKENS], F32, WINDOW4_AT))
-        nc.gpsimd.memset(window_of[7][:], 0.0)
-        dv = scaled((4, 5), sd_mx, k_mx, (SUMS4_AT, None))
-        scatter_vector(4, dv[0])
-        store(4)
-        scatter_scalar(5, dv[1], 0)
-        bank6 = ps.tile([P, SLOTS], F32, name="result_bank", tag="b4")
-        product(bank6, sd_mx, 2, k_mx)
-        dv6 = tile("sums6", [P, SLOTS], F32)
-        nc.scalar.copy(out=dv6[:], in_=bank6[:])
-        scatter_scalar(5, dv[1], 1)
-        store(5)
-        bank7 = ps.tile([P, SLOTS], F32, name="result_bank", tag="b6")
-        product(bank7, sd_mx, 3, k_mx)
-        dv7 = tile("sums7", [P, SLOTS], F32, SUMS4_AT)
-        nc.vector.tensor_tensor(out=dv7[:], in0=bank7[:], in1=ts_rows[:], op=MULT)
-        scatter_vector(6, dv6)
-        store(6)
-        for h in range(2):
-            scatter_scalar(7, dv7, h)
-        store(7)
+            scatter_scalar(windows[2], dv[3][:, half(h)], half(h))
+        store(7, windows[2])

@@ -25,13 +25,15 @@ FLOPS = 3 * 2 * K * K * K
 PLANE = 4 * TOKENS
 WINDOW0_AT = 0
 DO_WOVEN_AT = WINDOW0_AT
-WINDOW4_AT = PLANE
+WINDOW3_AT = PLANE
 DK0_AT = 2 * PLANE
 V_WOVEN1_AT = DK0_AT - ALIGN
 V_WOVEN1_SPAN = 2048 + 2 * ALIGN
 WINDOW2_AT = DK0_AT + 2048
-WINDOW3_AT = WINDOW2_AT + PLANE
-V_CODES1_AT = WINDOW3_AT
+WINDOW4_AT = WINDOW2_AT + PLANE
+V_CODES1_AT = WINDOW4_AT
+K_WOVEN0_AT = WINDOW4_AT + PLANE
+DK3_REST_AT = K_WOVEN0_AT
 
 
 def tile_attend_glin_kv_kernel(tc, kT, vT, cd, ce, do, qT, ts, offs, out_0, out_1):
@@ -227,12 +229,12 @@ def tile_attend_glin_kv_kernel(tc, kT, vT, cd, ce, do, qT, ts, offs, out_0, out_
             dk_banks[2 + h] = bank(PACK * h)
             for g in range(2):
                 product(dk_banks[2 + h][:, half(g)], se_mx, 2 + h, v_mx[g])
-        for w, at in ((4, WINDOW4_AT), (2, WINDOW2_AT), (3, WINDOW3_AT)):
+        for w, at in ((3, WINDOW3_AT), (4, WINDOW4_AT), (2, WINDOW2_AT)):
             windows[w] = tile("window%d" % w, [P, TOKENS], F32, at)
             nc.gpsimd.memset(windows[w][:], 0.0)
         nc.vector.tensor_copy(out=dk[1][:], in_=dk_banks[1][:])
-        for n in (2, 3):
-            empty_scaled(dk[n][:], dk_banks[n][:], whole)
+        empty_scaled(dk[2][:], dk_banks[2][:], whole)
+        nc.vector.tensor_copy(out=dk[3][:, half(1)], in_=dk_banks[3][:, half(1)])
 
         k_planes = tile("k_planes", [P, PACK, SLOTS], BF16)
         scatter_scalar(windows[0], dk[0][:, half(0)], half(0))
@@ -241,17 +243,15 @@ def tile_attend_glin_kv_kernel(tc, kT, vT, cd, ce, do, qT, ts, offs, out_0, out_
         store(0, windows[0])
         scatter_vector(windows[1], dk[1][:], whole)
         store(1, windows[1])
-        scatter_scalar(windows[2], dk[2][:, half(0)], half(0))
-        gather_scalar(k_planes[:, 1, :], k_raw[1], whole)
-        scatter_scalar(windows[2], dk[2][:, half(1)], half(1))
-        store(2, windows[2])
+        scatter_vector(windows[3], dk[3][:, half(1)], half(1))
+        for t in (1, 2):
+            gather_scalar(k_planes[:, t, :], k_raw[t], whole)
         for h in range(2):
-            scatter_scalar(windows[3], dk[3][:, half(h)], half(h))
-        store(3, windows[3])
+            scatter_scalar(windows[2], dk[2][:, half(h)], half(h))
+        store(2, windows[2])
 
-        k_woven = [tile("k_woven%d" % h, [P, HALF, PACK], BF16) for h in range(2)]
+        k_woven = [tile("k_woven%d" % h, [P, HALF, PACK], BF16, at) for h, at in enumerate((K_WOVEN0_AT, None))]
         k_mx = [operand("k%d" % h, E4M3, HALF) for h in range(2)]
-        gather_vector(k_planes[:, 2, :], k_raw[2], whole)
         for h in range(2):
             gather_vector(k_planes[:, last, half(h)], k_raw[last], half(h))
         for h in range(2):
@@ -267,17 +267,25 @@ def tile_attend_glin_kv_kernel(tc, kT, vT, cd, ce, do, qT, ts, offs, out_0, out_
                 product(sums_bank[:, half(h)], sd_mx, j, k_mx[h])
             return sums_bank
 
-        nc.vector.tensor_copy(out=dv[0][:], in_=dv_bank(0, 0)[:])
-        empty_scaled(dv[1][:], dv_bank(1, 1)[:], whole)
-        scatter_vector(windows[4], dv[0][:], whole)
-        store(4, windows[4])
-        scatter_scalar(windows[0], dv[1][:, half(0)], half(0))
-        nc.scalar.copy(out=dv[2][:], in_=dv_bank(2, 1)[:])
-        scatter_scalar(windows[0], dv[1][:, half(1)], half(1))
-        store(5, windows[0])
-        empty_scaled(dv[3][:], dv_bank(3, 2)[:], whole)
-        scatter_vector(windows[1], dv[2][:], whole)
-        store(6, windows[1])
+        dk3_rest = tile("dk3_rest", [P, HALF], F32, DK3_REST_AT)
+        nc.vector.tensor_copy(out=dk3_rest[:], in_=dk_banks[3][:, half(0)])
+        dv0_banks = [bank(h) for h in range(2)]
         for h in range(2):
-            scatter_scalar(windows[2], dv[3][:, half(h)], half(h))
+            product(dv0_banks[h][:, half(h)], sd_mx, 0, k_mx[h])
+        empty_scaled(dv[0][:, half(0)], dv0_banks[0][:, half(0)], half(0))
+        scatter_vector(windows[3], dk3_rest[:], half(0))
+        store(3, windows[3])
+        empty_scaled(dv[0][:, half(1)], dv0_banks[1][:, half(1)], half(1))
+        scatter_scalar(windows[4], dv[0][:, half(0)], half(0))
+        nc.scalar.copy(out=dv[1][:], in_=dv_bank(1, 0)[:])
+        scatter_scalar(windows[4], dv[0][:, half(1)], half(1))
+        store(4, windows[4])
+        empty_scaled(dv[2][:], dv_bank(2, PACK)[:], whole)
+        scatter_vector(windows[0], dv[1][:], whole)
+        store(5, windows[0])
+        scatter_scalar(windows[1], dv[2][:, half(0)], half(0))
+        nc.scalar.copy(out=dv[3][:], in_=dv_bank(3, PACK)[:])
+        scatter_scalar(windows[1], dv[2][:, half(1)], half(1))
+        store(6, windows[1])
+        scatter_vector(windows[2], dv[3][:], whole)
         store(7, windows[2])

@@ -19,6 +19,7 @@ TOKENS = 2048
 SLOTS = 512
 HALF = 256
 DO_VECTOR = 336
+K_SCALAR = 384
 ALIGN = 64
 FLOPS = 3 * 2 * K * K * K
 
@@ -26,14 +27,15 @@ PLANE = 4 * TOKENS
 WINDOW0_AT = 0
 DO_WOVEN_AT = WINDOW0_AT
 WINDOW3_AT = PLANE
-DK0_AT = 2 * PLANE
-V_WOVEN1_AT = DK0_AT - ALIGN
-V_WOVEN1_SPAN = 2048 + 2 * ALIGN
-WINDOW2_AT = DK0_AT + 2048
+WINDOW2_AT = 2 * PLANE
+V_WOVEN1_AT = WINDOW2_AT - 1024
 WINDOW4_AT = WINDOW2_AT + PLANE
 V_CODES1_AT = WINDOW4_AT
-K_WOVEN0_AT = WINDOW4_AT + PLANE
-DK3_REST_AT = K_WOVEN0_AT
+K_PLANES_AT = WINDOW4_AT + PLANE
+DK3_REST_AT = K_PLANES_AT
+V_PLANES_AT = K_PLANES_AT + 4096
+DK0_AT = V_PLANES_AT
+DK1_AT = V_PLANES_AT + 2048
 
 
 def tile_attend_glin_kv_kernel(tc, kT, vT, cd, ce, do, qT, ts, offs, out_0, out_1):
@@ -185,17 +187,21 @@ def tile_attend_glin_kv_kernel(tc, kT, vT, cd, ce, do, qT, ts, offs, out_0, out_
         nc.scalar.copy(out=ts_rows[:], in_=ts_bank[:].rearrange("p j n -> p (j n)"))
 
         last = PACK - 1
-        v_planes = tile("v_planes", [P, PACK, SLOTS], BF16)
-        for t in range(last):
+        v_planes = tile("v_planes", [P, PACK, SLOTS], BF16, V_PLANES_AT)
+        for t in range(2):
             gather_scalar(v_planes[:, t, :], v_raw[t], whole)
-        v_span = tile("v_woven1", [P, V_WOVEN1_SPAN // 2], BF16, V_WOVEN1_AT)
-        v_woven = [tile("v_woven0", [P, HALF, PACK], BF16), v_span[:, 0 : HALF * PACK].rearrange("p (c t) -> p c t", t=PACK)]
+        v_woven = [tile("v_woven%d" % h, [P, HALF, PACK], BF16, at) for h, at in enumerate((None, V_WOVEN1_AT))]
         v_mx = [operand("v%d" % h, E4M3, HALF, at) for h, at in enumerate((None, V_CODES1_AT))]
-        weave(nc.vector.tensor_copy, v_woven[0][:, :, 0:last], v_planes[:, 0:last, half(0)])
-        weave(nc.vector.tensor_copy, v_woven[1][:, :, 0:2], v_planes[:, 0:2, half(1)])
-        gather_vector(v_woven[0][:, :, last], v_raw[last], half(0))
-        gather_scalar(v_planes[:, last, half(1)], v_raw[last], half(1))
-        weave(nc.scalar.copy, v_woven[1][:, :, 2:PACK], v_planes[:, 2:PACK, half(1)])
+        for h in range(2):
+            weave(nc.vector.tensor_copy, v_woven[h][:, :, 0:2], v_planes[:, 0:2, half(h)])
+        for t in (2, last):
+            gather_vector(v_woven[0][:, :, t], v_raw[t], half(0))
+        gather_scalar(v_planes[:, 2, half(1)], v_raw[2], half(1))
+        quarters = [slice(HALF + P * i, HALF + P * (i + 1)) for i in range(2)]
+        for cols in quarters:
+            gather_scalar(v_planes[:, last, cols], v_raw[last], cols)
+        for i, cols in enumerate(quarters):
+            weave(nc.scalar.copy, v_woven[1][:, P * i : P * (i + 1), 2:PACK], v_planes[:, 2:PACK, cols])
 
         def bank(tag):
             return ps.tile([P, SLOTS], F32, name="result_bank", tag="b%d" % tag)
@@ -218,46 +224,49 @@ def tile_attend_glin_kv_kernel(tc, kT, vT, cd, ce, do, qT, ts, offs, out_0, out_
 
         for h in range(2):
             quantise(v_mx[h], v_woven[h][:])
-        dk = [tile("dk%d" % n, [P, SLOTS], F32, DK0_AT if n == 0 else None) for n in range(PACK)]
+        dk = [tile("dk%d" % n, [P, SLOTS], F32, at) for n, at in enumerate((DK0_AT, DK1_AT, None, None))]
         dk0_banks = [bank(0), bank(4)]
-        dk_banks = {1: bank(1)}
+        dk1_banks = [bank(1), bank(5)]
+        dk_banks = {}
         for h in range(2):
+            product(dk1_banks[h][:, half(h)], se_mx, 1, v_mx[h])
             product(dk0_banks[h][:, half(h)], se_mx, 0, v_mx[h])
-            product(dk_banks[1][:, half(h)], se_mx, 1, v_mx[h])
         for h in range(2):
+            nc.vector.tensor_copy(out=dk[1][:, half(h)], in_=dk1_banks[h][:, half(h)])
+        for h in (1, 0):
             empty_scaled(dk[0][:, half(h)], dk0_banks[h][:, half(h)], half(h))
-            dk_banks[2 + h] = bank(PACK * h)
+        for h in range(2):
+            dk_banks[2 + h] = bank(1 + PACK * h)
             for g in range(2):
                 product(dk_banks[2 + h][:, half(g)], se_mx, 2 + h, v_mx[g])
         for w, at in ((3, WINDOW3_AT), (4, WINDOW4_AT), (2, WINDOW2_AT)):
             windows[w] = tile("window%d" % w, [P, TOKENS], F32, at)
             nc.gpsimd.memset(windows[w][:], 0.0)
-        nc.vector.tensor_copy(out=dk[1][:], in_=dk_banks[1][:])
         empty_scaled(dk[2][:], dk_banks[2][:], whole)
-        nc.vector.tensor_copy(out=dk[3][:, half(1)], in_=dk_banks[3][:, half(1)])
 
-        k_planes = tile("k_planes", [P, PACK, SLOTS], BF16)
-        scatter_scalar(windows[0], dk[0][:, half(0)], half(0))
+        k_planes = tile("k_planes", [P, PACK, SLOTS], BF16, K_PLANES_AT)
         gather_scalar(k_planes[:, 0, :], k_raw[0], whole)
         scatter_scalar(windows[0], dk[0][:, half(1)], half(1))
+        nc.scalar.copy(out=dk[3][:, half(1)], in_=dk_banks[3][:, half(1)])
+        scatter_scalar(windows[0], dk[0][:, half(0)], half(0))
         store(0, windows[0])
         scatter_vector(windows[1], dk[1][:], whole)
         store(1, windows[1])
         scatter_vector(windows[3], dk[3][:, half(1)], half(1))
-        for t in (1, 2):
-            gather_scalar(k_planes[:, t, :], k_raw[t], whole)
+        gather_scalar(k_planes[:, 1, :], k_raw[1], whole)
+        gather_scalar(k_planes[:, 2, 0:K_SCALAR], k_raw[2], slice(0, K_SCALAR))
         for h in range(2):
             scatter_scalar(windows[2], dk[2][:, half(h)], half(h))
         store(2, windows[2])
 
-        k_woven = [tile("k_woven%d" % h, [P, HALF, PACK], BF16, at) for h, at in enumerate((K_WOVEN0_AT, None))]
+        k_woven = [tile("k_woven%d" % h, [P, HALF, PACK], BF16) for h in range(2)]
         k_mx = [operand("k%d" % h, E4M3, HALF) for h in range(2)]
+        gather_vector(k_planes[:, 2, K_SCALAR:SLOTS], k_raw[2], slice(K_SCALAR, SLOTS))
         for h in range(2):
             gather_vector(k_planes[:, last, half(h)], k_raw[last], half(h))
         for h in range(2):
             weave(nc.vector.tensor_copy, k_woven[h][:], k_planes[:, :, half(h)])
-        for h in range(2):
-            quantise(k_mx[h], k_woven[h][:])
+        quantise(k_mx[0], k_woven[0][:])
 
         dv = [tile("dv%d" % j, [P, SLOTS], F32) for j in range(PACK)]
 
@@ -269,9 +278,10 @@ def tile_attend_glin_kv_kernel(tc, kT, vT, cd, ce, do, qT, ts, offs, out_0, out_
 
         dk3_rest = tile("dk3_rest", [P, HALF], F32, DK3_REST_AT)
         nc.vector.tensor_copy(out=dk3_rest[:], in_=dk_banks[3][:, half(0)])
-        dv0_banks = [bank(h) for h in range(2)]
-        for h in range(2):
-            product(dv0_banks[h][:, half(h)], sd_mx, 0, k_mx[h])
+        dv0_banks = [bank(0), bank(PACK)]
+        product(dv0_banks[0][:, half(0)], sd_mx, 0, k_mx[0])
+        quantise(k_mx[1], k_woven[1][:])
+        product(dv0_banks[1][:, half(1)], sd_mx, 0, k_mx[1])
         empty_scaled(dv[0][:, half(0)], dv0_banks[0][:, half(0)], half(0))
         scatter_vector(windows[3], dk3_rest[:], half(0))
         store(3, windows[3])
@@ -280,11 +290,11 @@ def tile_attend_glin_kv_kernel(tc, kT, vT, cd, ce, do, qT, ts, offs, out_0, out_
         nc.scalar.copy(out=dv[1][:], in_=dv_bank(1, 0)[:])
         scatter_scalar(windows[4], dv[0][:, half(1)], half(1))
         store(4, windows[4])
-        empty_scaled(dv[2][:], dv_bank(2, PACK)[:], whole)
+        empty_scaled(dv[2][:], dv_bank(2, 5)[:], whole)
         scatter_vector(windows[0], dv[1][:], whole)
         store(5, windows[0])
         scatter_scalar(windows[1], dv[2][:, half(0)], half(0))
-        nc.scalar.copy(out=dv[3][:], in_=dv_bank(3, PACK)[:])
+        nc.scalar.copy(out=dv[3][:], in_=dv_bank(3, 5)[:])
         scatter_scalar(windows[1], dv[2][:, half(1)], half(1))
         store(6, windows[1])
         scatter_vector(windows[2], dv[3][:], whole)

from contextlib import ExitStack

import concourse.mybir as mybir

F32 = mybir.dt.float32
BF16 = mybir.dt.bfloat16
U32 = mybir.dt.uint32
U16 = mybir.dt.uint16
U8 = mybir.dt.uint8
E4M3 = mybir.dt.float8_e4m3fn_x4
E5M2 = mybir.dt.float8_e5m2_x4
MULT = mybir.AluOpType.mult
COPY = mybir.ActivationFunctionType.Copy

P = 128
PACK = 4
K = 512
TOKENS = 2048
SLOTS = 512
HALF = 256
DO_VECTOR = 336
K_SCALAR = 384
ALIGN = 64
FLOPS = 3 * 2 * K * K * K

PLANE = 4 * TOKENS
WINDOW0_AT = 0
DO_WOVEN_AT = WINDOW0_AT
WINDOW3_AT = PLANE
WINDOW2_AT = 2 * PLANE
V_WOVEN1_AT = WINDOW2_AT - 1024
WINDOW4_AT = WINDOW2_AT + PLANE
V_CODES1_AT = WINDOW4_AT
K_PLANES_AT = WINDOW4_AT + PLANE
DK3_REST_AT = K_PLANES_AT
V_PLANES_AT = K_PLANES_AT + 4096
DK0_AT = V_PLANES_AT
DK1_AT = V_PLANES_AT + 2048


def tile_attend_glin_kv_kernel(tc, kT, vT, cd, ce, do, qT, ts, offs, out_0, out_1):
    nc = tc.nc
    with ExitStack() as ctx:
        sb = ctx.enter_context(tc.tile_pool(name="sb", bufs=1))
        placed = ctx.enter_context(tc.tile_pool(name="placed", bufs=1))
        ps = ctx.enter_context(tc.psum_pool(name="ps", bufs=1))

        def tile(name, shape, dtype, at=None):
            if at is None:
                return sb.tile(shape, dtype, name=name, align_bytes=ALIGN)
            return placed.tile(shape, dtype, name=name, offset=at, align_bytes=ALIGN)

        def weave(engine_copy, woven, planes):
            engine_copy(out=woven.rearrange("p (c i) t -> p c t i", i=4), in_=planes.rearrange("p t (c i) -> p c t i", i=4))

        def operand(name, fmt, width=K, at=None):
            return tile(name + "_codes", [P, width], U32, at), tile(name + "_scales", [P, width], U8), fmt

        def quantise(mx, woven, first=0):
            codes, scales, fmt = mx
            cols = slice(first, first + woven.shape[1])
            nc.vector.quantize_mx(out=codes[:, cols].bitcast(fmt), scales=scales[:, cols], in_=woven.rearrange("p c t -> p (c t)"))

        def product(sums, stationary, j, moving):
            cols = slice(P * j, P * (j + 1))
            nc.tensor.matmul_mx(
                out=sums,
                lhsT=stationary[0][:, cols].bitcast(stationary[2]),
                lhsT_scale=stationary[1][:, cols],
                rhs=moving[0][:].bitcast(moving[2]),
                rhs_scale=moving[1][:],
                start=True,
                stop=True,
            )

        def turn(woven, word_runs, tag):
            woven_words = woven.rearrange("p c t -> p (c t)").bitcast(F32).rearrange("p (a m u) -> p a m u", a=2, u=2)
            bank = ps.tile([P, 2, 2, P], F32, name="turn_bank", tag=tag)
            for a in range(2):
                for u in range(2):
                    nc.tensor.transpose(bank[:, a, u, :], word_runs(a, u), ident[:])
            nc.scalar.copy(out=woven_words, in_=bank[:].rearrange("p a u m -> p a m u"))

        def spread(bank, columns):
            for j in range(PACK):
                nc.tensor.transpose(bank[:, j, :], columns[:, j : j + 1].to_broadcast([P, P]), ident[:])

        def half(h):
            return slice(HALF * h, HALF * (h + 1))

        def part(cols):
            return offsets[:, cols.start // 16 : cols.stop // 16]

        whole = slice(0, SLOTS)

        def gather_vector(out, raw, cols):
            nc.vector.tensor_copy(out=out, in_=raw[:].indirect(part(cols)))

        def gather_scalar(out, raw, cols):
            nc.scalar.activation(out=out, in_=raw[:].indirect(part(cols)), func=COPY)

        offsets = sb.tile([P, SLOTS // 16], U16, name="offsets")
        q_raw = [tile("q_raw%d" % h, [P, 2, K], F32) for h in range(2)]
        do_raw = tile("do_raw", [P, PACK, K], F32)
        cd_cols = tile("cd_cols", [P, PACK], F32)
        ce_cols = tile("ce_cols", [P, PACK], F32)
        ts_pool = tile("ts_pool", [P, TOKENS], F32)
        v_raw = [tile("v_raw%d" % t, [P, TOKENS], F32) for t in range(PACK)]
        k_raw = [tile("k_raw%d" % t, [P, TOKENS], F32) for t in range(PACK)]
        q_rows = qT.rearrange("(m t) r -> m t r", t=PACK)
        nc.sync.dma_start(out=q_raw[0][:], in_=q_rows[:, 0:2, :])
        nc.sync.dma_start(out=q_raw[1][:], in_=q_rows[:, 2:4, :])
        nc.sync.dma_start(offsets[:], offs)
        nc.sync.dma_start(out=ts_pool[P - 1 : P, :], in_=ts[0:1, :])
        nc.scalar.dma_start(out=ce_cols[:], in_=ce[0:1, :].rearrange("o (p j) -> (o p) j", j=PACK))
        nc.scalar.dma_start(out=cd_cols[:], in_=cd.rearrange("(p t) o -> p (t o)", t=PACK))
        nc.sync.dma_start(out=do_raw[:], in_=do.rearrange("(p t) e -> p t e", t=PACK))
        for raw, table in ((v_raw, vT), (k_raw, kT)):
            rows = table.rearrange("(p t) n -> t p n", t=PACK)
            for t in range(PACK):
                nc.sync.dma_start(out=raw[t][:], in_=rows[t])

        ident = tile("ident", [P, P], F32)
        nc.gpsimd.memset(ident[:], 0.0)
        nc.gpsimd.affine_select(out=ident[:], in_=ident[:], compare_op=mybir.AluOpType.not_equal, fill=1.0, base=0,
                                pattern=[[-1, P]], channel_multiplier=1)

        nc.vector.memset(ts_pool[0 : P - 1, :], 0.0)
        windows = {1: tile("window1", [P, TOKENS], F32)}
        nc.vector.memset(windows[1][:], 0.0)

        ce_bank = ps.tile([P, PACK, P], F32, name="ce_bank", tag="b2")
        spread(ce_bank, ce_cols)
        ce_rows = tile("ce_rows", [P, P, PACK], F32)
        nc.scalar.copy(out=ce_rows[:], in_=ce_bank[:].rearrange("p j n -> p n j"))

        q_bf = [tile("q_bf%d" % h, [P, 2 * K], BF16) for h in range(2)]
        q_woven = [tile("q_woven%d" % h, [P, HALF, PACK], BF16) for h in range(2)]
        q_mx = operand("q", E4M3)
        for h, engine_copy in enumerate((nc.scalar.copy, nc.vector.tensor_copy)):
            engine_copy(out=q_bf[h][:].rearrange("p (a u w i) -> p a u w i", a=2, u=2, i=2),
                        in_=q_raw[h][:].rearrange("p a (w u i) -> p a u w i", u=2, i=2))
        ts_gathered = tile("ts_gathered", [P, SLOTS], F32)
        gather_vector(ts_gathered[:], ts_pool, whole)
        for h in range(2):
            q_words = q_bf[h][:].bitcast(F32)
            turn(q_woven[h][:], lambda a, u: q_words[:, P * (2 * a + u) : P * (2 * a + u + 1)], "b%d" % h)
            quantise(q_mx, q_woven[h][:], HALF * h)

        do_woven = tile("do_woven", [P, K, PACK], BF16, DO_WOVEN_AT)
        weave(nc.scalar.copy, do_woven[:, DO_VECTOR:K, :], do_raw[:, :, DO_VECTOR:K])
        weave(nc.vector.tensor_copy, do_woven[:, 0:HALF, :], do_raw[:, :, 0:HALF])
        weave(nc.vector.tensor_copy, do_woven[:, HALF:DO_VECTOR, :], do_raw[:, :, HALF:DO_VECTOR])
        do_mx = operand("do", E5M2)
        for h in range(2):
            quantise(do_mx, do_woven[:, half(h), :], HALF * h)
        windows[0] = tile("window0", [P, TOKENS], F32, WINDOW0_AT)
        nc.gpsimd.memset(windows[0][:], 0.0)

        s_row = tile("s_planes", [P, PACK * K], BF16)
        s_planes = s_row[:].rearrange("p (t e) -> p t e", t=PACK)
        for t in range(PACK):
            s_bank = ps.tile([P, K], F32, name="s_bank", tag="b%d" % (4 + t))
            product(s_bank[:], q_mx, t, do_mx)
            nc.vector.scalar_tensor_tensor(
                out=s_planes[:, t, :], in0=s_bank[:], scalar=cd_cols[:, t : t + 1],
                in1=ce_rows[:].rearrange("p n j -> p (n j)"), op0=MULT, op1=MULT)
        se_woven = [tile("se_woven%d" % h, [P, HALF, PACK], BF16) for h in range(2)]
        se_mx = operand("se", E5M2)
        s_words = s_row[:].bitcast(F32)
        for h in range(2):
            turn(se_woven[h][:], lambda a, u: s_words[:, HALF * (2 * h + a) + u : HALF * (2 * h + a + 1) : 2], "b%d" % h)
            quantise(se_mx, se_woven[h][:], HALF * h)
        sd_woven = tile("sd_woven", [P, K, PACK], BF16)
        weave(nc.vector.tensor_copy, sd_woven[:], s_planes)
        sd_mx = operand("sd", E5M2)
        quantise(sd_mx, sd_woven[:])

        ts_turned = ps.tile([P, PACK, P], F32, name="ts_turned", tag="b3")
        for j in range(PACK):
            nc.tensor.transpose(ts_turned[:, j, :], ts_gathered[:, P * j : P * (j + 1)], ident[:])
        ts_cols = tile("ts_cols", [P, PACK], F32)
        nc.scalar.copy(out=ts_cols[:], in_=ts_turned[:, :, P - 1])
        ts_bank = ps.tile([P, PACK, P], F32, name="ts_bank", tag="b3")
        spread(ts_bank, ts_cols)
        ts_rows = tile("ts_rows", [P, SLOTS], F32)
        nc.scalar.copy(out=ts_rows[:], in_=ts_bank[:].rearrange("p j n -> p (j n)"))

        last = PACK - 1
        v_planes = tile("v_planes", [P, PACK, SLOTS], BF16, V_PLANES_AT)
        for t in range(2):
            gather_scalar(v_planes[:, t, :], v_raw[t], whole)
        v_woven = [tile("v_woven%d" % h, [P, HALF, PACK], BF16, at) for h, at in enumerate((None, V_WOVEN1_AT))]
        v_mx = [operand("v%d" % h, E4M3, HALF, at) for h, at in enumerate((None, V_CODES1_AT))]
        for h in range(2):
            weave(nc.vector.tensor_copy, v_woven[h][:, :, 0:2], v_planes[:, 0:2, half(h)])
        for t in (2, last):
            gather_vector(v_woven[0][:, :, t], v_raw[t], half(0))
        gather_scalar(v_planes[:, 2, half(1)], v_raw[2], half(1))
        quarters = [slice(HALF + P * i, HALF + P * (i + 1)) for i in range(2)]
        for cols in quarters:
            gather_scalar(v_planes[:, last, cols], v_raw[last], cols)
        for i, cols in enumerate(quarters):
            weave(nc.scalar.copy, v_woven[1][:, P * i : P * (i + 1), 2:PACK], v_planes[:, 2:PACK, cols])

        def bank(tag):
            return ps.tile([P, SLOTS], F32, name="result_bank", tag="b%d" % tag)

        def empty_scaled(sums, sums_bank, cols):
            nc.vector.tensor_tensor(out=sums, in0=sums_bank, in1=ts_rows[:, cols], op=MULT)

        def scatter_scalar(window, sums, cols):
            nc.scalar.activation(out=window[:].indirect(part(cols)), in_=sums, func=COPY)

        def scatter_vector(window, sums, cols):
            nc.vector.tensor_tensor(out=window[:].indirect(part(cols)), in0=sums, in1=ts_rows[:, cols], op=MULT)

        dk_rows = out_0.rearrange("(m t) n -> t m n", t=PACK)
        dv_rows = out_1.rearrange("(j m) n -> j m n", m=P)

        def store(n, window):
            rows = dk_rows[n] if n < PACK else dv_rows[n - PACK]
            nc.sync.dma_start(out=rows, in_=window[:])

        for h in range(2):
            quantise(v_mx[h], v_woven[h][:])
        dk = [tile("dk%d" % n, [P, SLOTS], F32, at) for n, at in enumerate((DK0_AT, DK1_AT, None, None))]
        dk0_banks = [bank(0), bank(4)]
        dk1_banks = [bank(1), bank(5)]
        dk_banks = {}
        for h in range(2):
            product(dk1_banks[h][:, half(h)], se_mx, 1, v_mx[h])
            product(dk0_banks[h][:, half(h)], se_mx, 0, v_mx[h])
        for h in range(2):
            nc.vector.tensor_copy(out=dk[1][:, half(h)], in_=dk1_banks[h][:, half(h)])
        for h in (1, 0):
            empty_scaled(dk[0][:, half(h)], dk0_banks[h][:, half(h)], half(h))
        for h in range(2):
            dk_banks[2 + h] = bank(1 + PACK * h)
            for g in range(2):
                product(dk_banks[2 + h][:, half(g)], se_mx, 2 + h, v_mx[g])
        for w, at in ((3, WINDOW3_AT), (4, WINDOW4_AT), (2, WINDOW2_AT)):
            windows[w] = tile("window%d" % w, [P, TOKENS], F32, at)
            nc.gpsimd.memset(windows[w][:], 0.0)
        empty_scaled(dk[2][:], dk_banks[2][:], whole)

        k_planes = tile("k_planes", [P, PACK, SLOTS], BF16, K_PLANES_AT)
        gather_scalar(k_planes[:, 0, :], k_raw[0], whole)
        scatter_scalar(windows[0], dk[0][:, half(1)], half(1))
        nc.scalar.copy(out=dk[3][:, half(1)], in_=dk_banks[3][:, half(1)])
        scatter_scalar(windows[0], dk[0][:, half(0)], half(0))
        store(0, windows[0])
        scatter_vector(windows[1], dk[1][:], whole)
        store(1, windows[1])
        scatter_vector(windows[3], dk[3][:, half(1)], half(1))
        gather_scalar(k_planes[:, 1, :], k_raw[1], whole)
        gather_scalar(k_planes[:, 2, 0:K_SCALAR], k_raw[2], slice(0, K_SCALAR))
        for h in range(2):
            scatter_scalar(windows[2], dk[2][:, half(h)], half(h))
        store(2, windows[2])

        k_woven = [tile("k_woven%d" % h, [P, HALF, PACK], BF16) for h in range(2)]
        k_mx = [operand("k%d" % h, E4M3, HALF) for h in range(2)]
        gather_vector(k_planes[:, 2, K_SCALAR:SLOTS], k_raw[2], slice(K_SCALAR, SLOTS))
        for h in range(2):
            gather_vector(k_planes[:, last, half(h)], k_raw[last], half(h))
        for h in range(2):
            weave(nc.vector.tensor_copy, k_woven[h][:], k_planes[:, :, half(h)])
        quantise(k_mx[0], k_woven[0][:])

        dv = [tile("dv%d" % j, [P, SLOTS], F32) for j in range(PACK)]

        def dv_bank(j, tag):
            sums_bank = bank(tag)
            for h in range(2):
                product(sums_bank[:, half(h)], sd_mx, j, k_mx[h])
            return sums_bank

        dk3_rest = tile("dk3_rest", [P, HALF], F32, DK3_REST_AT)
        nc.vector.tensor_copy(out=dk3_rest[:], in_=dk_banks[3][:, half(0)])
        dv0_banks = [bank(0), bank(PACK)]
        product(dv0_banks[0][:, half(0)], sd_mx, 0, k_mx[0])
        quantise(k_mx[1], k_woven[1][:])
        product(dv0_banks[1][:, half(1)], sd_mx, 0, k_mx[1])
        empty_scaled(dv[0][:, half(0)], dv0_banks[0][:, half(0)], half(0))
        scatter_vector(windows[3], dk3_rest[:], half(0))
        store(3, windows[3])
        empty_scaled(dv[0][:, half(1)], dv0_banks[1][:, half(1)], half(1))
        scatter_scalar(windows[4], dv[0][:, half(0)], half(0))
        nc.scalar.copy(out=dv[1][:], in_=dv_bank(1, 0)[:])
        scatter_scalar(windows[4], dv[0][:, half(1)], half(1))
        store(4, windows[4])
        empty_scaled(dv[2][:], dv_bank(2, 5)[:], whole)
        scatter_vector(windows[0], dv[1][:], whole)
        store(5, windows[0])
        scatter_scalar(windows[1], dv[2][:, half(0)], half(0))
        nc.scalar.copy(out=dv[3][:], in_=dv_bank(3, 5)[:])
        scatter_scalar(windows[1], dv[2][:, half(1)], half(1))
        store(6, windows[1])
        scatter_vector(windows[2], dv[3][:], whole)
        store(7, windows[2])
